import numpy as np, ml_dtypes
CORES = [2,7,18,23,34]
N = 5
BF = ml_dtypes.bfloat16
V, P, Q, RO, TS = 192, 3, 2, 3, 1024
M, B = 8 * N * V, V // P
def clip(a):
    return np.minimum(np.maximum(np.floor(a), -2 ** 20), 2 ** 20 - 1).astype(np.int64)
def walls(rng, base, size, gap):
    mid = base + size * (rng.random((N, 8, 16, V)) - 0.5)
    h = gap * (16 - np.arange(16)[:, None]) * 0.0625
    l = mid + h * rng.random((N, 8, 16, V)); r = mid - h * rng.random((N, 8, 16, V)); turn = rng.random((N, 8, 1, V)) < 0.25
    return clip(np.where(turn, r, l)), clip(np.where(turn, l, r))
def common(rng):
    return walls(rng, rng.integers(-2 ** 18, 2 ** 18, (N, 8, 1, V)), np.exp2(rng.integers(8, 18, (N, 8, 1, V))), 2.0 ** 17 * rng.random((N, 8, 1, V)))
def slots(rng):
    share = rng.choice(np.array([0.1, 0.4, 0.7, 0.9]), (N, 8, 2, 1, V))
    o = rng.integers(0, M, (N, 8, 16, V)); none = (rng.random((N, 8, 2, 8, V)) < share).reshape(N, 8, 16, V)
    return np.where(none, M, o)
def pack(l, r, o):
    return {"lw": np.ascontiguousarray(l.reshape(N, 128, V)).astype(np.int32), "rw": np.ascontiguousarray(r.reshape(N, 128, V)).astype(np.int32),
            "opts": np.ascontiguousarray(o.reshape(N, 128, V)).astype(np.int32)}
def setup_inputs(rng):
    l, r = common(rng)
    return pack(l, r, slots(rng))
def setup_inputs_ties(rng):
    ix = rng.integers(0, 5, (N, 8, V)); base = 65536 * np.array([0, 0, 12, 12, -13])[:, None] + 2 * rng.integers(-4, 5, (5, 1)); out = []
    for up in (rng.integers(0, 6), 0):
        prof = base + up + rng.integers(0, 2, (5, 16))
        a = prof[ix].transpose(0, 1, 3, 2)
        i = rng.integers(0, 16, (N, 8, 1, V)); d = rng.choice(np.array([-1, 1]), (N, 8, 1, V)) * (rng.random((N, 8, 1, V)) < 0.3)
        far = 65536 * (rng.random((N, 8, 1, V)) < 0.125)
        out.append(a + d * (np.arange(16)[:, None] == i) + far)
    return pack(out[0], out[1], np.where(rng.random((N, 8, 16, V)) < 0.3, M, rng.integers(0, M, (N, 8, 16, V))))
def setup_inputs_bare(rng):
    l, r = common(rng); kinds = np.zeros((7, 16), bool)
    kinds[1, :8] = True; kinds[2, 8:] = True; kinds[3] = True; kinds[4, [0, 15]] = True; kinds[5, [7, 8]] = True; kinds[6, 0] = True
    cls = rng.integers(0, 7, (N, 8, V)); cls[:, 3] = 0; cls[:, 5] = 3
    o = np.where(kinds[cls].transpose(0, 1, 3, 2), rng.integers(0, M, (N, 8, 16, V)), M)
    for g, s, e, d in ((1, 0, -2 ** 20, 1), (6, 15, 2 ** 20 - 1, -1)):
        l[:, g] = e + d * rng.integers(0, 64, (N, 16, V)); r[:, g] = e + d * rng.integers(0, 64, (N, 16, V))
        o[:, g] = M; o[:, g, s] = V * (8 * rng.integers(0, N, (N, V)) + g) + rng.integers(0, B, (N, V))
    return pack(l, r, o)
def setup_inputs_ends(rng):
    l, r = common(rng); o = slots(rng)
    o[:, ::2] = rng.choice(np.array([0, V - 1, V, 8 * V - 1, 8 * V, M - 1, M]), (N, 4, 16, V))
    o[:, 2] = rng.integers(0, M)
    own = V * np.arange(8 * N).reshape(N, 8, 1, 1) + np.arange(V)
    o[:, 1] = np.where(rng.random((N, 16, V)) < 0.5, own[:, 1], o[:, 1])
    o[:, 3, :8] = o[:, 3, :1]; o[:, 3, 8:] = o[:, 3, 8:9]
    here = 8 * V * np.arange(N)[:, None, None]; nxt = 8 * V * ((np.arange(N) + 1) % N)[:, None, None]
    o[:, 5] = nxt + rng.integers(0, 8 * V, (N, 16, V))
    o[:, 7] = np.where(o[:, 7] < M, here + rng.integers(0, 8 * V, (N, 16, V)), M)
    return pack(l, r, o)
def setup_inputs_late(rng):
    bump = rng.random((N, 8, 1, V)) < 0.0625; bump[:, 4] = False
    l = rng.integers(-2 ** 12, 2 ** 12, (16, 1)) + bump
    r = l + rng.choice(np.array([-3, 0, 3, 5001]), (16, 1))
    z = rng.integers(0, 8, (N, 8, 2, 1, V)); s = np.arange(8)[:, None]
    has = np.where(rng.random((N, 8, 2, 1, V)) < 0.4, s == z, s >= z).reshape(N, 8, 16, V)
    o = np.where(has, rng.integers(0, M, (N, 8, 16, V)), M)
    o[:, 4] = V * (8 * rng.integers(0, N, (N, 16, V)) + 4) + rng.integers(0, V, (N, 16, V))
    return pack(l, r, o)
def setup_inputs_spread(rng):
    base = rng.choice(np.array([-1.0, 1.0]), (N, 8, 1, V)) * np.exp2(20 * rng.random((N, 8, 1, V)))
    l, r = walls(rng, base, np.abs(base) * rng.random((N, 8, 1, V)), np.exp2(18 * rng.random((N, 8, 1, V))))
    e = rng.integers(1, 5, (1, 8, 1, 1))
    o = np.minimum((M * rng.random((N, 8, 16, V)) ** e).astype(np.int64), M - 1)
    share = rng.random((N, 8, 1, V)); share[rng.integers(0, N)] = 0.0
    return pack(l, r, np.where(rng.random((N, 8, 16, V)) < share, M, o))
def check_inputs(d):
    bad = []
    for k, lo, hi in (("lw", -2 ** 20, 2 ** 20 - 1), ("rw", -2 ** 20, 2 ** 20 - 1), ("opts", 0, M)):
        if np.min(d[k]) < lo or np.max(d[k]) > hi: bad.append("range of " + k)
    return bad
def world(a, last):
    w = a.reshape(N, 8, 16, V).transpose(2, 0, 1, 3).reshape(16, M).astype(np.int32)
    return np.concatenate([w, np.full((16, 1), last, np.int32)], axis=1)
def back(w):
    return np.ascontiguousarray(w[:, :M].reshape(16, N, 8, V).transpose(1, 2, 0, 3)).reshape(N, 128, V).astype(np.float32)
def inner(L, R, ix):
    return np.concatenate([R[:, ix[:8]], -L[:, ix[8:]]], axis=1)
def reference(lw, rw, opts):
    L, R, O = world(lw, 0), world(rw, 0), world(opts, M)
    temp = (TS * np.arange(16, dtype=np.int32))[:, None]; s16 = np.arange(16); left = (s16 < 8)[:, None]
    for t in range(RO):
        nL, nR, nO = L.copy(), R.copy(), O.copy()
        v = np.tile(B * (t % P) + np.arange(B), 8 * N); c = V * np.repeat(np.arange(8 * N), B) + v
        o = O[:, c]; xl, xr = L[:, c], R[:, c]; has = o < M
        u = inner(L, R, o); gone = np.zeros(o.shape, bool)
        for q in range(Q):
            p = s16 ^ (1 + (t + 3 * q) % 7); up = u[:, p]
            ge = np.all(up >= u, axis=0); eq = np.all(up == u, axis=0)
            gone = gone | (has & has[p] & ge & (~eq | (p < s16)[:, None]))
        sl = (v + t) & 7; k = O[np.where(left, 8 + sl, sl), o]
        kl, kr = L[:, k], R[:, k]; yl, yr = xl[:, None, :], xr[:, None, :]
        under = np.all((kl[:, :8] <= yl) & (kr[:, :8] <= yr), axis=0); over = np.all((kl[:, 8:] >= yl) & (kr[:, 8:] >= yr), axis=0)
        rev = (has & ~gone & (k < M) & np.concatenate([under, over], axis=0)).reshape(2, 8, -1).astype(np.int64)
        first = (rev == 1) & (np.add.accumulate(rev, axis=1) == 1)
        ch = np.where(np.any(first, axis=1), np.add.reduce(first * k.reshape(2, 8, -1), axis=1), M)
        ent = O[s16[:, None], np.repeat(ch, 8, axis=0)]
        n = np.where(has & ~gone & ~first.reshape(16, -1), o, ent); hn = n < M
        w = np.where(hn[None], inner(L, R, n), -2 ** 23)
        l = np.where(np.any(hn[:8], axis=0)[None], np.max(w[:, :8], axis=1) - temp, xl)
        r = np.where(np.any(hn[8:], axis=0)[None], temp - np.max(w[:, 8:], axis=1), xr)
        low = l < r; mid = (l + r) >> 1
        nL[:, c] = np.where(low, mid, l); nR[:, c] = np.where(low, mid, r); nO[:, c] = n
        L, R, O = nL, nR, nO
    return {"yl": back(L), "yr": back(R), "yo": back(O)}

@@ -1,0 +1,623 @@
+import numpy as np
+from concourse.bass import DstId, RemoteDMATransfer
+from concourse.mybir import dt, AluOpType, AxisListType, ActivationFunctionType
+
+A_ = AluOpType
+COPY = ActivationFunctionType.Copy
+IDENT = ActivationFunctionType.Identity
+RELU = ActivationFunctionType.Relu
+SIGN = ActivationFunctionType.Sign
+G1, R1, B1 = 2880, 576, 192
+WC = 8 * G1
+EC = 43264
+BIG = 8388608.0
+PN = [576, 192, 192]
+
+
+def _f(n): return ("sbuf", [128, n], "float32")
+def _i(n): return ("sbuf", [128, n], "int32")
+def _b(n): return ("sbuf", [128, n], "bfloat16")
+def _u(n): return ("sbuf", [128, n], "uint16")
+
+
+SCRATCH = {
+    "W": _f(WC + B1), "LI": _i(192), "RI": _i(192), "OI": _i(192),
+    "SB0": _f(576), "SB1": _f(192), "SB2": _f(192), "SB3": _f(192), "NB0": _f(576), "NB1": _f(192), "NB2": _f(192),
+    "i1": _i(192), "i2": _i(192), "i3": _i(192), "f1": _f(192), "f2": _f(192), "f3": _f(192), "f4": _f(192), "CD": _f(192),
+    "PI": _i(1), "pc": _i(16), "fc": _f(40), "CI": _f(176), "REL": _f(176), "tmp": _f(176), "tmp2": _f(176),
+    "QF": _f(512), "QB": _b(512), "GF": _f(512), "EM": _b(176), "AD": _b(1120), "BM": _b(176), "C1": _b(144),
+    "LT": _b(128), "SL": _b(256), "ID": _b(128), "IDF": _f(512), "UPC": _b(192),
+    "j1": _i(32), "j2": _i(32), "j3": _i(32), "j4": _i(8), "j5": _i(8), "j6": _i(8), "j7": _i(8), "j8": _i(8),
+    "SEL": _u(16), "XBL": _u(32), "CDL": _u(12), "DSL": _u(8), "ZB": _b(128), "LU": _u(192), "LO": _u(192), "NO": _b(192),
+    "XR": _f(1536), "XN": _f(1536), "XW": _f(384), "RS": _f(1024),
+    "U": _f(1024), "T0": _f(1024), "T1": _f(1024), "TL": _f(1024), "D1": _f(512), "D2": _f(512),
+    "IA1": _b(512), "IB1": _b(512), "IA2": _b(512), "IB2": _b(512), "VR": _b(1024), "VL": _b(1024),
+    "K": _f(64), "kz": _f(64), "ky": _f(64), "kf": _f(64), "KH": _b(64), "KL": _b(64), "LKR": _u(64), "LKL": _u(64),
+    "m1": _b(64), "m2": _b(64), "GX": _b(64), "FI": _b(64), "REV": _b(64), "FH": _b(64), "FL": _b(64), "FG": _b(64),
+    "DP": _f(128), "DS": _f(128), "EN": _f(128), "CLS": _u(8),
+    "o1": _f(64), "o2": _f(64), "o3": _f(64), "n1": _f(64), "nz": _f(64), "ny": _f(64), "LN": _u(64),
+    "U2": _f(1024), "SC": _f(1024), "ww": _f(128), "wn": _f(128), "ws": _f(64), "wi": _i(128),
+    "YL": _f(64), "YO": _f(64), "yy": _f(192), "y4": _f(64),
+    "PZ1": ("psum", [128, 512], "float32"), "PZ2": ("psum", [128, 512], "float32"), "PCN": ("psum", [128, 512], "float32"),
+    "PPF": ("psum", [128, 512], "float32"), "PDM": ("psum", [128, 512], "float32"), "PCH": ("psum", [128, 512], "float32"),
+    "PP2": ("psum", [128, 512], "float32"), "PG2": ("psum", [128, 512], "float32"),
+    "DA0": ("dram", [256, 576], "float32"), "DA1": ("dram", [256, 192], "float32"), "DA2": ("dram", [256, 192], "float32"),
+}
+SEMAPHORES = ["qv", "qs", "qp", "qg", "ls", "ldO", "ldL", "ldR", "go1", "go2"] + [
+    "%s%d" % (k, e) for k in ("arr", "own", "nbd", "fA", "fB", "dA", "oO", "oR", "oL") for e in range(3)]
+
+
+def pl(bits):
+    return sum(1 << b for b in bits)
+
+
+def dst(topo, c):
+    rid, pid, _ = topo.addr(c)
+    return DstId(rid=rid, pnc=pid)
+
+
+def plan(T, topo):
+    cores = list(T.cores)
+    role, of, extra = {}, {}, []
+    for r, c in enumerate(cores):
+        near = [h for h in topo.cores_of(c) if topo.die(h) == topo.die(c) and h not in cores]
+        off = [q for q, d in enumerate(cores) if topo.chip(d) != topo.chip(c)]
+        extra += [(r, q) for q in off[len(near):]]
+        for q, h in zip(off, near):
+            role[h] = {"rank": r, "A": q, "feed": cores[q], "fwd": []}
+            of[(r, q)] = h
+    for (r, q), h in of.items():
+        if topo.die(cores[r]) != topo.die(cores[q]):
+            for r2 in range(len(cores)):
+                if r2 != r and topo.chip(cores[r2]) == topo.chip(cores[r]) and topo.die(cores[r2]) == topo.die(cores[q]):
+                    role[h]["feed"] = of[(r2, q)]
+                    role[of[(r2, q)]]["fwd"].append(h)
+    return cores, role, extra
+
+
+def calls_of(info, cores):
+    if info["feed"] in cores:
+        return [[0], [1, 2, 3, 4], [5, 6], [7]]
+    return [[0, 1, 2, 3, 4, 5, 6, 7]]
+
+
+def helper(g, core, T, topo, cores, role):
+    info = role[core]
+    rc = cores[info["rank"]]
+    eng = topo.engines(core, rc)
+    direct = info["feed"] in cores
+    ls = 0
+    for e in range(3):
+        n, buf, fa = PN[e], T["DA%d" % e], T.sem["fA%d" % e]
+        got = len(topo.engines(info["feed"], core)) * (1 if direct else 2)
+        g.wait_ge(fa, got)
+        if direct:
+            g.sync.wait_ge(fa, got)
+            g.sync.dma_start(buf[128:240, :], buf[0:112, :]).then_inc(T.sem["dA%d" % e], 16)
+        for h in info["fwd"]:
+            en = topo.engines(core, h)
+            g.remote_dma_fused([RemoteDMATransfer(dst_ids=[dst(topo, h)] * 2, dma_engine_mask=pl(en), remote_sem=fa,
+                                                  srcs=[buf[0:128, :]], dsts=[buf[0:128, :], buf[128:256, :]])], local_sem=T.sem.ls)
+            ls += len(en)
+        if e:
+            g.wait_ge(T.sem["go%d" % e], 1)
+        for ci, call in enumerate(calls_of(info, cores)):
+            if ci == 1:
+                g.wait_ge(T.sem["dA%d" % e], 16)
+            w = len(eng) // len(call)
+            trs = []
+            for j, k in enumerate(call):
+                c0 = k * G1 + info["A"] * R1 + (e - 1) * B1 * (e > 0)
+                trs.append(RemoteDMATransfer(dst_ids=[dst(topo, rc)], dma_engine_mask=pl(eng[j * w:(j + 1) * w]), remote_sem=T.sem["arr%d" % e],
+                                             srcs=[buf[16 * k:16 * k + 128, :]], dsts=[T.W[:, c0:c0 + n]]))
+                ls += w
+            g.remote_dma_fused(trs, local_sem=T.sem.ls)
+    g.wait_ge(T.sem.ls, ls)
+
+
+def rank_program(g, core, T, topo):
+    cores, role, extra = plan(T, topo)
+    rank = T.rank_of(core)
+    if rank is None:
+        if core in role:
+            helper(g, core, T, topo, cores, role)
+        return
+    mine = [h for h in role if role[h]["rank"] == rank]
+    near = [q for q, c in enumerate(cores) if q != rank and topo.chip(c) == topo.chip(core)]
+    arr_n = sum(16 * len(calls_of(role[h], cores)) for h in mine)
+    Q = {"v": g.vector, "s": g.scalar, "p": g.tensor, "g": g, "y": g.sync}
+    QS = {"v": "qv", "s": "qs", "p": "qp", "g": "qg"}
+    cnt, known, lastw, readers, lastx = {}, {q: {} for q in Q}, {}, {}, {}
+
+    def need(q, tok):
+        _, sem, c, clock = tok
+        if known[q].get(sem, 0) >= c:
+            return
+        Q[q].wait_ge(T.sem[sem], c)
+        for s2, c2 in clock.items():
+            known[q][s2] = max(known[q].get(s2, 0), c2)
+        known[q][sem] = max(known[q].get(sem, 0), c)
+
+    def deps(q, rd, wr, ps):
+        toks = []
+        for k in rd:
+            if k in lastw:
+                toks.append(lastw[k])
+        for k in wr:
+            if k in lastw:
+                toks.append(lastw[k])
+            toks += readers.get(k, [])
+        for k in ps:
+            if k in lastx:
+                toks += [t for t in lastx[k].values() if t[0] != q]
+        best = {}
+        for t in toks:
+            if q == "p" and t[0] == "p":
+                continue
+            if t[1] not in best or best[t[1]][2] < t[2]:
+                best[t[1]] = t
+        for t in sorted(best.values(), key=lambda t: -t[2]):
+            need(q, t)
+
+    def note(q, rd, wr, ps, tok):
+        for k in rd:
+            readers.setdefault(k, [])
+            readers[k] = [t for t in readers[k] if not (t[0] == q and t[1] == tok[1])] + [tok]
+        for k in wr:
+            lastw[k] = tok
+            readers[k] = []
+        for k in ps:
+            lastx.setdefault(k, {})
+            lastx[k][q] = tok
+
+    def op(q, fn, rd=(), wr=(), ps=()):
+        deps(q, rd, wr, ps)
+        sem = QS[q]
+        c = cnt.get(sem, 0) + 1
+        cnt[sem] = c
+        fn(Q[q]).then_inc(T.sem[sem], 1)
+        clock = dict(known[q])
+        clock[sem] = c
+        note(q, rd, wr, ps, (q, sem, c, clock))
+
+    def dma(q, sem, pairs, rd=(), wr=()):
+        deps(q, rd, wr, ())
+        for o, i in pairs:
+            Q[q].dma_start(o, i).then_inc(T.sem[sem], 16)
+        cnt[sem] = cnt.get(sem, 0) + 16 * len(pairs)
+        clock = dict(known[q])
+        clock[sem] = cnt[sem]
+        note(q, rd, wr, (), (q, sem, cnt[sem], clock))
+
+    def split(xs):
+        ks = [x[0] for x in xs if isinstance(x, tuple)]
+        return [k for k in ks if k[0] != "P" or k == "PI"], [k for k in ks if k[0] == "P" and k != "PI"]
+
+    def raw(x):
+        return x[1] if isinstance(x, tuple) else x
+
+    def emit(q, fn, ins, out):
+        r, rp = split(ins)
+        w, wp = split([out])
+        return op(q, fn, r, w, rp + wp)
+
+    def ts(out, a, s1, o1, s2=None, o2=None):
+        if o2 is None:
+            return emit("v", lambda e: e.tensor_scalar(raw(out), raw(a), raw(s1), None, o1), [a, s1], out)
+        return emit("v", lambda e: e.tensor_scalar(raw(out), raw(a), raw(s1), raw(s2), o1, o2), [a, s1, s2], out)
+
+    def tt(out, a, b, o, more=()):
+        return emit("v", lambda e: e.tensor_tensor(raw(out), raw(a), raw(b), o), [a, b] + list(more), out)
+
+    def cp(out, a, more=()):
+        return emit("v", lambda e: e.tensor_copy(raw(out), raw(a)), [a] + list(more), out)
+
+    def act(out, a, f=COPY, scale=1.0, more=(), bias=0.0):
+        return emit("s", lambda e: e.activation(raw(out), raw(a), f, bias=raw(bias), scale=scale), [a, bias] + list(more), out)
+
+    def mm(out, l, r, start, stop):
+        return emit("p", lambda e: e.matmul(raw(out), raw(l), raw(r), start, stop), [l, r], out)
+
+    def C(name, a, b=None, st=None):
+        return (name, T[name][:, a:b:st])
+
+    def X(name):
+        return (name, T[name][:])
+
+    dma("y", "ldO", [(T.OI[:], T.opts[:])], wr=["OI"])
+    dma("y", "ldR", [(T.RI[:], T.rw[:])], wr=["RI"])
+    dma("y", "ldL", [(T.LI[:], T.lw[:])], wr=["LI"])
+    op("g", lambda e: e.iota(T.PI[:], [[0, 1]], 0, 1), wr=["PI"])
+    op("g", lambda e: e.iota(T.j1[:], [[1, 32]], 0, 0), wr=["j1"])
+    op("g", lambda e: e.iota(T.CI[:], [[1, 176]], 0, 0, allow_small_or_imprecise_dtypes=True), wr=["CI"])
+    npc, nfc, nls = [0], [0], [0]
+
+    def icol(shop, val):
+        k = npc[0]
+        npc[0] += 1
+        o = ("pc%d" % k, T.pc[:, k:k + 1])
+        ts(o, X("PI"), val, shop)
+        return o
+
+    def newf():
+        k = nfc[0]
+        nfc[0] += 1
+        return ("fc%d" % k, T.fc[:, k:k + 1])
+
+    def fcol(a, s1, o1):
+        o = newf()
+        ts(o, a, s1, o1)
+        return o
+
+    hh = icol(A_.logical_shift_right, 4)
+    p3i = icol(A_.bitwise_and, 8)
+    p4i = icol(A_.bitwise_and, 16)
+    p15 = icol(A_.bitwise_and, 15)
+    p7 = icol(A_.bitwise_and, 7)
+    pg = icol(A_.bitwise_and, 96)
+    p120 = icol(A_.bitwise_and, 120)
+    ub = {1: icol(A_.bitwise_and, 1), 2: icol(A_.bitwise_and, 2), 4: icol(A_.bitwise_and, 4)}
+    H = fcol(hh, float(G1), A_.mult)
+    nH = fcol(hh, -float(G1), A_.mult)
+    n = X("OI")
+    ts(X("i1"), n, 1.0 / 192, A_.mult, -95.5 / 192, A_.add)
+    ts(X("i2"), n, 1.0 / 1536, A_.mult, -767.5 / 1536, A_.add)
+    ts(X("i3"), n, 1.0 / 64, A_.mult, -31.5 / 64, A_.add)
+    ts(X("f4"), n, 7680, A_.is_ge, EC - 2880.0, A_.mult)
+    ts(X("f1"), X("i1"), 2304, A_.mult)
+    ts(X("f2"), X("i2"), -22464, A_.mult)
+    ts(X("f3"), X("i3"), 128, A_.mult)
+    tt(X("f4"), X("f4"), n, A_.add)
+    tt(X("f1"), X("f1"), X("f2"), A_.add)
+    tt(X("f3"), X("f3"), X("f4"), A_.add)
+    for t in range(3):
+        b, w = t * B1, 64 * t
+        tt(C("SB0", b + 128, b + 192), C("f1", w, w + 64), C("f3", w, w + 64), A_.add)
+        cp(C("SB0", b, b + 64), C("RI", w, w + 64))
+        ts(C("SB0", b + 64, b + 128), C("LI", w, w + 64), -1.0, A_.mult)
+
+    def send(e, name):
+        deps("g", [name], [], ())
+        offs = [(h, T["DA%d" % e][0:128, :]) for h in role if role[h]["feed"] == core]
+        offs += [(cores[r], T["NB%d" % e][:]) for r, q in extra if q == rank]
+        en = topo.engines(core, offs[0][0])
+        trs = [RemoteDMATransfer(dst_ids=[dst(topo, h) for h, _ in offs], dma_engine_mask=pl(en), remote_sem=T.sem["fA%d" % e],
+                                 srcs=[T[name][:]], dsts=[d for _, d in offs])]
+        nls[0] += len(en)
+        for q in near:
+            e2 = [x for x in topo.engines(core, cores[q]) if x not in en]
+            trs.append(RemoteDMATransfer(dst_ids=[dst(topo, cores[q])], dma_engine_mask=pl(e2), remote_sem=T.sem["fB%d" % e],
+                                         srcs=[T[name][:]], dsts=[T["NB%d" % e][:]]))
+            nls[0] += len(e2)
+        g.remote_dma_fused(trs, local_sem=T.sem.ls)
+
+    def put(qu, e, sem, name, src, rd):
+        nn = PN[e]
+        c0 = src * R1 + (e - 1) * B1 * (e > 0)
+        pairs = [(T.W[:, c0:c0 + nn], T[name][:])]
+        for k in range(1, 8):
+            c = c0 + k * G1
+            pairs.append((T.W[0:128 - 16 * k, c:c + nn], T[name][16 * k:128, :]))
+            pairs.append((T.W[128 - 16 * k:128, c:c + nn], T[name][0:16 * k, :]))
+        dma(qu, sem + str(e), pairs, rd=rd, wr=[sem])
+
+    def spread(e, name):
+        deps("s", [], ["W"], ())
+        deps("y", [], ["W"], ())
+        put("s", e, "own", name, rank, [name])
+        for q in near + [q for r, q in extra if r == rank]:
+            h = [h for h in role if role[h]["feed"] == cores[q]][0]
+            en = topo.engines(cores[q], core)
+            Q["y"].wait_ge(T.sem["f%s%d" % ("B" if q in near else "A", e)],
+                           len([x for x in en if x not in topo.engines(cores[q], h)] if q in near else en))
+            put("y", e, "nbd", "NB%d" % e, q, [])
+
+    send(0, "SB0")
+    spread(0, "SB0")
+    op("g", lambda e: e.iota(T.RS[:], [[0, 1024]], 0, 0, allow_small_or_imprecise_dtypes=True), wr=["RS"])
+    op("g", lambda e: e.affine_select(T.RS[:], T.RS[:], [[0, 128], [1, 8]], A_.not_equal, -2.0 ** 25, 0, 0), rd=["RS"], wr=["RS"])
+    nH64 = fcol(nH, 64.0, A_.add)
+    nH128 = fcol(nH, 128.0, A_.add)
+    p15f = fcol(p15, 1.0, A_.mult)
+    p3f = fcol(p3i, 1.0, A_.mult)
+    pf = fcol(X("PI"), 1.0, A_.mult)
+    j5 = X("j5")
+    ts(j5, C("j1", 0, 8), 16, A_.mult, p15f, A_.add)
+    ts(X("j6"), j5, 5, A_.logical_shift_right)
+    ts(X("j7"), j5, 24, A_.bitwise_and)
+    ts(X("j8"), j5, 7, A_.bitwise_and)
+    ts(X("j6"), X("j6"), 192, A_.mult, 128, A_.add)
+    ts(X("j7"), X("j7"), 2, A_.mult)
+    tt(X("j8"), X("j8"), X("j6"), A_.add)
+    tt(X("j8"), X("j8"), X("j7"), A_.add)
+    cp(C("CDL", 0, 6), C("j8", 0, 6))
+    ts(C("CDL", 6, 12), C("j8", 0, 6), 8, A_.add)
+    act(X("CD"), ("SB0", T.SB0[:].indirect(T.CDL[:])), more=[("CDL", 0)])
+    ts(X("j2"), X("j1"), 24, A_.bitwise_and)
+    ts(X("j3"), X("j1"), 7, A_.bitwise_and)
+    ts(X("j2"), X("j2"), 2, A_.mult, p3f, A_.add)
+    tt(X("j2"), X("j2"), X("j3"), A_.add)
+    cp(X("XBL"), X("j2"))
+    temp = fcol(p15, 1024.0, A_.mult)
+    ntemp = fcol(temp, -1.0, A_.mult)
+
+    def own_walls(t):
+        b = t * B1
+        act(C("XR", 512 * t, 512 * t + 512), ("SB0", T.SB0[:, b:b + 64].indirect(T.XBL[:])), more=[("XBL", 0)])
+        act(C("XN", 512 * t, 512 * t + 512), ("SB0", T.SB0[:, b + 64:b + 128].indirect(T.XBL[:])), more=[("XBL", 0)])
+        act(C("XW", 128 * t, 128 * t + 64), C("SB0", b + 64, b + 128), IDENT, scale=-1.0, bias=temp)
+        act(C("XW", 128 * t + 64, 128 * t + 128), C("SB0", b, b + 64), IDENT, scale=-1.0, bias=temp)
+
+    def sel2(base, col, big, full):
+        x, y0, y1, y2 = newf(), newf(), newf(), newf()
+        ts(x, col, big, A_.mult)
+        tt(y0, base, x, A_.add)
+        tt(y1, base, x, A_.subtract)
+        ts(y2, y1, full, A_.add)
+        return y0, y2
+
+    A3 = sel2(pf, p3i, 125.0, 1000.0)
+    for a in range(2):
+        for b in range(2):
+            o = 128 * (2 * a + b)
+            ts(C("QF", o, o + 128), C("CI", 0, 128), -8.0 * (b - a), A_.add, A3[a], A_.is_equal)
+    act(X("QB"), X("QF"))
+    gb = fcol(p3i, 2.0, A_.mult)
+    gc, gd = newf(), newf()
+    tt(gc, gb, pg, A_.add)
+    tt(gd, gc, p7, A_.add)
+    A4 = sel2(gd, p4i, 100.0, 1600.0)
+    for b in range(2):
+        for a in range(2):
+            o = 128 * (2 * b + a)
+            ts(C("GF", o, o + 128), C("CI", 0, 128), -8.0 * a, A_.add, A4[b], A_.is_equal)
+    for bank, M in (("PP2", "QF"), ("PG2", "GF")):
+        for x in range(2):
+            for a in range(2):
+                o = 128 * (2 * x + a)
+                mm(C(bank, 96 * x, 96 * x + 96), C(M, o, o + 128), C("CD", 96 * a, 96 * a + 96), a == 0, a == 1)
+    op("v", lambda e: e.memset(T.W[:, WC:WC + 128], -BIG), wr=["Wemp"])
+    op("v", lambda e: e.memset(T.W[:, WC + 128:WC + 192], float(EC)), wr=["Wemp"])
+    ts(X("f1"), C("PP2", 0, 192), H, A_.is_lt, float(WC), A_.mult)
+    tt(X("f2"), X("f1"), C("PP2", 0, 192), A_.add)
+    ts(X("f3"), C("PG2", 0, 192), H, A_.is_lt, float(WC), A_.mult)
+    tt(X("f4"), X("f3"), C("PG2", 0, 192), A_.add)
+
+    def lists(t):
+        for side in range(2):
+            i, o = 96 * side + 32 * t, 64 * t + 32 * side
+            ts(C("LU", o, o + 32), C("f2", i, i + 32), nH64 if side else nH, A_.add, float(WC + 64 * side), A_.min)
+        for b in range(2):
+            ts(C("LO", 64 * t + b, 64 * t + 64, 2), C("f4", 96 * b + 32 * t, 96 * b + 32 * t + 32), nH128, A_.add, float(WC + 128), A_.min)
+
+    def empties(t):
+        for side in range(2):
+            i, o = 96 * side + 32 * t, 64 * t + 32 * side
+            ts(C("NO", o, o + 32), C("f2", i, i + 32), EC - 32.0, A_.is_ge)
+
+    lists(0)
+    h16 = fcol(hh, 16.0, A_.mult)
+    ts(X("REL"), X("CI"), h16, A_.subtract)
+    ts(X("EM"), X("REL"), 24.0, A_.is_equal)
+    act(X("BM"), X("EM"), scale=-2.0 ** 30)
+
+    def diffs(ds, hbs):
+        for d in ds:
+            tt(C("AD", 160 * d, 160 * d + 160), C("EM", 8, 168), C("EM", 8 - d, 168 - d), A_.subtract)
+        for hb in hbs:
+            u = fcol(ub[hb], 0.5 / hb, A_.mult)
+            ts(C("UPC", 64 * (hb // 2), 64 * (hb // 2) + 64), C("CI", 0, 64), 0.0, A_.mult, u, A_.add)
+
+    ts(X("ID"), C("CI", 0, 128), pf, A_.is_equal)
+    diffs((1, 4), (1, 4))
+    ts(X("j6"), j5, 31, A_.bitwise_and)
+    ts(X("j7"), j5, 5, A_.logical_shift_right)
+    ts(X("j6"), X("j6"), 32, A_.mult, 8, A_.add)
+    ts(X("j7"), X("j7"), 8, A_.mult)
+    tt(X("j6"), X("j6"), X("j7"), A_.add)
+
+    def sels(t):
+        ts(X("j4"), j5, t, A_.add)
+        ts(X("j4"), X("j4"), 7, A_.bitwise_and)
+        tt(X("j4"), X("j4"), X("j6"), A_.add)
+        cp(C("SEL", 4 * t, 4 * t + 4), C("j4", 0, 4))
+
+    sels(0)
+    own_walls(0)
+    act(X("PP2"), C("XN", 0, 512))
+    for j, f in enumerate((1.0, -7488.0, 1344.0, -128.0)):
+        act(C("IDF", 128 * j, 128 * j + 128), X("ID"), scale=f)
+    empties(0)
+    p8f = fcol(p120, 1.0, A_.mult)
+    ts(X("tmp"), X("CI"), p8f, A_.subtract)
+    ts(X("C1"), C("tmp", 0, 144), 8.0, A_.is_equal)
+    ts(C("tmp2", 0, 128), C("tmp", 0, 128), 8.0, A_.is_lt)
+    ts(C("tmp", 0, 128), C("CI", 0, 128), pf, A_.is_gt)
+    tt(C("tmp2", 0, 128), C("tmp2", 0, 128), C("tmp", 0, 128), A_.mult)
+    ts(C("tmp", 0, 128), C("CI", 0, 128), pf, A_.is_equal, -0.5, A_.mult)
+    tt(X("LT"), C("tmp2", 0, 128), C("tmp", 0, 128), A_.add)
+    EH = fcol(nH, EC + 128.0, A_.add)
+    s64 = fcol(p3i, 8.0, A_.mult)
+    capN = fcol(s64, float(WC), A_.add)
+    nHs = newf()
+    tt(nHs, s64, nH, A_.add)
+    big1 = fcol(p3i, -BIG / 8, A_.mult)
+    big0 = newf()
+    ts(big0, big1, -1.0, A_.mult, -BIG, A_.add)
+    ts(C("tmp", 0, 128), C("REL", 0, 128), 0.0, A_.is_ge)
+    ts(C("tmp2", 0, 128), C("REL", 0, 128), 16.0, A_.is_lt)
+    tt(C("tmp", 0, 128), C("tmp", 0, 128), C("tmp2", 0, 128), A_.mult)
+    ts(C("SL", 0, 128), C("tmp", 0, 128), big0, A_.mult)
+    ts(C("SL", 128, 256), C("tmp", 0, 128), big1, A_.mult)
+    op("v", lambda e: e.memset(T.ZB[:], 0.0), wr=["ZB"])
+
+    def win(L, lo, hi):
+        return ("W", T.W[:].indirect(T[L][:, lo:hi]))
+
+    def wm(L):
+        return [(L, 0), ("own", 0), ("nbd", 0), ("Wemp", 0)]
+
+    for t in range(3):
+        xb = 512 * t
+        for q in "vs":
+            Q[q].wait_ge(T.sem["arr%d" % t], arr_n)
+        cp(("Ua", T.U[:, 0:512]), win("LU", 64 * t, 64 * t + 32), more=wm("LU"))
+        act(("Ub", T.U[:, 512:1024]), win("LU", 64 * t + 32, 64 * t + 64), more=wm("LU"))
+        act(X("T0"), win("LO", 64 * t, 64 * t + 64), more=wm("LO"))
+        for z, k in enumerate((1 + t % 7, 1 + (t + 3) % 7)):
+            D, IA, IB, PZ = "D%d" % (z + 1), "IA%d" % (z + 1), "IB%d" % (z + 1), "PZ%d" % (z + 1)
+            hb = 4 if k >= 4 else 2 if k >= 2 else 1
+            m = 4 // hb
+            off, where = 0, {}
+            for r in range(2 * hb):
+                if r & hb:
+                    continue
+                tt((D, T[D][:, off:off + 128 * m]), ("Ua", T.U[:, r ^ k::2 * hb]), ("Ub", T.U[:, r::2 * hb]), A_.subtract)
+                for i in range(m):
+                    where[r + 2 * hb * i] = off + i
+                off += 128 * m
+            act(X(IA), X(D), RELU)
+            act(X(IB), X(D), RELU, scale=-1.0)
+            o = C(PZ, 0, 64)
+            mm(o, X("ID"), C("UPC", 64 * (hb // 2), 64 * (hb // 2) + 64), True, False)
+            todo = [(a, s, x) for x in (0, 1) for a in range(2) for s in sorted(where)]
+            for i, (a, s, x) in enumerate(todo):
+                qs, lo, d = 8 * a + s, where[s] + a * m, (s ^ k) - s
+                l = C("BM", 24 - qs, 152 - qs) if x else C("AD", 160 * d + 16 - qs, 160 * d + 144 - qs)
+                mm(o, l, C(IB if x else IA, lo, lo + 2 * m * 63 + 1, 2 * m), False, i == len(todo) - 1)
+        emit("v", lambda e: e.transpose(T.T1[:], T.T0[:]), [("T0", 0)], ("T1", 0))
+        cp(X("K"), ("T1", T.T1[:].indirect(T.SEL[:, 4 * t:4 * t + 4])), more=[("SEL", 0)])
+        ts(X("kz"), X("K"), H, A_.is_lt, float(WC), A_.mult)
+        tt(X("ky"), X("kz"), X("K"), A_.add)
+        ts(X("LKL"), X("ky"), nH64, A_.add, float(WC + 64), A_.min)
+        ts(X("LKR"), X("ky"), nH, A_.add, float(WC), A_.min)
+        for side in range(2):
+            act(("TL%d" % side, T.TL[:, 512 * side:512 * side + 512]), win("LKL", 32 * side, 32 * side + 32), more=wm("LKL"))
+            tt(C("VR", 512 * side, 512 * side + 512), win("LKR", 32 * side, 32 * side + 32), C("XR", xb, xb + 512), (A_.is_gt, A_.is_lt)[side], more=wm("LKR"))
+        o = C("PCN", 0, 64)
+        for i in range(16):
+            mm(o, C("EM", 24 - i, 152 - i), C("VR", i, None, 16), i == 0, False)
+        mm(C("PDM", 0, 128), X("ID"), X("ZB"), True, False)
+        for par in range(2):
+            for side in range(2):
+                c = slice(512 * side + par, 512 * side + 512, 2)
+                tt(("VL%d" % par, T.VL[:, c]), ("TL%d" % side, T.TL[:, c]), C("PP2", par, 512, 2), (A_.is_lt, A_.is_gt)[side])
+        if t == 0:
+            p34 = fcol(p3i, 4.0, A_.mult)
+            p347 = newf()
+            tt(p347, p34, p7, A_.add)
+            ts(C("j2", 0, 8), C("j1", 0, 8), 4, A_.bitwise_and)
+            ts(C("j3", 0, 8), C("j1", 0, 8), 3, A_.bitwise_and)
+            ts(C("j2", 0, 8), C("j2", 0, 8), 16, A_.mult, p347, A_.add)
+            ts(C("j3", 0, 8), C("j3", 0, 8), 8, A_.mult)
+            tt(C("j2", 0, 8), C("j2", 0, 8), C("j3", 0, 8), A_.add)
+            cp(X("DSL"), C("j2", 0, 8))
+        for z in (1, 2):
+            act(X("m%d" % z), C("PZ%d" % z, 0, 64), RELU, bias=-0.25)
+        o = C("PZ1", 64, 128)
+        mm(o, X("ID"), C("NO", 64 * t, 64 * t + 64), True, False)
+        mm(o, X("ID"), X("m1"), False, False)
+        mm(o, X("ID"), X("m2"), False, True)
+        act(X("kf"), X("ky"), IDENT, bias=-float(EC))
+        act(X("KH"), X("kf"))
+        act(X("GX"), o, SIGN)
+        tt(X("KL"), X("kf"), X("KH"), A_.subtract)
+        o = C("PCN", 0, 64)
+        for i in list(range(0, 16, 2)) + list(range(1, 16, 2)):
+            mm(o, C("EM", 24 - i, 152 - i), ("VL%d" % (i % 2), T.VL[:, i::16]), False, False)
+        mm(o, X("ID"), X("GX"), False, True)
+        dm = [(C("PDM", 64 * side + 32 * a, 64 * side + 32 * a + 32), C("QB", 128 * (2 * a + side), 128 * (2 * a + side) + 128), 32 * side)
+              for side in range(2) for a in range(2)]
+        for oo, l, w in dm:
+            mm(oo, l, C("GX", w, w + 32), False, False)
+        ts(X("REV"), o, 0.0, A_.is_equal)
+        mm(C("PPF", 0, 64), X("LT"), X("REV"), True, True)
+        ts(X("FI"), C("PPF", 0, 64), 0.0, A_.is_lt)
+        tt(X("FH"), X("FI"), X("KH"), A_.mult)
+        tt(X("FL"), X("FI"), X("KL"), A_.mult)
+        for j, (oo, l, w) in enumerate(dm):
+            mm(oo, l, C("FI", w, w + 32), False, j == 3)
+        o = C("PCH", 0, 8)
+        for x in ("FH", "FL"):
+            for c in range(8):
+                mm(o, C("C1", 8 - c, 136 - c), C(x, c, None, 8), x == "FH" and c == 0, x == "FL" and c == 7)
+        oc = C("SB0", t * B1 + 128, t * B1 + 192)
+        act(X("DP"), C("PDM", 0, 128))
+        act(X("DS"), ("DP", T.DP[:].indirect(T.DSL[:])), more=[("DSL", 0)])
+        tt(X("o1"), C("DS", 0, 64), C("DS", 64, 128), A_.add)
+        tt(X("o2"), X("o1"), oc, A_.mult)
+        ts(X("CLS"), o, EH, A_.add, float(WC + 128), A_.min)
+        sides = (("PPF", 0), ("PCH", 1))
+        for b, side in sides:
+            w = 128 * t + 64 * side
+            mm(C(b, 64, 128), C("IDF", 0, 128), C("XW", w, w + 64), True, False)
+        tt(X("o3"), oc, X("o2"), A_.subtract)
+        tt(X("EN"), win("CLS", 0, 8), X("DS"), A_.mult, more=wm("CLS"))
+        tt(X("n1"), C("EN", 0, 64), C("EN", 64, 128), A_.add)
+        sb = "SB%d" % (t + 1)
+        nw = C(sb, 128, 192)
+        tt(nw, X("n1"), X("o3"), A_.add)
+        ts(X("nz"), nw, H, A_.is_lt, float(WC), A_.mult)
+        tt(X("ny"), X("nz"), nw, A_.add)
+        ts(X("LN"), X("ny"), nHs, A_.add, capN, A_.min)
+        cp(("U2a", T.U2[:, 0:384]), win("LN", 0, 24), more=wm("LN"))
+        act(("U2b", T.U2[:, 384:1024]), win("LN", 24, 64), more=wm("LN"))
+        act(X("FG"), nw, IDENT, scale=-1.0, bias=float(EC))
+        for b, side in sides:
+            mm(C(b, 64, 128), C("SL", 128 * side, 128 * side + 128), X("FG"), False, True)
+        if t < 2:
+            need("g", lastw["U2a"])
+            need("g", lastw["U2b"])
+            g.remote_dma_fused([RemoteDMATransfer(dst_ids=[dst(topo, h)], dma_engine_mask=1 << topo.engines(core, h)[j],
+                                                  remote_sem=T.sem["go%d" % (t + 1)]) for j, h in enumerate(mine)], local_sem=T.sem.ls)
+            nls[0] += len(mine)
+
+        def numbers():
+            ts(X("y4"), nw, float(WC), A_.is_ge, 4736.0, A_.mult)
+            ys = [("yy%d" % j, T.yy[:, 64 * j:64 * j + 64]) for j in range(3)]
+            for j, d in enumerate((2880, 576, 192)):
+                act(ys[j], nw, IDENT, scale=1.0 / d, bias=-(d - 1) / 2.0 / d)
+            for big in (12582912.0, -12582912.0):
+                for y in ys:
+                    act(y, y, IDENT, bias=big)
+            o = C("PG2", 0, 64)
+            for j, r in enumerate([nw, X("y4")] + ys):
+                w = max(0, j - 1)
+                mm(o, C("IDF", 128 * w, 128 * w + 128), r, j == 0, j == 4)
+            act(X("YO"), o)
+            dma("y", "oO%d" % t, [(T.yo[:, 64 * t:64 * t + 64], T.YO[:])], rd=["YO"])
+
+        if t == 2:
+            numbers()
+        for hf, lo, hi in (("a", 0, 384), ("b", 384, 1024)):
+            emit("v", lambda e, c=slice(lo, hi): e.tensor_tensor_scan(T.SC[:, c], T.RS[:, c], T.U2[:, c], 0.0, A_.add, A_.max),
+                 [("RS", 0), ("U2" + hf, 0)], ("SC" + hf, 0))
+        for b, side in sides:
+            tt(C("ww", 64 * side, 64 * side + 64), C("SC", 7 + 8 * side, None, 16), C(b, 64, 128), A_.max, more=[("SCa", 0), ("SCb", 0)])
+        act(C("wn", 0, 64), C("ww", 64, 128), IDENT, scale=-1.0, bias=temp)
+        act(C("wn", 64, 128), C("ww", 0, 64), IDENT, scale=-1.0 if t < 2 else 1.0, bias=temp if t < 2 else ntemp)
+        tt(X("ws"), C("ww", 0, 64), C("ww", 64, 128), A_.subtract)
+        ts(C("wi", 0, 64), X("ws"), 0.5, A_.mult, -0.25, A_.add)
+        if t < 2:
+            ts(C("wi", 64, 128), X("ws"), -0.5, A_.mult, 0.25, A_.add)
+            tt(C(sb, 0, 128), X("wn"), X("wi"), A_.min)
+            send(t + 1, sb)
+            spread(t + 1, sb)
+            act(X("YL"), C(sb, 64, 128), scale=-1.0)
+        else:
+            tt(C(sb, 0, 64), C("wn", 0, 64), C("wi", 0, 64), A_.min)
+            tt(X("YL"), C("wn", 64, 128), C("wi", 0, 64), A_.max)
+        dma("y", "oR%d" % t, [(T.yr[:, 64 * t:64 * t + 64], T[sb][:, 0:64])], rd=[sb])
+        dma("y", "oL%d" % t, [(T.yl[:, 64 * t:64 * t + 64], T.YL[:])], rd=["YL"])
+        if t < 2:
+            lists(t + 1)
+            sels(t + 1)
+            own_walls(t + 1)
+            act(X("PP2"), C("XN", 512 * t + 512, 512 * t + 1024))
+            empties(t + 1)
+            diffs(((2, 3, 5), (6,))[t], ((2,), ())[t])
+            numbers()
+    g.wait_ge(T.sem.ls, nls[0])
+    for sem, c in cnt.items():
+        if known["g"].get(sem, 0) < c:
+            g.wait_ge(T.sem[sem], c)

@@ -7,11 +7,13 @@ COPY = ActivationFunctionType.Copy
 IDENT = ActivationFunctionType.Identity
 RELU = ActivationFunctionType.Relu
 SIGN = ActivationFunctionType.Sign
-G1, R1, B1 = 2880, 576, 192
-WC = 8 * G1
-EC = 43264
+ABS = ActivationFunctionType.Abs
+G1, R1, B1 = 2304, 384, 128
+WC = 4 * G1
+EC = 5 * R1
 BIG = 8388608.0
-PN = [576, 192, 192]
+PN = [384, 128, 128]
+KS = [(1, 4), (2, 5), (3, 6)]
 
 
 def _f(n): return ("sbuf", [128, n], "float32")
@@ -21,30 +23,31 @@ def _u(n): return ("sbuf", [128, n], "uint16")
 
 
 SCRATCH = {
-    "W": _f(WC + B1), "LI": _i(192), "RI": _i(192), "OI": _i(192),
-    "SB0": _f(576), "SB1": _f(192), "SB2": _f(192), "SB3": _f(192), "NB0": _f(576), "NB1": _f(192), "NB2": _f(192),
-    "i1": _i(192), "i2": _i(192), "i3": _i(192), "f1": _f(192), "f2": _f(192), "f3": _f(192), "f4": _f(192), "CD": _f(192),
-    "PI": _i(1), "pc": _i(16), "fc": _f(40), "CI": _f(176), "REL": _f(176), "tmp": _f(176), "tmp2": _f(176),
-    "QF": _f(512), "QB": _b(512), "GF": _f(512), "EM": _b(176), "AD": _b(1120), "BM": _b(176), "C1": _b(144),
-    "LT": _b(128), "SL": _b(256), "ID": _b(128), "IDF": _f(512), "UPC": _b(192),
-    "j1": _i(32), "j2": _i(32), "j3": _i(32), "j4": _i(8), "j5": _i(8), "j6": _i(8), "j7": _i(8), "j8": _i(8),
-    "SEL": _u(16), "XBL": _u(32), "CDL": _u(12), "DSL": _u(8), "ZB": _b(128), "LU": _u(192), "LO": _u(192), "NO": _b(192),
-    "XR": _f(1536), "XN": _f(1536), "XW": _f(384), "RS": _f(1024),
-    "U": _f(1024), "T0": _f(1024), "T1": _f(1024), "TL": _f(1024), "D1": _f(512), "D2": _f(512),
-    "IA1": _b(512), "IB1": _b(512), "IA2": _b(512), "IB2": _b(512), "VR": _b(1024), "VL": _b(1024),
-    "K": _f(64), "kz": _f(64), "ky": _f(64), "kf": _f(64), "KH": _b(64), "KL": _b(64), "LKR": _u(64), "LKL": _u(64),
-    "m1": _b(64), "m2": _b(64), "GX": _b(64), "FI": _b(64), "REV": _b(64), "FH": _b(64), "FL": _b(64), "FG": _b(64),
-    "DP": _f(128), "DS": _f(128), "EN": _f(128), "CLS": _u(8),
-    "o1": _f(64), "o2": _f(64), "o3": _f(64), "n1": _f(64), "nz": _f(64), "ny": _f(64), "LN": _u(64),
-    "U2": _f(1024), "SC": _f(1024), "ww": _f(128), "wn": _f(128), "ws": _f(64), "wi": _i(128),
-    "YL": _f(64), "YO": _f(64), "yy": _f(192), "y4": _f(64),
-    "PZ1": ("psum", [128, 512], "float32"), "PZ2": ("psum", [128, 512], "float32"), "PCN": ("psum", [128, 512], "float32"),
-    "PPF": ("psum", [128, 512], "float32"), "PDM": ("psum", [128, 512], "float32"), "PCH": ("psum", [128, 512], "float32"),
-    "PP2": ("psum", [128, 512], "float32"), "PG2": ("psum", [128, 512], "float32"),
-    "DA0": ("dram", [256, 576], "float32"), "DA1": ("dram", [256, 192], "float32"), "DA2": ("dram", [256, 192], "float32"),
+    "WW": _f(WC), "WO": _b(WC), "WI": _i(384), "OI": _i(192),
+    "SW0": _f(384), "SW1": _f(128), "SW2": _f(128), "SO0": _b(384), "SO1": _b(128), "SO2": _b(128), "SO3": _b(128),
+    "NW0": _f(384), "NW1": _f(128), "NW2": _f(128), "NO0": _b(384), "NO1": _b(128), "NO2": _b(128),
+    "PI": _i(1), "pc": _i(16), "fc": _f(128), "CI": _f(176), "tmp": _f(176), "tb": _b(176), "tb2": _b(176),
+    "EH": _b(256), "EL": _b(256), "MS": _b(1280), "fl": _b(960), "ni": _i(192), "OZ": _b(384), "OW": _b(384),
+    "jx": _i(32), "js": _i(8), "RS": _f(384),
+    "ID": _b(128), "SWB": _b(128), "NSW": _f(128), "TMPT": _b(128), "PLM": _b(136), "ED": _b(420), "EMS": _b(192), "EMB": _b(192),
+    "AD": _b(144 * 15), "UPC": _b(192), "EWP": _b(160), "EWN": _b(160), "KM": _b(320), "KZ": _b(320), "KZF": _f(320), "CM": _b(144),
+    "DM": _b(256), "LT": _b(128), "SLM": _b(128), "ZB": _b(160), "ON": _b(192), "SG": _b(160), "NM": _b(432),
+    "SEL": _u(24), "XBL": _u(32), "LU": _u(192), "LD": _u(288), "NE": _b(192),
+    "T0": _b(1024), "T1": _b(1024), "PK": _b(128), "PW": _b(64), "pz": _b(64), "LK": _u(128), "KH": _b(64), "KL": _b(64),
+    "XL": _f(512), "U1": _f(512), "D1": _b(512), "D2": _b(512), "IA1": _b(512), "IB1": _b(512), "IA2": _b(512), "IB2": _b(512),
+    "TL": _f(1536), "VI": _b(2048), "m1": _b(64), "m2": _b(64), "GX": _b(64), "REV": _b(64), "FI": _b(64), "FH": _b(64), "FL": _b(64),
+    "CLS": _u(8), "dd": _f(128), "ee": _f(128), "zN": _b(128), "FG": _b(128), "LN": _u(64), "U2": _f(1024), "SC": _f(1024),
+    "ww": _f(128), "ws": _f(128), "wi": _i(128), "wn": _f(128), "nA": _b(128), "nB": _b(128), "YR": _f(192), "YL": _f(192), "YO": _f(192),
+    "PX0": ("psum", [128, 512], "float32"), "PX1": ("psum", [128, 512], "float32"), "PZ1": ("psum", [128, 512], "float32"),
+    "PZ2": ("psum", [128, 512], "float32"), "PCN": ("psum", [128, 512], "float32"), "PPF": ("psum", [128, 512], "float32"),
+    "PCH": ("psum", [128, 512], "float32"), "PDM": ("psum", [128, 512], "float32"),
+    "DW0": ("dram", [256, 384], "float32"), "DW1": ("dram", [256, 128], "float32"), "DW2": ("dram", [256, 128], "float32"),
+    "DO0": ("dram", [256, 384], "bfloat16"), "DO1": ("dram", [256, 128], "bfloat16"), "DO2": ("dram", [256, 128], "bfloat16"),
 }
-SEMAPHORES = ["qv", "qs", "qp", "qg", "ls", "ldO", "ldL", "ldR", "go1", "go2"] + [
-    "%s%d" % (k, e) for k in ("arr", "own", "nbd", "fA", "fB", "dA", "oO", "oR", "oL") for e in range(3)]
+SEMAPHORES = ["qv", "qs", "qp", "qg", "ls", "ldO", "ldW", "go1", "go2"] + [
+    "%s%s%d" % (k, x, e) for k in ("arr", "own", "nbd", "fA", "fB", "dA") for x in "WO" for e in range(3)] + [
+    "%s%d" % (k, e) for k in ("oO", "oR", "oL") for e in range(1, 3)]
+ORDER = ["WO", "OW", "OW"]
 
 
 def pl(bits):
@@ -54,6 +57,10 @@ def pl(bits):
 def dst(topo, c):
     rid, pid, _ = topo.addr(c)
     return DstId(rid=rid, pnc=pid)
+
+
+def par(x):
+    return bin(x).count("1") & 1
 
 
 def plan(T, topo):
@@ -75,12 +82,6 @@ def plan(T, topo):
     return cores, role, extra
 
 
-def calls_of(info, cores):
-    if info["feed"] in cores:
-        return [[0], [1, 2, 3, 4], [5, 6], [7]]
-    return [[0, 1, 2, 3, 4, 5, 6, 7]]
-
-
 def helper(g, core, T, topo, cores, role):
     info = role[core]
     rc = cores[info["rank"]]
@@ -88,28 +89,29 @@ def helper(g, core, T, topo, cores, role):
     direct = info["feed"] in cores
     ls = 0
     for e in range(3):
-        n, buf, fa = PN[e], T["DA%d" % e], T.sem["fA%d" % e]
-        got = len(topo.engines(info["feed"], core)) * (1 if direct else 2)
-        g.wait_ge(fa, got)
-        if direct:
-            g.sync.wait_ge(fa, got)
-            g.sync.dma_start(buf[128:240, :], buf[0:112, :]).then_inc(T.sem["dA%d" % e], 16)
-        for h in info["fwd"]:
-            en = topo.engines(core, h)
-            g.remote_dma_fused([RemoteDMATransfer(dst_ids=[dst(topo, h)] * 2, dma_engine_mask=pl(en), remote_sem=fa,
-                                                  srcs=[buf[0:128, :]], dsts=[buf[0:128, :], buf[128:256, :]])], local_sem=T.sem.ls)
-            ls += len(en)
-        if e:
-            g.wait_ge(T.sem["go%d" % e], 1)
-        for ci, call in enumerate(calls_of(info, cores)):
-            if ci == 1:
-                g.wait_ge(T.sem["dA%d" % e], 16)
-            w = len(eng) // len(call)
+        for x in ORDER[e]:
+            n, buf, fa = PN[e], T["D%s%d" % (x, e)], T.sem["fA%s%d" % (x, e)]
+            got = len(topo.engines(info["feed"], core)) * (1 if direct else 2)
+            g.wait_ge(fa, got)
+            if direct:
+                g.sync.wait_ge(fa, got)
+                g.sync.dma_start(buf[128:224, :], buf[0:96, :]).then_inc(T.sem["dA%s%d" % (x, e)], 16)
+            for h in info["fwd"]:
+                en = topo.engines(core, h)
+                g.remote_dma_fused([RemoteDMATransfer(dst_ids=[dst(topo, h)] * 2, dma_engine_mask=pl(en), remote_sem=fa,
+                                                      srcs=[buf[0:128, :]], dsts=[buf[0:128, :], buf[128:256, :]])], local_sem=T.sem.ls)
+                ls += len(en)
+            if e and x == ORDER[e][0]:
+                g.wait_ge(T.sem["go%d" % e], 1)
+            if direct:
+                g.wait_ge(T.sem["dA%s%d" % (x, e)], 16)
+            w = len(eng) // 4
             trs = []
-            for j, k in enumerate(call):
+            for k in range(4):
                 c0 = k * G1 + info["A"] * R1 + (e - 1) * B1 * (e > 0)
-                trs.append(RemoteDMATransfer(dst_ids=[dst(topo, rc)], dma_engine_mask=pl(eng[j * w:(j + 1) * w]), remote_sem=T.sem["arr%d" % e],
-                                             srcs=[buf[16 * k:16 * k + 128, :]], dsts=[T.W[:, c0:c0 + n]]))
+                trs.append(RemoteDMATransfer(dst_ids=[dst(topo, rc)], dma_engine_mask=pl(eng[k * w:(k + 1) * w]),
+                                             remote_sem=T.sem["arr%s%d" % (x, e)],
+                                             srcs=[buf[32 * k:32 * k + 128, :]], dsts=[T["W" + x][:, c0:c0 + n]]))
                 ls += w
             g.remote_dma_fused(trs, local_sem=T.sem.ls)
     g.wait_ge(T.sem.ls, ls)
@@ -124,7 +126,7 @@ def rank_program(g, core, T, topo):
         return
     mine = [h for h in role if role[h]["rank"] == rank]
     near = [q for q, c in enumerate(cores) if q != rank and topo.chip(c) == topo.chip(core)]
-    arr_n = sum(16 * len(calls_of(role[h], cores)) for h in mine)
+    arr_n = sum(len(topo.engines(h, core)) for h in mine)
     Q = {"v": g.vector, "s": g.scalar, "p": g.tensor, "g": g, "y": g.sync}
     QS = {"v": "qv", "s": "qs", "p": "qp", "g": "qg"}
     cnt, known, lastw, readers, lastx = {}, {q: {} for q in Q}, {}, {}, {}
@@ -189,9 +191,11 @@ def rank_program(g, core, T, topo):
         clock[sem] = cnt[sem]
         note(q, rd, wr, (), (q, sem, cnt[sem], clock))
 
+    banks = [k for k, v in SCRATCH.items() if v[0] == "psum"]
+
     def split(xs):
         ks = [x[0] for x in xs if isinstance(x, tuple)]
-        return [k for k in ks if k[0] != "P" or k == "PI"], [k for k in ks if k[0] == "P" and k != "PI"]
+        return [k for k in ks if k not in banks], [k for k in ks if k in banks]
 
     def raw(x):
         return x[1] if isinstance(x, tuple) else x
@@ -201,10 +205,10 @@ def rank_program(g, core, T, topo):
         w, wp = split([out])
         return op(q, fn, r, w, rp + wp)
 
-    def ts(out, a, s1, o1, s2=None, o2=None):
+    def ts(out, a, s1, o1, s2=None, o2=None, more=()):
         if o2 is None:
-            return emit("v", lambda e: e.tensor_scalar(raw(out), raw(a), raw(s1), None, o1), [a, s1], out)
-        return emit("v", lambda e: e.tensor_scalar(raw(out), raw(a), raw(s1), raw(s2), o1, o2), [a, s1, s2], out)
+            return emit("v", lambda e: e.tensor_scalar(raw(out), raw(a), raw(s1), None, o1), [a, s1] + list(more), out)
+        return emit("v", lambda e: e.tensor_scalar(raw(out), raw(a), raw(s1), raw(s2), o1, o2), [a, s1, s2] + list(more), out)
 
     def tt(out, a, b, o, more=()):
         return emit("v", lambda e: e.tensor_tensor(raw(out), raw(a), raw(b), o), [a, b] + list(more), out)
@@ -213,23 +217,17 @@ def rank_program(g, core, T, topo):
         return emit("v", lambda e: e.tensor_copy(raw(out), raw(a)), [a] + list(more), out)
 
     def act(out, a, f=COPY, scale=1.0, more=(), bias=0.0):
-        return emit("s", lambda e: e.activation(raw(out), raw(a), f, bias=raw(bias), scale=scale), [a, bias] + list(more), out)
+        return emit("s", lambda e: e.activation(raw(out), raw(a), f, bias=raw(bias), scale=raw(scale)), [a, bias, scale] + list(more), out)
 
-    def mm(out, l, r, start, stop):
-        return emit("p", lambda e: e.matmul(raw(out), raw(l), raw(r), start, stop), [l, r], out)
+    def mm(out, l, r, start, stop, more=()):
+        return emit("p", lambda e: e.matmul(raw(out), raw(l), raw(r), start, stop), [l, r] + list(more), out)
 
-    def C(name, a, b=None, st=None):
-        return (name, T[name][:, a:b:st])
+    def C(name, a, b=None, st=None, key=None):
+        return (key or name, T[name][:, a:b:st])
 
     def X(name):
         return (name, T[name][:])
 
-    dma("y", "ldO", [(T.OI[:], T.opts[:])], wr=["OI"])
-    dma("y", "ldR", [(T.RI[:], T.rw[:])], wr=["RI"])
-    dma("y", "ldL", [(T.LI[:], T.lw[:])], wr=["LI"])
-    op("g", lambda e: e.iota(T.PI[:], [[0, 1]], 0, 1), wr=["PI"])
-    op("g", lambda e: e.iota(T.j1[:], [[1, 32]], 0, 0), wr=["j1"])
-    op("g", lambda e: e.iota(T.CI[:], [[1, 176]], 0, 0, allow_small_or_imprecise_dtypes=True), wr=["CI"])
     npc, nfc, nls = [0], [0], [0]
 
     def icol(shop, val):
@@ -239,384 +237,496 @@ def rank_program(g, core, T, topo):
         ts(o, X("PI"), val, shop)
         return o
 
-    def newf():
+    def col(a, s1, o1, s2=None, o2=None):
         k = nfc[0]
         nfc[0] += 1
-        return ("fc%d" % k, T.fc[:, k:k + 1])
-
-    def fcol(a, s1, o1):
-        o = newf()
-        ts(o, a, s1, o1)
+        o = ("fc%d" % k, T.fc[:, k:k + 1])
+        ts(o, a, s1, o1, s2, o2)
         return o
 
-    hh = icol(A_.logical_shift_right, 4)
-    p3i = icol(A_.bitwise_and, 8)
-    p4i = icol(A_.bitwise_and, 16)
-    p15 = icol(A_.bitwise_and, 15)
-    p7 = icol(A_.bitwise_and, 7)
-    pg = icol(A_.bitwise_and, 96)
-    p120 = icol(A_.bitwise_and, 120)
-    ub = {1: icol(A_.bitwise_and, 1), 2: icol(A_.bitwise_and, 2), 4: icol(A_.bitwise_and, 4)}
-    H = fcol(hh, float(G1), A_.mult)
-    nH = fcol(hh, -float(G1), A_.mult)
-    n = X("OI")
-    ts(X("i1"), n, 1.0 / 192, A_.mult, -95.5 / 192, A_.add)
-    ts(X("i2"), n, 1.0 / 1536, A_.mult, -767.5 / 1536, A_.add)
-    ts(X("i3"), n, 1.0 / 64, A_.mult, -31.5 / 64, A_.add)
-    ts(X("f4"), n, 7680, A_.is_ge, EC - 2880.0, A_.mult)
-    ts(X("f1"), X("i1"), 2304, A_.mult)
-    ts(X("f2"), X("i2"), -22464, A_.mult)
-    ts(X("f3"), X("i3"), 128, A_.mult)
-    tt(X("f4"), X("f4"), n, A_.add)
-    tt(X("f1"), X("f1"), X("f2"), A_.add)
-    tt(X("f3"), X("f3"), X("f4"), A_.add)
-    for t in range(3):
-        b, w = t * B1, 64 * t
-        tt(C("SB0", b + 128, b + 192), C("f1", w, w + 64), C("f3", w, w + 64), A_.add)
-        cp(C("SB0", b, b + 64), C("RI", w, w + 64))
-        ts(C("SB0", b + 64, b + 128), C("LI", w, w + 64), -1.0, A_.mult)
+    def lin(*terms):
+        acc = float(terms[-1])
+        for c, w in terms[:-1]:
+            acc = col(c, float(w), A_.mult, acc, A_.add)
+        return acc
 
-    def send(e, name):
+    def hot(out, lo, tgt, shift=0.0):
+        n = raw(out).shape[1]
+        ts(out, C("CI", lo, lo + n), -float(shift), A_.add, tgt, A_.is_equal)
+
+    dma("y", "ldO", [(T.OI[:], T.opts[:])], wr=["OI"])
+    lds = [(T.WI[32 * a + 16 * b:32 * a + 16 * b + 16, 192 * f:192 * f + 192], (T.rw, T.lw)[b][32 * a + 16 * f:32 * a + 16 * f + 16, :])
+           for a in range(4) for b in range(2) for f in range(2)]
+    dma("s", "ldW", lds[:9], wr=["WIa"])
+    dma("y", "ldW", lds[9:], wr=["WI"])
+    op("g", lambda e: e.iota(T.PI[:], [[0, 1]], 0, 1), wr=["PI"])
+    op("g", lambda e: e.iota(T.CI[:], [[1, 176]], 0, 0, allow_small_or_imprecise_dtypes=True), wr=["CI"])
+    pa, pb, ph, p7 = icol(A_.bitwise_and, 96), icol(A_.bitwise_and, 16), icol(A_.bitwise_and, 8), icol(A_.bitwise_and, 7)
+    sgn = lin((pb, -0.125), 1)
+    tO = lin((p7, 1), (pa, 1), (ph, -2), 16)
+    tO0 = lin((pb, 64), 0)
+    tO1 = col(tO0, -1.0, A_.mult, 1024.0, A_.add)
+    for f, m in enumerate((tO0, tO1)):
+        tf = col(m, 1.0, A_.mult, tO, A_.add)
+        hot(C("EH", 128 * f, 128 * f + 128), 0, tf)
+        hot(C("EL", 128 * f, 128 * f + 128), 0, tf, 8)
+    for j, (M, w) in enumerate((("EH", 128.0), ("EH", -384.0), ("EH", 2304.0), ("EH", -8832.0), ("EL", -2.0))):
+        act(C("MS", 256 * j, 256 * j + 256, key="MS%d" % j), X(M), scale=w)
+    for f in range(2):
+        ts(C("SW0", f, None, 2), C("WI", 192 * f, 192 * f + 192), sgn, A_.mult)
+
+    def send(e, x):
+        name = "S%s%d" % (x, e)
         deps("g", [name], [], ())
-        offs = [(h, T["DA%d" % e][0:128, :]) for h in role if role[h]["feed"] == core]
-        offs += [(cores[r], T["NB%d" % e][:]) for r, q in extra if q == rank]
+        offs = [(h, T["D%s%d" % (x, e)][0:128, :]) for h in role if role[h]["feed"] == core]
+        offs += [(cores[r], T["N%s%d" % (x, e)][:]) for r, q in extra if q == rank]
         en = topo.engines(core, offs[0][0])
-        trs = [RemoteDMATransfer(dst_ids=[dst(topo, h) for h, _ in offs], dma_engine_mask=pl(en), remote_sem=T.sem["fA%d" % e],
+        trs = [RemoteDMATransfer(dst_ids=[dst(topo, h) for h, _ in offs], dma_engine_mask=pl(en), remote_sem=T.sem["fA%s%d" % (x, e)],
                                  srcs=[T[name][:]], dsts=[d for _, d in offs])]
         nls[0] += len(en)
         for q in near:
-            e2 = [x for x in topo.engines(core, cores[q]) if x not in en]
-            trs.append(RemoteDMATransfer(dst_ids=[dst(topo, cores[q])], dma_engine_mask=pl(e2), remote_sem=T.sem["fB%d" % e],
-                                         srcs=[T[name][:]], dsts=[T["NB%d" % e][:]]))
+            e2 = [y for y in topo.engines(core, cores[q]) if y not in en]
+            trs.append(RemoteDMATransfer(dst_ids=[dst(topo, cores[q])], dma_engine_mask=pl(e2), remote_sem=T.sem["fB%s%d" % (x, e)],
+                                         srcs=[T[name][:]], dsts=[T["N%s%d" % (x, e)][:]]))
             nls[0] += len(e2)
         g.remote_dma_fused(trs, local_sem=T.sem.ls)
 
-    def put(qu, e, sem, name, src, rd):
-        nn = PN[e]
+    def put(qu, e, x, sem, name, src, rd):
+        nn, W = PN[e], T["W" + x]
         c0 = src * R1 + (e - 1) * B1 * (e > 0)
-        pairs = [(T.W[:, c0:c0 + nn], T[name][:])]
-        for k in range(1, 8):
+        pairs = [(W[:, c0:c0 + nn], T[name][:])]
+        for k in range(1, 4):
             c = c0 + k * G1
-            pairs.append((T.W[0:128 - 16 * k, c:c + nn], T[name][16 * k:128, :]))
-            pairs.append((T.W[128 - 16 * k:128, c:c + nn], T[name][0:16 * k, :]))
-        dma(qu, sem + str(e), pairs, rd=rd, wr=[sem])
+            pairs.append((W[0:128 - 32 * k, c:c + nn], T[name][32 * k:128, :]))
+            pairs.append((W[128 - 32 * k:128, c:c + nn], T[name][0:32 * k, :]))
+        deps(qu, [], ["W" + x], ())
+        dma(qu, sem + x + str(e), pairs, rd=rd, wr=[sem + x])
 
-    def spread(e, name):
-        deps("s", [], ["W"], ())
-        deps("y", [], ["W"], ())
-        put("s", e, "own", name, rank, [name])
+    def put_own(qu, e, x):
+        put(qu, e, x, "own", "S%s%d" % (x, e), rank, ["S%s%d" % (x, e)])
+
+    def put_nb(qu, e, x):
         for q in near + [q for r, q in extra if r == rank]:
             h = [h for h in role if role[h]["feed"] == cores[q]][0]
             en = topo.engines(cores[q], core)
-            Q["y"].wait_ge(T.sem["f%s%d" % ("B" if q in near else "A", e)],
-                           len([x for x in en if x not in topo.engines(cores[q], h)] if q in near else en))
-            put("y", e, "nbd", "NB%d" % e, q, [])
+            Q[qu].wait_ge(T.sem["f%s%s%d" % ("B" if q in near else "A", x, e)],
+                          len([y for y in en if y not in topo.engines(cores[q], h)] if q in near else en))
+            put(qu, e, x, "nbd", "N%s%d" % (x, e), q, [])
 
-    send(0, "SB0")
-    spread(0, "SB0")
-    op("g", lambda e: e.iota(T.RS[:], [[0, 1024]], 0, 0, allow_small_or_imprecise_dtypes=True), wr=["RS"])
-    op("g", lambda e: e.affine_select(T.RS[:], T.RS[:], [[0, 128], [1, 8]], A_.not_equal, -2.0 ** 25, 0, 0), rd=["RS"], wr=["RS"])
-    nH64 = fcol(nH, 64.0, A_.add)
-    nH128 = fcol(nH, 128.0, A_.add)
-    p15f = fcol(p15, 1.0, A_.mult)
-    p3f = fcol(p3i, 1.0, A_.mult)
-    pf = fcol(X("PI"), 1.0, A_.mult)
-    j5 = X("j5")
-    ts(j5, C("j1", 0, 8), 16, A_.mult, p15f, A_.add)
-    ts(X("j6"), j5, 5, A_.logical_shift_right)
-    ts(X("j7"), j5, 24, A_.bitwise_and)
-    ts(X("j8"), j5, 7, A_.bitwise_and)
-    ts(X("j6"), X("j6"), 192, A_.mult, 128, A_.add)
-    ts(X("j7"), X("j7"), 2, A_.mult)
-    tt(X("j8"), X("j8"), X("j6"), A_.add)
-    tt(X("j8"), X("j8"), X("j7"), A_.add)
-    cp(C("CDL", 0, 6), C("j8", 0, 6))
-    ts(C("CDL", 6, 12), C("j8", 0, 6), 8, A_.add)
-    act(X("CD"), ("SB0", T.SB0[:].indirect(T.CDL[:])), more=[("CDL", 0)])
-    ts(X("j2"), X("j1"), 24, A_.bitwise_and)
-    ts(X("j3"), X("j1"), 7, A_.bitwise_and)
-    ts(X("j2"), X("j2"), 2, A_.mult, p3f, A_.add)
-    tt(X("j2"), X("j2"), X("j3"), A_.add)
-    cp(X("XBL"), X("j2"))
-    temp = fcol(p15, 1024.0, A_.mult)
-    ntemp = fcol(temp, -1.0, A_.mult)
+    send(0, "W")
+    put_own("y", 0, "W")
+    n = X("OI")
+    fls = [C("fl", 192 * j, 192 * j + 192, key="fl%d" % j) for j in range(5)]
+    for j, d in enumerate((64, 192, 384, 1536)):
+        ts(fls[j], n, 1.0 / d, A_.mult, 129 - (d - 1) / 2.0 / d, A_.add)
+    ts(X("ni"), n, 63, A_.bitwise_and)
+    ts(fls[4], X("ni"), -1.0, A_.mult)
+    bO = lin((ph, (129 - 875136) / 8), 875136)
+    terms = [("MS", 0, 0), ("MS", 1, 1), ("EL", 0, 1), ("MS", 2, 2), ("MS", 4, 2), ("MS", 3, 3), ("MS", 4, 4)]
+    for i, (M, j, r) in enumerate(terms):
+        for f in range(2):
+            mm(C("PX%d" % f, 0, 192), C(M, 256 * j + 128 * f, 256 * j + 128 * f + 128, key="MS%d" % j if M == "MS" else M), fls[r],
+               i == 0, i == len(terms) - 1)
+    act(C("SO0", 0, None, 2, key="SO0a"), C("PX0", 0, 192), IDENT, bias=bO)
+    ts(C("SO0", 1, None, 2), C("PX1", 0, 192), bO, A_.add, more=[("SO0a", 0)])
+    send(0, "O")
+    put_own("s", 0, "O")
+    put_nb("y", 0, "W")
+    put_nb("y", 0, "O")
+    def fill(out, val):
+        emit("g", lambda e: e.iota(raw(out), [[0, raw(out).shape[1]]], val, 0, allow_small_or_imprecise_dtypes=True), [], out)
 
-    def own_walls(t):
-        b = t * B1
-        act(C("XR", 512 * t, 512 * t + 512), ("SB0", T.SB0[:, b:b + 64].indirect(T.XBL[:])), more=[("XBL", 0)])
-        act(C("XN", 512 * t, 512 * t + 512), ("SB0", T.SB0[:, b + 64:b + 128].indirect(T.XBL[:])), more=[("XBL", 0)])
-        act(C("XW", 128 * t, 128 * t + 64), C("SB0", b + 64, b + 128), IDENT, scale=-1.0, bias=temp)
-        act(C("XW", 128 * t + 64, 128 * t + 128), C("SB0", b, b + 64), IDENT, scale=-1.0, bias=temp)
+    def pick(out, src, levels, row0, val):
+        emit("g", lambda e: e.affine_select(raw(out), raw(src), [[-s, c] for s, c in levels], A_.not_equal, val, -row0, 1), [src], out)
 
-    def sel2(base, col, big, full):
-        x, y0, y1, y2 = newf(), newf(), newf(), newf()
-        ts(x, col, big, A_.mult)
-        tt(y0, base, x, A_.add)
-        tt(y1, base, x, A_.subtract)
-        ts(y2, y1, full, A_.add)
-        return y0, y2
+    def band(out, src, levels, row0, rows):
+        emit("g", lambda e: e.affine_select(raw(out), raw(src), [[-s, c] for s, c in levels], A_.is_ge, 0.0, -row0, 1), [src], out)
+        emit("g", lambda e: e.affine_select(raw(out), raw(out), [[s, c] for s, c in levels], A_.is_ge, 0.0, row0 + rows - 1, -1), [out], out)
 
-    A3 = sel2(pf, p3i, 125.0, 1000.0)
-    for a in range(2):
-        for b in range(2):
-            o = 128 * (2 * a + b)
-            ts(C("QF", o, o + 128), C("CI", 0, 128), -8.0 * (b - a), A_.add, A3[a], A_.is_equal)
-    act(X("QB"), X("QF"))
-    gb = fcol(p3i, 2.0, A_.mult)
-    gc, gd = newf(), newf()
-    tt(gc, gb, pg, A_.add)
-    tt(gd, gc, p7, A_.add)
-    A4 = sel2(gd, p4i, 100.0, 1600.0)
-    for b in range(2):
-        for a in range(2):
-            o = 128 * (2 * b + a)
-            ts(C("GF", o, o + 128), C("CI", 0, 128), -8.0 * a, A_.add, A4[b], A_.is_equal)
-    for bank, M in (("PP2", "QF"), ("PG2", "GF")):
-        for x in range(2):
-            for a in range(2):
-                o = 128 * (2 * x + a)
-                mm(C(bank, 96 * x, 96 * x + 96), C(M, o, o + 128), C("CD", 96 * a, 96 * a + 96), a == 0, a == 1)
-    op("v", lambda e: e.memset(T.W[:, WC:WC + 128], -BIG), wr=["Wemp"])
-    op("v", lambda e: e.memset(T.W[:, WC + 128:WC + 192], float(EC)), wr=["Wemp"])
-    ts(X("f1"), C("PP2", 0, 192), H, A_.is_lt, float(WC), A_.mult)
-    tt(X("f2"), X("f1"), C("PP2", 0, 192), A_.add)
-    ts(X("f3"), C("PG2", 0, 192), H, A_.is_lt, float(WC), A_.mult)
-    tt(X("f4"), X("f3"), C("PG2", 0, 192), A_.add)
+    act(X("SG"), C("CI", 0, 160), IDENT, scale=0.0, bias=sgn)
+    fill(X("ON"), 1)
+    fill(X("ZB"), 0)
+    band(X("EMS"), X("ON"), [(32, 6), (-16, 2), (1000, 16)], -16, 16)
+    pick(X("ID"), C("ZB", 0, 128), [(1, 128)], 0, 1.0)
+    op("g", lambda e: e.iota(T.jx[:], [[4, 32]], 0, 0), wr=["jx"])
+    op("g", lambda e: e.iota(T.js[:], [[8, 2], [16, 2], [512, 2]], 0, 0), wr=["js"])
+    for y in range(2):
+        pick(C("KM", 160 * y, 160 * y + 160, key="KM%d" % y), C("ZB", 0, 160), [(32, 5), (8, 8), (1, 4)], 4 * y - 32, 1.0)
+    for y in range(2):
+        pick(C("KZ", 160 * y, 160 * y + 160, key="KZ%d" % y), C("ZB", 0, 160), [(32, 5), (-1000, 2), (1, 16)], 1000 + 16 * y, 1.0)
+    pick(X("SWB"), C("ZB", 0, 128), [(32, 4), (-16, 2), (1, 16)], 16, 1.0)
+    band(X("EWP"), X("SG"), [(32, 5), (1000, 32)], -32, 32)
+    band(X("LT"), C("ON", 0, 128), [(8, 16), (0, 8)], 0, 8)
+    emit("g", lambda e: e.affine_select(T.LT[:], T.LT[:], [[1, 128]], A_.is_gt, 0.0, 0, -1), [X("LT")], X("LT"))
+    pick(X("LT"), X("LT"), [(1, 128)], 0, -0.5)
+    for y in range(2):
+        pick(C("DM", 128 * y, 128 * y + 128, key="DM%d" % y), C("ZB", 0, 128), [(16, 8), (0, 2), (1, 8)], 8 * y, 1.0)
+    band(X("CM"), C("ON", 0, 144), [(16, 9), (1000, 8), (8, 2)], -16, 8)
+    fill(X("SLM"), -131072)
+    band(X("SLM"), X("SLM"), [(32, 4), (-16, 2), (0, 16)], 16, 8)
+    fill(X("RS"), 0)
+    op("g", lambda e: e.affine_select(T.RS[:], T.RS[:], [[0, 48], [1, 8]], A_.not_equal, -2.0 ** 25, 0, 0), rd=["RS"], wr=["RS"])
+    p15, p12 = icol(A_.bitwise_and, 15), icol(A_.bitwise_and, 12)
+    ub = [icol(A_.bitwise_and, 1), icol(A_.bitwise_and, 2), icol(A_.bitwise_and, 4)]
+    pf = col(X("PI"), 1.0, A_.mult)
+    H = lin((pa, G1 / 32), 0)
+    nH = lin((pa, -G1 / 32), 0)
+    nsg = lin((pb, 0.125), -1)
+    lo8 = lin((ph, -4096), 0)
+    Hh = col(H, 1.0, A_.mult, lo8, A_.add)
+    ECw = col(H, 1.0, A_.is_ge, float(WC), A_.mult)
+    ECw = col(ECw, float(EC), A_.add)
+    ts(X("OZ"), X("SO0"), Hh, A_.is_lt, float(WC), A_.mult)
+    tt(X("OW"), X("OZ"), X("SO0"), A_.add)
+    base = lin((pa, 1), (pb, -1), 16)
+    tL = col(p7, 1.0, A_.mult, base, A_.add)
+    hot(X("PLM"), 0, tL, 8)
+    F = {1: lin((ub[0], 1), 0), 2: lin((ub[1], 0.5), 0), 4: lin((ub[2], 0.25), 0)}
+    for m, x, y in ((3, 1, 2), (5, 1, 4), (6, 2, 4), (7, 3, 4)):
+        F[m] = col(F[x], F[y], A_.not_equal)
+    sets = []
+    for k1, k2 in KS:
+        phi = [m for m in range(1, 8) if par(m & k1) and par(m & k2)][0]
+        one = [s for s in range(8) if par(s & phi)]
+        ps1, ps2 = [(x, y) for x in (1, 2, 4) for y in (1, 2, 4) if len(set(par(s & x) + 2 * par(s & y) for s in one)) == 4][0]
+        one.sort(key=lambda s: par(s & ps1) + 2 * par(s & ps2))
+        sets.append((phi, ps1, ps2, one))
 
     def lists(t):
-        for side in range(2):
-            i, o = 96 * side + 32 * t, 64 * t + 32 * side
-            ts(C("LU", o, o + 32), C("f2", i, i + 32), nH64 if side else nH, A_.add, float(WC + 64 * side), A_.min)
-        for b in range(2):
-            ts(C("LO", 64 * t + b, 64 * t + 64, 2), C("f4", 96 * b + 32 * t, 96 * b + 32 * t + 32), nH128, A_.add, float(WC + 128), A_.min)
-
-    def empties(t):
-        for side in range(2):
-            i, o = 96 * side + 32 * t, 64 * t + 32 * side
-            ts(C("NO", o, o + 32), C("f2", i, i + 32), EC - 32.0, A_.is_ge)
+        c0 = 128 * t
+        for y in range(2):
+            mm(C("PCN", 0, 64), C("PLM", 8 - 8 * y, 136 - 8 * y), C("OW", c0 + y, c0 + 128, 2), y == 0, y == 1)
+        phi, ps1, ps2, one = sets[t]
+        for j, k in enumerate((0,) + KS[t]):
+            s1, s2, s3 = (-1 if j == 0 else 1), 1 - 2 * par(ps1 & k), 1 - 2 * par(ps2 & k)
+            tg = col(F[phi], 1000.0 * s1, A_.mult, base, A_.add)
+            tg = col(F[ps1], float(s2), A_.mult, tg, A_.add)
+            tg = col(F[ps2], 2.0 * s3, A_.mult, tg, A_.add)
+            hot(C("ED", 140 * j, 140 * j + 140, key="ED%d" % j), 0, tg, 12 + 1000 * (j == 0) + par(ps1 & k) + 2 * par(ps2 & k))
+            for y in range(4):
+                o = 140 * j + 12 - 4 * y
+                mm(C("PDM", 32 * j, 32 * j + 32), C("ED", o, o + 128, key="ED%d" % j), C("OW", c0 + y, c0 + 128, 4), y == 0, y == 3)
+        ts(C("LU", 64 * t, 64 * t + 64), C("PCN", 0, 64), nH, A_.add)
+        ts(C("NE", 64 * t, 64 * t + 64), C("PCN", 0, 64), ECw, A_.is_equal)
+        ts(C("LD", 96 * t, 96 * t + 96), C("PDM", 0, 96), nH, A_.add)
 
     lists(0)
-    h16 = fcol(hh, 16.0, A_.mult)
-    ts(X("REL"), X("CI"), h16, A_.subtract)
-    ts(X("EM"), X("REL"), 24.0, A_.is_equal)
-    act(X("BM"), X("EM"), scale=-2.0 ** 30)
+    op("v", lambda e: e.memset(T.WW[:, EC::G1], -BIG), wr=["WWe"])
+    eo = lin((ph, -EC / 8), EC)
+    ts(("WOe", T.WO[:, EC::G1]), C("CI", 0, 4), 0.0, A_.mult, eo, A_.add)
+    act(X("EMB"), X("EMS"), scale=-2.0 ** 30)
+    made = set()
 
-    def diffs(ds, hbs):
-        for d in ds:
-            tt(C("AD", 160 * d, 160 * d + 160), C("EM", 8, 168), C("EM", 8 - d, 168 - d), A_.subtract)
-        for hb in hbs:
-            u = fcol(ub[hb], 0.5 / hb, A_.mult)
-            ts(C("UPC", 64 * (hb // 2), 64 * (hb // 2) + 64), C("CI", 0, 64), 0.0, A_.mult, u, A_.add)
+    def diffs(t):
+        for k in KS[t]:
+            for d in sorted(set((s ^ k) - s for s in range(8)) - made):
+                made.add(d)
+                tt(C("AD", 144 * (d + 7), 144 * (d + 8), key="AD%d" % d), C("EMS", 16, 160), C("EMB", 16 - d, 160 - d), A_.add)
+            hb = 2 if k >= 4 else 1 if k >= 2 else 0
+            if "u%d" % hb not in made:
+                made.add("u%d" % hb)
+                u = lin((F[1 << hb], 0.5), 0)
+                ts(C("UPC", 64 * hb, 64 * hb + 64, key="UPC%d" % hb), C("CI", 0, 64), 0.0, A_.mult, u, A_.add)
 
-    ts(X("ID"), C("CI", 0, 128), pf, A_.is_equal)
-    diffs((1, 4), (1, 4))
-    ts(X("j6"), j5, 31, A_.bitwise_and)
-    ts(X("j7"), j5, 5, A_.logical_shift_right)
-    ts(X("j6"), X("j6"), 32, A_.mult, 8, A_.add)
-    ts(X("j7"), X("j7"), 8, A_.mult)
-    tt(X("j6"), X("j6"), X("j7"), A_.add)
+    diffs(0)
+    y1 = lin((pb, 0.0625), 0)
+    q32 = lin((p15, 32), 0)
+    v2 = col(p15, 2.0, A_.mult, y1, A_.add)
 
     def sels(t):
-        ts(X("j4"), j5, t, A_.add)
-        ts(X("j4"), X("j4"), 7, A_.bitwise_and)
-        tt(X("j4"), X("j4"), X("j6"), A_.add)
-        cp(C("SEL", 4 * t, 4 * t + 4), C("j4", 0, 4))
+        k = npc[0]
+        npc[0] += 2
+        i1, i2 = ("pc%d" % k, T.pc[:, k:k + 1]), ("pc%d" % (k + 1), T.pc[:, k + 1:k + 2])
+        ts(i1, v2, float(t), A_.add)
+        ts(i2, i1, 7, A_.bitwise_and)
+        ts(C("SEL", 8 * t, 8 * t + 8), X("js"), col(i2, 1.0, A_.mult, q32, A_.add), A_.add)
 
     sels(0)
+    ts(X("XBL"), X("jx"), lin((p12, 0.25), 0), A_.add)
+    dL = lin((pb, -1 / 32), 0)
+    dR = lin((pb, 1 / 16), -0.5)
+
+    def own_walls(t):
+        act(X("XL"), ("SW0", T.SW0[:, 128 * t:128 * t + 128].indirect(T.XBL[:])), IDENT, bias=dL, more=[("XBL", 0)])
+        act(X("PX0"), X("XL"))
+        act(X("PX1"), X("XL"), IDENT, bias=dR)
+
     own_walls(0)
-    act(X("PP2"), C("XN", 0, 512))
-    for j, f in enumerate((1.0, -7488.0, 1344.0, -128.0)):
-        act(C("IDF", 128 * j, 128 * j + 128), X("ID"), scale=f)
-    empties(0)
-    p8f = fcol(p120, 1.0, A_.mult)
-    ts(X("tmp"), X("CI"), p8f, A_.subtract)
-    ts(X("C1"), C("tmp", 0, 144), 8.0, A_.is_equal)
-    ts(C("tmp2", 0, 128), C("tmp", 0, 128), 8.0, A_.is_lt)
-    ts(C("tmp", 0, 128), C("CI", 0, 128), pf, A_.is_gt)
-    tt(C("tmp2", 0, 128), C("tmp2", 0, 128), C("tmp", 0, 128), A_.mult)
-    ts(C("tmp", 0, 128), C("CI", 0, 128), pf, A_.is_equal, -0.5, A_.mult)
-    tt(X("LT"), C("tmp2", 0, 128), C("tmp", 0, 128), A_.add)
-    EH = fcol(nH, EC + 128.0, A_.add)
-    s64 = fcol(p3i, 8.0, A_.mult)
-    capN = fcol(s64, float(WC), A_.add)
-    nHs = newf()
-    tt(nHs, s64, nH, A_.add)
-    big1 = fcol(p3i, -BIG / 8, A_.mult)
-    big0 = newf()
-    ts(big0, big1, -1.0, A_.mult, -BIG, A_.add)
-    ts(C("tmp", 0, 128), C("REL", 0, 128), 0.0, A_.is_ge)
-    ts(C("tmp2", 0, 128), C("REL", 0, 128), 16.0, A_.is_lt)
-    tt(C("tmp", 0, 128), C("tmp", 0, 128), C("tmp2", 0, 128), A_.mult)
-    ts(C("SL", 0, 128), C("tmp", 0, 128), big0, A_.mult)
-    ts(C("SL", 128, 256), C("tmp", 0, 128), big1, A_.mult)
-    op("v", lambda e: e.memset(T.ZB[:], 0.0), wr=["ZB"])
+    nEC = col(ECw, -1.0, A_.mult)
+    EHc = col(ECw, 1.0, A_.mult, nH, A_.add)
+    temp = lin((p15, 1024), 0)
+    act(X("TMPT"), C("CI", 0, 128), IDENT, scale=0.0, bias=temp)
+    hc = col(sgn, -0.25, A_.mult, lin((p15, -512), 0), A_.add)
+    lists(1)
+    sels(1)
+    diffs(1)
+    act(X("EWN"), X("EWP"), scale=-1.0)
+    act(X("NSW"), X("SWB"), scale=-1.0)
+    act(X("KZF"), ("KZ0", T.KZ[:]), more=[("KZ1", 0)])
+    later = {}
 
-    def win(L, lo, hi):
-        return ("W", T.W[:].indirect(T[L][:, lo:hi]))
+    def out_setup():
+        tN = lin((pa, 1), (pb, -0.5), (p7, 1), 8)
+        hot(C("tmp", 0, 144), 0, tN, 16)
+        for j, (wh, wl) in enumerate(((0.5, 192), (1344, -384), (-8832, 1))):
+            ts(C("NM", 144 * j, 144 * j + 144), C("tmp", 0, 144), lin((ph, (wl - wh) / 8), wh), A_.mult)
+        later["sA"] = lin((ph, (0.5 - 1 / 384) / 8), 1 / 384)
+        later["bA"] = lin((ph, (1 / 3 - 0.25) / 8), 129 - 1 / 3)
+        later["sB"] = lin((ph, (0.5 - 1 / 2304) / 8), 1 / 2304)
+        later["bB"] = lin((ph, (8.5 / 18 - 0.25) / 8), 129 - 8.5 / 18)
+        later["nt"] = lin((p15, -1024), 0)
+        later["hf"] = lin((p15, 512), -0.25)
 
-    def wm(L):
-        return [(L, 0), ("own", 0), ("nbd", 0), ("Wemp", 0)]
+    def win(x, L, lo, hi):
+        return ("W" + x, T["W" + x][:].indirect(T[L][:, lo:hi]))
+
+    def wm(x, L):
+        return [(L, 0), ("own" + x, 0), ("nbd" + x, 0), ("W%se" % x, 0)]
+
+    def arrived(x, t):
+        for q in "vs":
+            Q[q].wait_ge(T.sem["arr%s%d" % (x, t)], arr_n)
+
+    def gather_slots(t):
+        arrived("O", t)
+        cp(C("T0", 0, 512, key="T0a"), win("O", "LU", 64 * t, 64 * t + 32), more=wm("O", "LU"))
+        act(C("T0", 512, 1024, key="T0b"), win("O", "LU", 64 * t + 32, 64 * t + 64), more=wm("O", "LU"))
+
+    def replies(t):
+        for h, c in (("a", slice(0, 512)), ("b", slice(512, 1024))):
+            emit("v", lambda e, c=c: e.transpose(T.T1[:, c], T.T0[:, c]), [("T0" + h, 0)], ("T1" + h, 0))
+        cp(X("PK"), ("T1a", T.T1[:].indirect(T.SEL[:, 8 * t:8 * t + 8])), more=[("SEL", 0), ("T1b", 0)])
+        ts(X("pz"), C("PK", 0, 64), H, A_.is_lt, float(WC), A_.mult)
+        tt(X("PW"), X("pz"), C("PK", 0, 64), A_.add)
+        for s2 in range(2):
+            o, l = C("PPF", 64 * s2, 64 * s2 + 64), C("KM", 160 * s2 + 16, 160 * s2 + 144, key="KM%d" % s2)
+            mm(o, l, C("PK", 64, 128), True, False)
+            mm(o, l, X("PW"), False, True)
+        for hl in range(2):
+            for y in range(2):
+                for b in range(2):
+                    o = 160 * y + 16 - 16 * b
+                    mm(C("PCH", 64 * hl + y, 64 * hl + 64, 2), C("KZ", o, o + 128, key="KZ%d" % y),
+                       C("PK", 96 - 32 * b, 128 - 32 * b) if hl else C("PW", 32 - 32 * b, 64 - 32 * b), b == 0, b == 1)
+        ts(X("LK"), C("PPF", 0, 128), nH, A_.add)
+
+    def reply_parts():
+        act(X("KH"), C("PCH", 0, 64), IDENT, bias=nEC)
+        act(X("KL"), C("PCH", 64, 128))
+
+    def gather_one(t):
+        act(X("U1"), win("W", "LD", 96 * t, 96 * t + 32), more=wm("W", "LD"))
+
+    def diff(t, z):
+        tt(X("D%d" % z), win("W", "LD", 96 * t + 32 * z, 96 * t + 32 * z + 32), X("U1"), A_.subtract, more=wm("W", "LD"))
+
+    def signs(z, q):
+        for name, sc in (("IA%d" % z, 1.0), ("IB%d" % z, -1.0)):
+            if q == "v":
+                ts(X(name), X("D%d" % z), sc, A_.mult, 0.0, A_.max)
+            else:
+                act(X(name), X("D%d" % z), RELU, scale=sc)
+
+    def count_del(t, z, x):
+        k = KS[t][z - 1]
+        hb = 2 if k >= 4 else 1 if k >= 2 else 0
+        o = C("PZ%d" % z, 0, 64)
+        if x == 0:
+            mm(o, X("ID"), C("UPC", 64 * hb, 64 * hb + 64, key="UPC%d" % hb), True, False)
+        for y in range(2):
+            for i, s in enumerate(sets[t][3]):
+                a, b = (s ^ k, s) if x else (s, s ^ k)
+                w = 144 * (b - a + 7) + 16 - 8 * y - a
+                mm(o, C("AD", w, w + 128, key="AD%d" % (b - a)), C(("IA%d", "IB%d")[x] % z, 4 * y + i, None, 8), False, x == 1 and y == 1 and i == 3)
+
+    def fetch(j):
+        act(C("TL", 512 * j - 512, 512 * j, key="TL%d" % j), win("W", "LK", 32 * j, 32 * j + 32), more=wm("W", "LK"))
+
+    def compare(j):
+        o = C("VI", 512 * j, 512 * j + 512, key="VI%d" % j)
+        if j == 0:
+            tt(o, win("W", "LK", 0, 32), X("XL"), A_.is_gt, more=wm("W", "LK"))
+        else:
+            tt(o, C("TL", 512 * j - 512, 512 * j, key="TL%d" % j), X("PX%d" % (j & 1)), A_.is_gt)
+
+    def count_rep(j):
+        for y in range(2):
+            for s in range(4):
+                w = 32 - (16 * (1 - (j & 1)) + 8 * y + 4 * (j >> 1) + s)
+                mm(C("PCN", 0, 64), C(("EWP", "EWN")[j & 1], w, w + 128), C("VI", 512 * j + 4 * y + s, 512 * j + 512, 8, key="VI%d" % j),
+                   False, j == 3 and y == 1 and s == 3)
+
+    def flags(z):
+        act(X("m%d" % z), C("PZ%d" % z, 0, 64), RELU, bias=-0.25)
+
+    def Y(x, t):
+        return C("Y" + x, 64 * t, 64 * t + 64, key="Y%s%d" % (x, t))
+
+    def store(q, x, t):
+        lo = 0 if t == 1 else 64 * t
+        dma(q, "o%s%d" % (x, t), [(T["y" + x.lower()][:, lo:64 * t + 64], T["Y" + x][:, lo:64 * t + 64])], rd=["Y%s%d" % (x, t), "Y%s0" % x])
+
+    def numbers(t):
+        nw = X("SO%d" % (t + 1))
+        act(X("nA"), nw, IDENT, scale=later["sA"], bias=later["bA"])
+        act(X("nB"), nw, IDENT, scale=later["sB"], bias=later["bB"])
+        for j, r in enumerate(("SO%d" % (t + 1), "nA", "nB")):
+            for f in range(2):
+                o = 144 * j + 16 - 16 * f
+                mm(C("PCN", 0, 64), C("NM", o, o + 128), C(r, f, None, 2), j + f == 0, j + f == 3)
+        act(Y("O", t), C("PCN", 0, 64), IDENT, bias=1015359.0)
+        if t:
+            store("y", "O", t)
+
+    def unpair(src, banks2):
+        for b in range(2):
+            for f in range(2):
+                o = 160 * b + 16 - 16 * f
+                mm(C(banks2[b], 256, 320), C("KZF", o, o + 128), C(src, f, None, 2), f == 0, f == 1)
 
     for t in range(3):
-        xb = 512 * t
-        for q in "vs":
-            Q[q].wait_ge(T.sem["arr%d" % t], arr_n)
-        cp(("Ua", T.U[:, 0:512]), win("LU", 64 * t, 64 * t + 32), more=wm("LU"))
-        act(("Ub", T.U[:, 512:1024]), win("LU", 64 * t + 32, 64 * t + 64), more=wm("LU"))
-        act(X("T0"), win("LO", 64 * t, 64 * t + 64), more=wm("LO"))
-        for z, k in enumerate((1 + t % 7, 1 + (t + 3) % 7)):
-            D, IA, IB, PZ = "D%d" % (z + 1), "IA%d" % (z + 1), "IB%d" % (z + 1), "PZ%d" % (z + 1)
-            hb = 4 if k >= 4 else 2 if k >= 2 else 1
-            m = 4 // hb
-            off, where = 0, {}
-            for r in range(2 * hb):
-                if r & hb:
-                    continue
-                tt((D, T[D][:, off:off + 128 * m]), ("Ua", T.U[:, r ^ k::2 * hb]), ("Ub", T.U[:, r::2 * hb]), A_.subtract)
-                for i in range(m):
-                    where[r + 2 * hb * i] = off + i
-                off += 128 * m
-            act(X(IA), X(D), RELU)
-            act(X(IB), X(D), RELU, scale=-1.0)
-            o = C(PZ, 0, 64)
-            mm(o, X("ID"), C("UPC", 64 * (hb // 2), 64 * (hb // 2) + 64), True, False)
-            todo = [(a, s, x) for x in (0, 1) for a in range(2) for s in sorted(where)]
-            for i, (a, s, x) in enumerate(todo):
-                qs, lo, d = 8 * a + s, where[s] + a * m, (s ^ k) - s
-                l = C("BM", 24 - qs, 152 - qs) if x else C("AD", 160 * d + 16 - qs, 160 * d + 144 - qs)
-                mm(o, l, C(IB if x else IA, lo, lo + 2 * m * 63 + 1, 2 * m), False, i == len(todo) - 1)
-        emit("v", lambda e: e.transpose(T.T1[:], T.T0[:]), [("T0", 0)], ("T1", 0))
-        cp(X("K"), ("T1", T.T1[:].indirect(T.SEL[:, 4 * t:4 * t + 4])), more=[("SEL", 0)])
-        ts(X("kz"), X("K"), H, A_.is_lt, float(WC), A_.mult)
-        tt(X("ky"), X("kz"), X("K"), A_.add)
-        ts(X("LKL"), X("ky"), nH64, A_.add, float(WC + 64), A_.min)
-        ts(X("LKR"), X("ky"), nH, A_.add, float(WC), A_.min)
-        for side in range(2):
-            act(("TL%d" % side, T.TL[:, 512 * side:512 * side + 512]), win("LKL", 32 * side, 32 * side + 32), more=wm("LKL"))
-            tt(C("VR", 512 * side, 512 * side + 512), win("LKR", 32 * side, 32 * side + 32), C("XR", xb, xb + 512), (A_.is_gt, A_.is_lt)[side], more=wm("LKR"))
-        o = C("PCN", 0, 64)
-        for i in range(16):
-            mm(o, C("EM", 24 - i, 152 - i), C("VR", i, None, 16), i == 0, False)
-        mm(C("PDM", 0, 128), X("ID"), X("ZB"), True, False)
-        for par in range(2):
-            for side in range(2):
-                c = slice(512 * side + par, 512 * side + 512, 2)
-                tt(("VL%d" % par, T.VL[:, c]), ("TL%d" % side, T.TL[:, c]), C("PP2", par, 512, 2), (A_.is_lt, A_.is_gt)[side])
+        oc = C("SO0", 128 * t, 128 * t + 128)
+        ne = C("NE", 64 * t, 64 * t + 64)
         if t == 0:
-            p34 = fcol(p3i, 4.0, A_.mult)
-            p347 = newf()
-            tt(p347, p34, p7, A_.add)
-            ts(C("j2", 0, 8), C("j1", 0, 8), 4, A_.bitwise_and)
-            ts(C("j3", 0, 8), C("j1", 0, 8), 3, A_.bitwise_and)
-            ts(C("j2", 0, 8), C("j2", 0, 8), 16, A_.mult, p347, A_.add)
-            ts(C("j3", 0, 8), C("j3", 0, 8), 8, A_.mult)
-            tt(C("j2", 0, 8), C("j2", 0, 8), C("j3", 0, 8), A_.add)
-            cp(X("DSL"), C("j2", 0, 8))
+            arrived("W", t)
+            gather_one(t)
+            diff(t, 1)
+            signs(1, "v")
+            count_del(t, 1, 0)
+            count_del(t, 1, 1)
+            diff(t, 2)
+            gather_slots(t)
+            signs(2, "s")
+            count_del(t, 2, 0)
+            replies(t)
+            count_del(t, 2, 1)
+            mm(C("PCN", 0, 64), X("SWB"), ne, True, False)
+            fetch(1)
+            compare(0)
+            count_rep(0)
+            flags(1)
+            flags(2)
+            fetch(2)
+            compare(1)
+            count_rep(1)
+            reply_parts()
+            fetch(3)
+            compare(2)
+            count_rep(2)
+        else:
+            arrived("W", t)
+            mm(C("PCN", 0, 64), X("SWB"), ne, True, False)
+            gather_one(t)
+            compare(0)
+            count_rep(0)
+            fetch(1)
+            diff(t, 1)
+            signs(1, "v")
+            count_del(t, 1, 0)
+            count_del(t, 1, 1)
+            fetch(2)
+            diff(t, 2)
+            signs(2, "s")
+            compare(1)
+            count_rep(1)
+            count_del(t, 2, 0)
+            fetch(3)
+            compare(2)
+            count_rep(2)
+            count_del(t, 2, 1)
+            flags(1)
+            flags(2)
+        compare(3)
         for z in (1, 2):
-            act(X("m%d" % z), C("PZ%d" % z, 0, 64), RELU, bias=-0.25)
+            mm(C("PCN", 0, 64), X("ID"), X("m%d" % z), False, False)
+        count_rep(3)
         o = C("PZ1", 64, 128)
-        mm(o, X("ID"), C("NO", 64 * t, 64 * t + 64), True, False)
+        mm(o, X("SWB"), ne, True, False)
         mm(o, X("ID"), X("m1"), False, False)
         mm(o, X("ID"), X("m2"), False, True)
-        act(X("kf"), X("ky"), IDENT, bias=-float(EC))
-        act(X("KH"), X("kf"))
         act(X("GX"), o, SIGN)
-        tt(X("KL"), X("kf"), X("KH"), A_.subtract)
-        o = C("PCN", 0, 64)
-        for i in list(range(0, 16, 2)) + list(range(1, 16, 2)):
-            mm(o, C("EM", 24 - i, 152 - i), ("VL%d" % (i % 2), T.VL[:, i::16]), False, False)
-        mm(o, X("ID"), X("GX"), False, True)
-        dm = [(C("PDM", 64 * side + 32 * a, 64 * side + 32 * a + 32), C("QB", 128 * (2 * a + side), 128 * (2 * a + side) + 128), 32 * side)
-              for side in range(2) for a in range(2)]
-        for oo, l, w in dm:
-            mm(oo, l, C("GX", w, w + 32), False, False)
-        ts(X("REV"), o, 0.0, A_.is_equal)
+        ts(X("REV"), C("PCN", 0, 64), -15.9, A_.is_lt)
         mm(C("PPF", 0, 64), X("LT"), X("REV"), True, True)
+        mm(C("PDM", 0, 128), X("ID"), C("ZB", 0, 128), True, False)
+        for y in range(2):
+            mm(C("PDM", y, 128, 2), C("DM", 128 * y, 128 * y + 128, key="DM%d" % y), X("GX"), False, False)
         ts(X("FI"), C("PPF", 0, 64), 0.0, A_.is_lt)
         tt(X("FH"), X("FI"), X("KH"), A_.mult)
         tt(X("FL"), X("FI"), X("KL"), A_.mult)
-        for j, (oo, l, w) in enumerate(dm):
-            mm(oo, l, C("FI", w, w + 32), False, j == 3)
-        o = C("PCH", 0, 8)
         for x in ("FH", "FL"):
             for c in range(8):
-                mm(o, C("C1", 8 - c, 136 - c), C(x, c, None, 8), x == "FH" and c == 0, x == "FL" and c == 7)
-        oc = C("SB0", t * B1 + 128, t * B1 + 192)
-        act(X("DP"), C("PDM", 0, 128))
-        act(X("DS"), ("DP", T.DP[:].indirect(T.DSL[:])), more=[("DSL", 0)])
-        tt(X("o1"), C("DS", 0, 64), C("DS", 64, 128), A_.add)
-        tt(X("o2"), X("o1"), oc, A_.mult)
-        ts(X("CLS"), o, EH, A_.add, float(WC + 128), A_.min)
-        sides = (("PPF", 0), ("PCH", 1))
-        for b, side in sides:
-            w = 128 * t + 64 * side
-            mm(C(b, 64, 128), C("IDF", 0, 128), C("XW", w, w + 64), True, False)
-        tt(X("o3"), oc, X("o2"), A_.subtract)
-        tt(X("EN"), win("CLS", 0, 8), X("DS"), A_.mult, more=wm("CLS"))
-        tt(X("n1"), C("EN", 0, 64), C("EN", 64, 128), A_.add)
-        sb = "SB%d" % (t + 1)
-        nw = C(sb, 128, 192)
-        tt(nw, X("n1"), X("o3"), A_.add)
-        ts(X("nz"), nw, H, A_.is_lt, float(WC), A_.mult)
-        tt(X("ny"), X("nz"), nw, A_.add)
-        ts(X("LN"), X("ny"), nHs, A_.add, capN, A_.min)
-        cp(("U2a", T.U2[:, 0:384]), win("LN", 0, 24), more=wm("LN"))
-        act(("U2b", T.U2[:, 384:1024]), win("LN", 24, 64), more=wm("LN"))
-        act(X("FG"), nw, IDENT, scale=-1.0, bias=float(EC))
-        for b, side in sides:
-            mm(C(b, 64, 128), C("SL", 128 * side, 128 * side + 128), X("FG"), False, True)
+                mm(C("PCH", 0, 8), C("CM", 16 - 2 * c, 144 - 2 * c), C(x, c, None, 8), x == "FH" and c == 0, x == "FL" and c == 7)
+        for y in range(2):
+            mm(C("PDM", y, 128, 2), C("DM", 128 * y, 128 * y + 128, key="DM%d" % y), X("FI"), False, y == 1)
+        mm(C("PZ2", 0, 128), X("ID"), X("TMPT"), True, False)
+        mm(C("PZ2", 0, 128), X("NSW"), C("SW0", 128 * t, 128 * t + 128), False, False)
+        ts(X("CLS"), C("PCH", 0, 8), EHc, A_.add)
+        tt(X("dd"), win("O", "CLS", 0, 8), oc, A_.subtract, more=wm("O", "CLS"))
+        tt(X("ee"), X("dd"), C("PDM", 0, 128), A_.mult)
+        so = "SO%d" % (t + 1)
+        tt(X(so), X("ee"), oc, A_.add)
+        ts(X("zN"), X(so), Hh, A_.is_lt, float(WC), A_.mult)
+        for j, r in enumerate((so, "zN")):
+            for y in range(2):
+                mm(C("PX1", 0, 64), C("PLM", 8 - 8 * y, 136 - 8 * y), C(r, y, None, 2), j + y == 0, j + y == 2)
+        act(X("FG"), X(so), ABS, bias=-float(EC))
+        mm(C("PZ2", 0, 128), X("SLM"), X("FG"), False, True)
+        ts(X("LN"), C("PX1", 0, 64), nH, A_.add)
+        if t < 2:
+            send(t + 1, "O")
+            put_own("y", t + 1, "O")
+            mm(C("PX0", 0, 128), X("ID"), X("TMPT"), True, False)
+        cp(C("U2", 0, 384, key="U2a"), win("W", "LN", 0, 24), more=wm("W", "LN"))
+        act(C("U2", 384, 704, key="U2b"), win("W", "LN", 24, 44), more=wm("W", "LN"))
+        act(C("U2", 704, 1024, key="U2c"), win("W", "LN", 44, 64), more=wm("W", "LN"))
         if t < 2:
             need("g", lastw["U2a"])
-            need("g", lastw["U2b"])
+            need("g", lastw["U2c"])
             g.remote_dma_fused([RemoteDMATransfer(dst_ids=[dst(topo, h)], dma_engine_mask=1 << topo.engines(core, h)[j],
                                                   remote_sem=T.sem["go%d" % (t + 1)]) for j, h in enumerate(mine)], local_sem=T.sem.ls)
             nls[0] += len(mine)
-
-        def numbers():
-            ts(X("y4"), nw, float(WC), A_.is_ge, 4736.0, A_.mult)
-            ys = [("yy%d" % j, T.yy[:, 64 * j:64 * j + 64]) for j in range(3)]
-            for j, d in enumerate((2880, 576, 192)):
-                act(ys[j], nw, IDENT, scale=1.0 / d, bias=-(d - 1) / 2.0 / d)
-            for big in (12582912.0, -12582912.0):
-                for y in ys:
-                    act(y, y, IDENT, bias=big)
-            o = C("PG2", 0, 64)
-            for j, r in enumerate([nw, X("y4")] + ys):
-                w = max(0, j - 1)
-                mm(o, C("IDF", 128 * w, 128 * w + 128), r, j == 0, j == 4)
-            act(X("YO"), o)
-            dma("y", "oO%d" % t, [(T.yo[:, 64 * t:64 * t + 64], T.YO[:])], rd=["YO"])
-
-        if t == 2:
-            numbers()
-        for hf, lo, hi in (("a", 0, 384), ("b", 384, 1024)):
-            emit("v", lambda e, c=slice(lo, hi): e.tensor_tensor_scan(T.SC[:, c], T.RS[:, c], T.U2[:, c], 0.0, A_.add, A_.max),
-                 [("RS", 0), ("U2" + hf, 0)], ("SC" + hf, 0))
-        for b, side in sides:
-            tt(C("ww", 64 * side, 64 * side + 64), C("SC", 7 + 8 * side, None, 16), C(b, 64, 128), A_.max, more=[("SCa", 0), ("SCb", 0)])
-        act(C("wn", 0, 64), C("ww", 64, 128), IDENT, scale=-1.0, bias=temp)
-        act(C("wn", 64, 128), C("ww", 0, 64), IDENT, scale=-1.0 if t < 2 else 1.0, bias=temp if t < 2 else ntemp)
-        tt(X("ws"), C("ww", 0, 64), C("ww", 64, 128), A_.subtract)
-        ts(C("wi", 0, 64), X("ws"), 0.5, A_.mult, -0.25, A_.add)
-        if t < 2:
-            ts(C("wi", 64, 128), X("ws"), -0.5, A_.mult, 0.25, A_.add)
-            tt(C(sb, 0, 128), X("wn"), X("wi"), A_.min)
-            send(t + 1, sb)
-            spread(t + 1, sb)
-            act(X("YL"), C(sb, 64, 128), scale=-1.0)
         else:
-            tt(C(sb, 0, 64), C("wn", 0, 64), C("wi", 0, 64), A_.min)
-            tt(X("YL"), C("wn", 64, 128), C("wi", 0, 64), A_.max)
-        dma("y", "oR%d" % t, [(T.yr[:, 64 * t:64 * t + 64], T[sb][:, 0:64])], rd=[sb])
-        dma("y", "oL%d" % t, [(T.yl[:, 64 * t:64 * t + 64], T.YL[:])], rd=["YL"])
+            numbers(t)
+        for hf, lo, hi in (("a", 0, 384), ("b", 384, 704), ("c", 704, 1024)):
+            emit("v", lambda e, c=slice(lo, hi), w=hi - lo: e.tensor_tensor_scan(T.SC[:, c], T.RS[:, 0:w], T.U2[:, c], 0.0, A_.add, A_.max),
+                 [("RS", 0), ("U2" + hf, 0)], ("SC" + hf, 0))
+        tt(X("ww"), C("SC", 7, None, 8, key="SCa"), C("PZ2", 0, 128), A_.max, more=[("SCb", 0), ("SCc", 0)])
         if t < 2:
-            lists(t + 1)
-            sels(t + 1)
+            sw = "SW%d" % (t + 1)
+            mm(C("PX0", 0, 128), X("NSW"), X("ww"), False, True)
+            tt(X("ws"), X("ww"), C("PX0", 0, 128), A_.add)
+            ts(X("wi"), X("ws"), 0.5, A_.mult, hc, A_.add)
+            tt(X(sw), X("wi"), C("PX0", 0, 128), A_.min)
+            send(t + 1, "W")
+            put_own("s", t + 1, "W")
+            put_nb("y", t + 1, "O")
+            put_nb("y", t + 1, "W")
             own_walls(t + 1)
-            act(X("PP2"), C("XN", 512 * t + 512, 512 * t + 1024))
-            empties(t + 1)
-            diffs(((2, 3, 5), (6,))[t], ((2,), ())[t])
-            numbers()
+            if t == 0:
+                lists(2)
+                sels(2)
+                diffs(2)
+            else:
+                out_setup()
+                numbers(0)
+                numbers(1)
+            unpair(sw, ("PZ1", "PZ2"))
+            act(Y("R", t), C("PZ1", 256, 320))
+            act(Y("L", t), C("PZ2", 256, 320), scale=-1.0)
+            gather_slots(t + 1)
+            replies(t + 1)
+            reply_parts()
+        else:
+            unpair("ww", ("PX0", "PX1"))
+            act(C("wn", 0, 64, key="wl"), C("PX0", 256, 320), IDENT, bias=later["nt"])
+            tt(C("ws", 0, 64), C("wn", 0, 64, key="wl"), C("PX1", 256, 320), A_.subtract)
+            act(C("wn", 64, 128, key="wr"), C("PX1", 256, 320), IDENT, scale=-1.0, bias=temp)
+            ts(C("wi", 0, 64), C("ws", 0, 64), 0.5, A_.mult, later["hf"], A_.add)
+            tt(Y("L", t), C("wn", 0, 64, key="wl"), C("wi", 0, 64), A_.max)
+            tt(Y("R", t), C("wn", 64, 128, key="wr"), C("wi", 0, 64), A_.min)
+        if t:
+            store("y", "L", t)
+            store("s" if t == 2 else "y", "R", t)
     g.wait_ge(T.sem.ls, nls[0])
     for sem, c in cnt.items():
         if known["g"].get(sem, 0) < c:

@@ -129,7 +129,7 @@ def rank_program(g, core, T, topo):
     arr_n = sum(len(topo.engines(h, core)) for h in mine)
     Q = {"v": g.vector, "s": g.scalar, "p": g.tensor, "g": g, "y": g.sync}
     QS = {"v": "qv", "s": "qs", "p": "qp", "g": "qg"}
-    cnt, known, lastw, readers, lastx = {}, {q: {} for q in Q}, {}, {}, {}
+    cnt, known, lastw, readers, lastx, alias = {}, {q: {} for q in Q}, {}, {}, {}, {}
 
     def need(q, tok):
         _, sem, c, clock = tok
@@ -142,7 +142,7 @@ def rank_program(g, core, T, topo):
 
     def deps(q, rd, wr, ps):
         toks = []
-        for k in rd:
+        for k in [k2 for k in rd for k2 in alias.get(k, [k])]:
             if k in lastw:
                 toks.append(lastw[k])
         for k in wr:
@@ -228,7 +228,10 @@ def rank_program(g, core, T, topo):
     def X(name):
         return (name, T[name][:])
 
-    npc, nfc, nls = [0], [0], [0]
+    npc, nfc, nls = [0], [16], [0]
+
+    def both(name):
+        alias[name] = [name + "a", name + "b"]
 
     def icol(shop, val):
         k = npc[0]
@@ -244,10 +247,17 @@ def rank_program(g, core, T, topo):
         ts(o, a, s1, o1, s2, o2)
         return o
 
-    def lin(*terms):
-        acc = float(terms[-1])
+    def scol(a, w, b, f=IDENT):
+        k = nfc[0]
+        nfc[0] += 1
+        o = ("fc%d" % k, T.fc[:, k:k + 1])
+        act(o, a, f, scale=w, bias=b)
+        return o
+
+    def lin(*terms, q="s"):
+        acc = terms[-1] if isinstance(terms[-1], tuple) and not isinstance(terms[-1][0], tuple) else float(terms[-1])
         for c, w in terms[:-1]:
-            acc = col(c, float(w), A_.mult, acc, A_.add)
+            acc = col(c, float(w), A_.mult, acc, A_.add) if q == "v" else scol(c, float(w), acc)
         return acc
 
     def hot(out, lo, tgt, shift=0.0):
@@ -261,19 +271,21 @@ def rank_program(g, core, T, topo):
     dma("y", "ldW", lds[9:], wr=["WI"])
     op("g", lambda e: e.iota(T.PI[:], [[0, 1]], 0, 1), wr=["PI"])
     op("g", lambda e: e.iota(T.CI[:], [[1, 176]], 0, 0, allow_small_or_imprecise_dtypes=True), wr=["CI"])
-    pa, pb, ph, p7 = icol(A_.bitwise_and, 96), icol(A_.bitwise_and, 16), icol(A_.bitwise_and, 8), icol(A_.bitwise_and, 7)
-    sgn = lin((pb, -0.125), 1)
-    tO = lin((p7, 1), (pa, 1), (ph, -2), 16)
-    tO0 = lin((pb, 64), 0)
-    tO1 = col(tO0, -1.0, A_.mult, 1024.0, A_.add)
-    for f, m in enumerate((tO0, tO1)):
-        tf = col(m, 1.0, A_.mult, tO, A_.add)
-        hot(C("EH", 128 * f, 128 * f + 128), 0, tf)
-        hot(C("EL", 128 * f, 128 * f + 128), 0, tf, 8)
-    for j, (M, w) in enumerate((("EH", 128.0), ("EH", -384.0), ("EH", 2304.0), ("EH", -8832.0), ("EL", -2.0))):
-        act(C("MS", 256 * j, 256 * j + 256, key="MS%d" % j), X(M), scale=w)
-    for f in range(2):
-        ts(C("SW0", f, None, 2), C("WI", 192 * f, 192 * f + 192), sgn, A_.mult)
+    masks = (103, 8, 16, 96, 7, 15, 12, 1, 2, 4)
+    p103, ph, pb = [icol(A_.bitwise_and, m) for m in masks[:3]]
+    tO = lin((p103, 1), 16, q="v")
+    sgn = lin((pb, -0.125), 1, q="v")
+    tO = lin((ph, -2), tO, q="v")
+    bO = lin((ph, (129 - 875136) / 8), 875136, q="v")
+    tf = [lin((pb, 64 - 128 * f), tO, q="v") for f in range(2)]
+    for M, o in (("EH", 0), ("EL", 8)):
+        for f in range(2):
+            hot(C(M, 128 * f, 128 * f + 128, key=M + str(f)), 0, tf[f], o + 1024 * f)
+    for j, (M, w) in enumerate((("EH", 128.0), ("EH", -384.0), ("EH", 2304.0), ("EL", -2.0), ("EH", -8832.0))):
+        act(C("MS", 256 * j, 256 * j + 256, key="MS%d" % j), (M + "0", T[M][:]), scale=w, more=[(M + "1", 0)])
+    ts(C("SW0", 0, None, 2, key="SW0a"), C("WI", 0, 192), sgn, A_.mult)
+    ts(C("SW0", 1, None, 2, key="SW0b"), C("WI", 192, 384), sgn, A_.mult)
+    both("SW0")
 
     def send(e, x):
         name = "S%s%d" % (x, e)
@@ -321,14 +333,18 @@ def rank_program(g, core, T, topo):
         ts(fls[j], n, 1.0 / d, A_.mult, 129 - (d - 1) / 2.0 / d, A_.add)
     ts(X("ni"), n, 63, A_.bitwise_and)
     ts(fls[4], X("ni"), -1.0, A_.mult)
-    bO = lin((ph, (129 - 875136) / 8), 875136)
-    terms = [("MS", 0, 0), ("MS", 1, 1), ("EL", 0, 1), ("MS", 2, 2), ("MS", 4, 2), ("MS", 3, 3), ("MS", 4, 4)]
+    for m in masks[3:]:
+        icol(A_.bitwise_and, m)
+    cp(C("fc", 0, len(masks), key="pf"), ("pc0", T.pc[:, 0:len(masks)]), more=[("pc%d" % k, 0) for k in range(len(masks))])
+    p103, ph, pb, pa, p7, p15, p12, u1, u2, u4 = [("pf", T.fc[:, k:k + 1]) for k in range(len(masks))]
+    terms = [("MS", 0, 0), ("EL", 0, 1), ("MS", 1, 1), ("MS", 2, 2), ("MS", 3, 2), ("MS", 4, 3), ("MS", 3, 4)]
     for i, (M, j, r) in enumerate(terms):
         for f in range(2):
-            mm(C("PX%d" % f, 0, 192), C(M, 256 * j + 128 * f, 256 * j + 128 * f + 128, key="MS%d" % j if M == "MS" else M), fls[r],
+            mm(C("PX%d" % f, 0, 192), C(M, 256 * j + 128 * f, 256 * j + 128 * f + 128, key="MS%d" % j if M == "MS" else M + str(f)), fls[r],
                i == 0, i == len(terms) - 1)
     act(C("SO0", 0, None, 2, key="SO0a"), C("PX0", 0, 192), IDENT, bias=bO)
-    ts(C("SO0", 1, None, 2), C("PX1", 0, 192), bO, A_.add, more=[("SO0a", 0)])
+    ts(C("SO0", 1, None, 2, key="SO0b"), C("PX1", 0, 192), bO, A_.add)
+    both("SO0")
     send(0, "O")
     put_own("s", 0, "O")
     put_nb("y", 0, "W")
@@ -366,24 +382,18 @@ def rank_program(g, core, T, topo):
     band(X("SLM"), X("SLM"), [(32, 4), (-16, 2), (0, 16)], 16, 8)
     fill(X("RS"), 0)
     op("g", lambda e: e.affine_select(T.RS[:], T.RS[:], [[0, 48], [1, 8]], A_.not_equal, -2.0 ** 25, 0, 0), rd=["RS"], wr=["RS"])
-    p15, p12 = icol(A_.bitwise_and, 15), icol(A_.bitwise_and, 12)
-    ub = [icol(A_.bitwise_and, 1), icol(A_.bitwise_and, 2), icol(A_.bitwise_and, 4)]
-    pf = col(X("PI"), 1.0, A_.mult)
-    H = lin((pa, G1 / 32), 0)
-    nH = lin((pa, -G1 / 32), 0)
-    nsg = lin((pb, 0.125), -1)
-    lo8 = lin((ph, -4096), 0)
-    Hh = col(H, 1.0, A_.mult, lo8, A_.add)
-    ECw = col(H, 1.0, A_.is_ge, float(WC), A_.mult)
-    ECw = col(ECw, float(EC), A_.add)
-    ts(X("OZ"), X("SO0"), Hh, A_.is_lt, float(WC), A_.mult)
-    tt(X("OW"), X("OZ"), X("SO0"), A_.add)
-    base = lin((pa, 1), (pb, -1), 16)
-    tL = col(p7, 1.0, A_.mult, base, A_.add)
-    hot(X("PLM"), 0, tL, 8)
-    F = {1: lin((ub[0], 1), 0), 2: lin((ub[1], 0.5), 0), 4: lin((ub[2], 0.25), 0)}
-    for m, x, y in ((3, 1, 2), (5, 1, 4), (6, 2, 4), (7, 3, 4)):
+    H = lin((pa, G1 / 32), 0, q="v")
+    base = lin((pb, -1), pa, q="v")
+    F = {1: u1, 2: lin((u2, 0.5), 0, q="v"), 4: lin((u4, 0.25), 0, q="v")}
+    Hh = lin((ph, -4096), H, q="v")
+    tL = lin((p7, 1), base, q="v")
+    for m, x, y in ((5, 1, 4), (3, 1, 2), (6, 2, 4), (7, 3, 4)):
         F[m] = col(F[x], F[y], A_.not_equal)
+    nH = lin((pa, -G1 / 32), 0, q="v")
+    ECw = col(H, 1.0, A_.is_ge, float(WC), A_.mult)
+    ts(X("OZ"), X("SO0"), Hh, A_.is_lt, float(WC), A_.mult)
+    hot(X("PLM"), 0, tL, 24)
+    ECw = col(ECw, float(EC), A_.add)
     sets = []
     for k1, k2 in KS:
         phi = [m for m in range(1, 8) if par(m & k1) and par(m & k2)][0]
@@ -394,57 +404,60 @@ def rank_program(g, core, T, topo):
 
     def lists(t):
         c0 = 128 * t
-        for y in range(2):
-            mm(C("PCN", 0, 64), C("PLM", 8 - 8 * y, 136 - 8 * y), C("OW", c0 + y, c0 + 128, 2), y == 0, y == 1)
         phi, ps1, ps2, one = sets[t]
-        for j, k in enumerate((0,) + KS[t]):
-            s1, s2, s3 = (-1 if j == 0 else 1), 1 - 2 * par(ps1 & k), 1 - 2 * par(ps2 & k)
-            tg = col(F[phi], 1000.0 * s1, A_.mult, base, A_.add)
-            tg = col(F[ps1], float(s2), A_.mult, tg, A_.add)
-            tg = col(F[ps2], 2.0 * s3, A_.mult, tg, A_.add)
-            hot(C("ED", 140 * j, 140 * j + 140, key="ED%d" % j), 0, tg, 12 + 1000 * (j == 0) + par(ps1 & k) + 2 * par(ps2 & k))
-            for y in range(4):
-                o = 140 * j + 12 - 4 * y
-                mm(C("PDM", 32 * j, 32 * j + 32), C("ED", o, o + 128, key="ED%d" % j), C("OW", c0 + y, c0 + 128, 4), y == 0, y == 3)
-        ts(C("LU", 64 * t, 64 * t + 64), C("PCN", 0, 64), nH, A_.add)
-        ts(C("NE", 64 * t, 64 * t + 64), C("PCN", 0, 64), ECw, A_.is_equal)
-        ts(C("LD", 96 * t, 96 * t + 96), C("PDM", 0, 96), nH, A_.add)
+        ks = (0,) + KS[t]
+        tg = [lin((F[phi], -1000 if k == 0 else 1000), base, q="v") for k in ks[:2]]
+        tg = [lin((F[ps1], 1 - 2 * par(ps1 & k)), tg[min(j, 1)], q="v") for j, k in enumerate(ks)]
+        tg = [lin((F[ps2], 2 - 4 * par(ps2 & k)), tg[j], q="v") for j, k in enumerate(ks)]
+        for j, k in enumerate(ks):
+            hot(C("ED", 140 * j, 140 * j + 140, key="ED%d" % j), 0, tg[j], 28 + 1000 * (j == 0) + par(ps1 & k) + 2 * par(ps2 & k))
+        for j in range(3):
+            for r in ("SO0", "OZ"):
+                for y in range(4):
+                    o = 140 * j + 12 - 4 * y
+                    mm(C("PDM", 32 * j, 32 * j + 32), C("ED", o, o + 128, key="ED%d" % j), C(r, c0 + y, c0 + 128, 4),
+                       y == 0 and r == "SO0", y == 3 and r == "OZ")
+        for r in ("SO0", "OZ"):
+            for y in range(2):
+                mm(C("PCN", 0, 64), C("PLM", 8 - 8 * y, 136 - 8 * y), C(r, c0 + y, c0 + 128, 2), y == 0 and r == "SO0", y == 1 and r == "OZ")
+
+    def lists2(t):
+        ts(C("LD", 96 * t, 96 * t + 96, key="LD%d" % t), C("PDM", 0, 96), nH, A_.add)
+        ts(C("LU", 64 * t, 64 * t + 64, key="LU%d" % t), C("PCN", 0, 64), nH, A_.add)
+        ts(C("NE", 64 * t, 64 * t + 64, key="NE%d" % t), C("PCN", 0, 64), ECw, A_.is_equal)
 
     lists(0)
     op("v", lambda e: e.memset(T.WW[:, EC::G1], -BIG), wr=["WWe"])
     eo = lin((ph, -EC / 8), EC)
-    ts(("WOe", T.WO[:, EC::G1]), C("CI", 0, 4), 0.0, A_.mult, eo, A_.add)
-    act(X("EMB"), X("EMS"), scale=-2.0 ** 30)
-    made = set()
-
-    def diffs(t):
-        for k in KS[t]:
-            for d in sorted(set((s ^ k) - s for s in range(8)) - made):
-                made.add(d)
-                tt(C("AD", 144 * (d + 7), 144 * (d + 8), key="AD%d" % d), C("EMS", 16, 160), C("EMB", 16 - d, 160 - d), A_.add)
-            hb = 2 if k >= 4 else 1 if k >= 2 else 0
-            if "u%d" % hb not in made:
-                made.add("u%d" % hb)
-                u = lin((F[1 << hb], 0.5), 0)
-                ts(C("UPC", 64 * hb, 64 * hb + 64, key="UPC%d" % hb), C("CI", 0, 64), 0.0, A_.mult, u, A_.add)
-
-    diffs(0)
-    y1 = lin((pb, 0.0625), 0)
-    q32 = lin((p15, 32), 0)
-    v2 = col(p15, 2.0, A_.mult, y1, A_.add)
-
-    def sels(t):
-        k = npc[0]
-        npc[0] += 2
-        i1, i2 = ("pc%d" % k, T.pc[:, k:k + 1]), ("pc%d" % (k + 1), T.pc[:, k + 1:k + 2])
-        ts(i1, v2, float(t), A_.add)
-        ts(i2, i1, 7, A_.bitwise_and)
-        ts(C("SEL", 8 * t, 8 * t + 8), X("js"), col(i2, 1.0, A_.mult, q32, A_.add), A_.add)
-
-    sels(0)
-    ts(X("XBL"), X("jx"), lin((p12, 0.25), 0), A_.add)
+    act(("WOe", T.WO[:, EC::G1]), C("CI", 0, 4), IDENT, scale=0.0, bias=eo)
+    w8 = lin((u1, 2), (u2, 2), (pb, 0.0625), 0)
+    q32 = lin((p15, 32), w8)
+    xb = lin((p12, 0.25), 0)
     dL = lin((pb, -1 / 32), 0)
     dR = lin((pb, 1 / 16), -0.5)
+    ts(X("XBL"), X("jx"), xb, A_.add)
+    lists2(0)
+
+    def sels(t):
+        z = col(w8, 8.0 - t, A_.is_ge, -8.0, A_.mult)
+        ts(C("SEL", 8 * t, 8 * t + 8, key="SEL%d" % t), X("js"), z, A_.add, lin((q32, 1), t, q="v") if t else q32, A_.add)
+
+    sels(0)
+    act(X("EMB"), X("EMS"), scale=-2.0 ** 30)
+    made = {}
+
+    def diffs(t):
+        ds = sorted(set((s ^ k) - s for s in range(8) for k in KS[t]) - set(made))
+        for i in range(0, len(ds), 3):
+            bank, o = "PZ%d" % (1 + i // 3), 144 * len(made)
+            for j, d in enumerate(ds[i:i + 3]):
+                made[d] = (144 * len(made), "AD%d" % o)
+                mm(C(bank, 144 * j, 144 * j + 144), X("ID"), C("EMS", 16, 160), True, False)
+                mm(C(bank, 144 * j, 144 * j + 144), X("ID"), C("EMB", 16 - d, 160 - d), False, True)
+            act(C("AD", o, 144 * len(made), key="AD%d" % o), C(bank, 0, 144 * len(made) - o))
+
+    diffs(0)
+    tie = {hb: lin((F[hb], 0.5), -0.25) for hb in (1, 2, 4)}
 
     def own_walls(t):
         act(X("XL"), ("SW0", T.SW0[:, 128 * t:128 * t + 128].indirect(T.XBL[:])), IDENT, bias=dL, more=[("XBL", 0)])
@@ -452,36 +465,46 @@ def rank_program(g, core, T, topo):
         act(X("PX1"), X("XL"), IDENT, bias=dR)
 
     own_walls(0)
-    nEC = col(ECw, -1.0, A_.mult)
-    EHc = col(ECw, 1.0, A_.mult, nH, A_.add)
-    temp = lin((p15, 1024), 0)
+    nEC = lin((ECw, -1), 0, q="v")
+    EHc = lin((ECw, 1), nH, q="v")
+    temp = lin((p15, 1024), 0, q="v")
+    hc = lin((p15, -512), (sgn, -0.25), 0, q="v")
     act(X("TMPT"), C("CI", 0, 128), IDENT, scale=0.0, bias=temp)
-    hc = col(sgn, -0.25, A_.mult, lin((p15, -512), 0), A_.add)
-    lists(1)
-    sels(1)
-    diffs(1)
     act(X("EWN"), X("EWP"), scale=-1.0)
     act(X("NSW"), X("SWB"), scale=-1.0)
+    lists(1)
+    sels(1)
+    lists2(1)
+    lists(2)
+    diffs(1)
+    sels(2)
+    lists2(2)
     act(X("KZF"), ("KZ0", T.KZ[:]), more=[("KZ1", 0)])
     later = {}
 
-    def out_setup():
-        tN = lin((pa, 1), (pb, -0.5), (p7, 1), 8)
-        hot(C("tmp", 0, 144), 0, tN, 16)
-        for j, (wh, wl) in enumerate(((0.5, 192), (1344, -384), (-8832, 1))):
-            ts(C("NM", 144 * j, 144 * j + 144), C("tmp", 0, 144), lin((ph, (wl - wh) / 8), wh), A_.mult)
-        later["sA"] = lin((ph, (0.5 - 1 / 384) / 8), 1 / 384)
-        later["bA"] = lin((ph, (1 / 3 - 0.25) / 8), 129 - 1 / 3)
-        later["sB"] = lin((ph, (0.5 - 1 / 2304) / 8), 1 / 2304)
-        later["bB"] = lin((ph, (8.5 / 18 - 0.25) / 8), 129 - 8.5 / 18)
-        later["nt"] = lin((p15, -1024), 0)
-        later["hf"] = lin((p15, 512), -0.25)
+    def out_setup(part):
+        if part == 0:
+            later["tN"] = lin((pb, 0.5), tL, q="v")
+            later["w"] = [lin((ph, (wl - wh) / 8), wh, q="v") for wh, wl in ((0.5, 192), (1344, -384), (-8832, 1))]
+            later["tN"] = col(later["tN"], 24.0, A_.add)
+            later["sA"] = lin((ph, (0.5 - 1 / 384) / 8), 1 / 384, q="v")
+            later["bA"] = lin((ph, (1 / 3 - 0.25) / 8), 129 - 1 / 3, q="v")
+        elif part == 1:
+            later["sB"] = lin((ph, (0.5 - 1 / 2304) / 8), 1 / 2304, q="v")
+            later["bB"] = lin((ph, (8.5 / 18 - 0.25) / 8), 129 - 8.5 / 18, q="v")
+            later["nt"] = lin((p15, -1024), 0, q="v")
+            later["hf"] = lin((p15, 512), -0.25, q="v")
+        else:
+            for j in range(3):
+                ts(C("NM", 144 * j, 144 * j + 144, key="NM%d" % j), C("CI", 0, 144), later["tN"], A_.is_equal, later["w"][j], A_.mult)
 
     def win(x, L, lo, hi):
         return ("W" + x, T["W" + x][:].indirect(T[L][:, lo:hi]))
 
+    now = [0]
+
     def wm(x, L):
-        return [(L, 0), ("own" + x, 0), ("nbd" + x, 0), ("W%se" % x, 0)]
+        return [(L, 0), (L + str(now[0]), 0), ("own" + x, 0), ("nbd" + x, 0), ("W%se" % x, 0)]
 
     def arrived(x, t):
         for q in "vs":
@@ -495,7 +518,7 @@ def rank_program(g, core, T, topo):
     def replies(t):
         for h, c in (("a", slice(0, 512)), ("b", slice(512, 1024))):
             emit("v", lambda e, c=c: e.transpose(T.T1[:, c], T.T0[:, c]), [("T0" + h, 0)], ("T1" + h, 0))
-        cp(X("PK"), ("T1a", T.T1[:].indirect(T.SEL[:, 8 * t:8 * t + 8])), more=[("SEL", 0), ("T1b", 0)])
+        cp(X("PK"), ("T1a", T.T1[:].indirect(T.SEL[:, 8 * t:8 * t + 8])), more=[("SEL%d" % t, 0), ("T1b", 0)])
         ts(X("pz"), C("PK", 0, 64), H, A_.is_lt, float(WC), A_.mult)
         tt(X("PW"), X("pz"), C("PK", 0, 64), A_.add)
         for s2 in range(2):
@@ -529,15 +552,13 @@ def rank_program(g, core, T, topo):
 
     def count_del(t, z, x):
         k = KS[t][z - 1]
-        hb = 2 if k >= 4 else 1 if k >= 2 else 0
         o = C("PZ%d" % z, 0, 64)
-        if x == 0:
-            mm(o, X("ID"), C("UPC", 64 * hb, 64 * hb + 64, key="UPC%d" % hb), True, False)
         for y in range(2):
             for i, s in enumerate(sets[t][3]):
                 a, b = (s ^ k, s) if x else (s, s ^ k)
-                w = 144 * (b - a + 7) + 16 - 8 * y - a
-                mm(o, C("AD", w, w + 128, key="AD%d" % (b - a)), C(("IA%d", "IB%d")[x] % z, 4 * y + i, None, 8), False, x == 1 and y == 1 and i == 3)
+                w = made[b - a][0] + 16 - 8 * y - a
+                mm(o, C("AD", w, w + 128, key=made[b - a][1]), C(("IA%d", "IB%d")[x] % z, 4 * y + i, None, 8),
+                   x + y + i == 0, x == 1 and y == 1 and i == 3)
 
     def fetch(j):
         act(C("TL", 512 * j - 512, 512 * j, key="TL%d" % j), win("W", "LK", 32 * j, 32 * j + 32), more=wm("W", "LK"))
@@ -557,7 +578,8 @@ def rank_program(g, core, T, topo):
                    False, j == 3 and y == 1 and s == 3)
 
     def flags(z):
-        act(X("m%d" % z), C("PZ%d" % z, 0, 64), RELU, bias=-0.25)
+        k = KS[now[0]][z - 1]
+        act(X("m%d" % z), C("PZ%d" % z, 0, 64), RELU, bias=tie[4 if k >= 4 else 2 if k >= 2 else 1])
 
     def Y(x, t):
         return C("Y" + x, 64 * t, 64 * t + 64, key="Y%s%d" % (x, t))
@@ -573,7 +595,7 @@ def rank_program(g, core, T, topo):
         for j, r in enumerate(("SO%d" % (t + 1), "nA", "nB")):
             for f in range(2):
                 o = 144 * j + 16 - 16 * f
-                mm(C("PCN", 0, 64), C("NM", o, o + 128), C(r, f, None, 2), j + f == 0, j + f == 3)
+                mm(C("PCN", 0, 64), C("NM", o, o + 128, key="NM%d" % j), C(r, f, None, 2), j + f == 0, j + f == 3)
         act(Y("O", t), C("PCN", 0, 64), IDENT, bias=1015359.0)
         if t:
             store("y", "O", t)
@@ -586,7 +608,8 @@ def rank_program(g, core, T, topo):
 
     for t in range(3):
         oc = C("SO0", 128 * t, 128 * t + 128)
-        ne = C("NE", 64 * t, 64 * t + 64)
+        ne = C("NE", 64 * t, 64 * t + 64, key="NE%d" % t)
+        now[0] = t
         if t == 0:
             arrived("W", t)
             gather_one(t)
@@ -645,6 +668,8 @@ def rank_program(g, core, T, topo):
         mm(o, X("ID"), X("m1"), False, False)
         mm(o, X("ID"), X("m2"), False, True)
         act(X("GX"), o, SIGN)
+        if t < 2:
+            own_walls(t + 1)
         ts(X("REV"), C("PCN", 0, 64), -15.9, A_.is_lt)
         mm(C("PPF", 0, 64), X("LT"), X("REV"), True, True)
         mm(C("PDM", 0, 128), X("ID"), C("ZB", 0, 128), True, False)
@@ -660,6 +685,8 @@ def rank_program(g, core, T, topo):
             mm(C("PDM", y, 128, 2), C("DM", 128 * y, 128 * y + 128, key="DM%d" % y), X("FI"), False, y == 1)
         mm(C("PZ2", 0, 128), X("ID"), X("TMPT"), True, False)
         mm(C("PZ2", 0, 128), X("NSW"), C("SW0", 128 * t, 128 * t + 128), False, False)
+        if t == 0:
+            out_setup(0)
         ts(X("CLS"), C("PCH", 0, 8), EHc, A_.add)
         tt(X("dd"), win("O", "CLS", 0, 8), oc, A_.subtract, more=wm("O", "CLS"))
         tt(X("ee"), X("dd"), C("PDM", 0, 128), A_.mult)
@@ -668,14 +695,14 @@ def rank_program(g, core, T, topo):
         ts(X("zN"), X(so), Hh, A_.is_lt, float(WC), A_.mult)
         for j, r in enumerate((so, "zN")):
             for y in range(2):
-                mm(C("PX1", 0, 64), C("PLM", 8 - 8 * y, 136 - 8 * y), C(r, y, None, 2), j + y == 0, j + y == 2)
+                mm(C("PPF", 0, 64), C("PLM", 8 - 8 * y, 136 - 8 * y), C(r, y, None, 2), j + y == 0, j + y == 2)
         act(X("FG"), X(so), ABS, bias=-float(EC))
         mm(C("PZ2", 0, 128), X("SLM"), X("FG"), False, True)
-        ts(X("LN"), C("PX1", 0, 64), nH, A_.add)
+        ts(X("LN"), C("PPF", 0, 64), nH, A_.add)
         if t < 2:
             send(t + 1, "O")
             put_own("y", t + 1, "O")
-            mm(C("PX0", 0, 128), X("ID"), X("TMPT"), True, False)
+            mm(C("PCH", 0, 128), X("ID"), X("TMPT"), True, False)
         cp(C("U2", 0, 384, key="U2a"), win("W", "LN", 0, 24), more=wm("W", "LN"))
         act(C("U2", 384, 704, key="U2b"), win("W", "LN", 24, 44), more=wm("W", "LN"))
         act(C("U2", 704, 1024, key="U2c"), win("W", "LN", 44, 64), more=wm("W", "LN"))
@@ -693,26 +720,24 @@ def rank_program(g, core, T, topo):
         tt(X("ww"), C("SC", 7, None, 8, key="SCa"), C("PZ2", 0, 128), A_.max, more=[("SCb", 0), ("SCc", 0)])
         if t < 2:
             sw = "SW%d" % (t + 1)
-            mm(C("PX0", 0, 128), X("NSW"), X("ww"), False, True)
-            tt(X("ws"), X("ww"), C("PX0", 0, 128), A_.add)
+            mm(C("PCH", 0, 128), X("NSW"), X("ww"), False, True)
+            if t == 0:
+                out_setup(1)
+            tt(X("ws"), X("ww"), C("PCH", 0, 128), A_.add)
             ts(X("wi"), X("ws"), 0.5, A_.mult, hc, A_.add)
-            tt(X(sw), X("wi"), C("PX0", 0, 128), A_.min)
+            tt(X(sw), X("wi"), C("PCH", 0, 128), A_.min)
             send(t + 1, "W")
             put_own("s", t + 1, "W")
             put_nb("y", t + 1, "O")
             put_nb("y", t + 1, "W")
-            own_walls(t + 1)
             if t == 0:
-                lists(2)
-                sels(2)
+                out_setup(2)
                 diffs(2)
-            else:
-                out_setup()
-                numbers(0)
-                numbers(1)
+            numbers(t)
             unpair(sw, ("PZ1", "PZ2"))
             act(Y("R", t), C("PZ1", 256, 320))
             act(Y("L", t), C("PZ2", 256, 320), scale=-1.0)
+            now[0] = t + 1
             gather_slots(t + 1)
             replies(t + 1)
             reply_parts()

@@ -33,21 +33,28 @@ SCRATCH = {
     "AD": _b(144 * 15), "UPC": _b(192), "EWP": _b(160), "EWN": _b(160), "KM": _b(320), "KZ": _b(320), "KZF": _f(320), "CM": _b(144),
     "DM": _b(256), "LT": _b(128), "SLM": _b(128), "ZB": _b(160), "ON": _b(192), "SG": _b(160), "NM": _b(432),
     "SEL": _u(24), "XBL": _u(32), "LU": _u(192), "LD": _u(288), "NE": _b(192),
-    "T0": _b(1024), "T1": _b(1024), "PK": _b(128), "PW": _b(64), "pz": _b(64), "LK": _u(128), "KH": _b(64), "KL": _b(64),
-    "XL": _f(512), "U1": _f(512), "D1": _b(512), "D2": _b(512), "IA1": _b(512), "IB1": _b(512), "IA2": _b(512), "IB2": _b(512),
+    "T0": _b(1024), "T1": _b(1024), "PK": _b(128), "PW": _b(64), "pz": _b(64), "LK": _u(128), "NEC": _b(64), "HHT": _b(128),
+    "NID": _b(128), "PLW": _b(136), "N31": _b(128), "DG": _b(384), "AR1": _b(64), "AR2": _b(64), "AQ1": _b(64), "AQ2": _b(64),
+    "XL": _f(512), "U1": _f(512), "D1": _b(512), "D2": _b(512), "IA1": _b(512), "IA2": _b(512),
     "TL": _f(1536), "VI": _b(2048), "m1": _b(64), "m2": _b(64), "GX": _b(64), "REV": _b(64), "FI": _b(64), "FH": _b(64), "FL": _b(64),
-    "CLS": _u(8), "dd": _f(128), "ee": _f(128), "zN": _b(128), "FG": _b(128), "LN": _u(64), "U2": _f(1024), "SC": _f(1024),
+    "CLS": _u(8), "dd": _f(128), "ee": _b(128), "zN": _b(128), "FG": _b(128), "LN": _u(64), "U2": _f(1024), "SC": _f(1024),
     "ww": _f(128), "ws": _f(128), "wi": _i(128), "wn": _f(128), "nA": _b(128), "nB": _b(128), "YR": _f(192), "YL": _f(192), "YO": _f(192),
     "PX0": ("psum", [128, 512], "float32"), "PX1": ("psum", [128, 512], "float32"), "PZ1": ("psum", [128, 512], "float32"),
     "PZ2": ("psum", [128, 512], "float32"), "PCN": ("psum", [128, 512], "float32"), "PPF": ("psum", [128, 512], "float32"),
     "PCH": ("psum", [128, 512], "float32"), "PDM": ("psum", [128, 512], "float32"),
-    "DW0": ("dram", [256, 384], "float32"), "DW1": ("dram", [256, 128], "float32"), "DW2": ("dram", [256, 128], "float32"),
-    "DO0": ("dram", [256, 384], "bfloat16"), "DO1": ("dram", [256, 128], "bfloat16"), "DO2": ("dram", [256, 128], "bfloat16"),
 }
+PARTS = {"Wa": ("W", 0, 0, 192), "O0": ("O", 0, 0, 384), "Wb": ("W", 0, 192, 384),
+         "O1": ("O", 1, 0, 128), "W1": ("W", 1, 0, 128), "O2": ("O", 2, 0, 128), "W2": ("W", 2, 0, 128)}
+CALLS = {"Wa": [[0], [1, 2], [3]], "O0": [[0], [1, 2], [3]], "Wb": [[0], [1, 2], [3]]}
+for _n, (_x, _e, _lo, _hi) in PARTS.items():
+    SCRATCH["D" + _n] = ("dram", [256, _hi - _lo], "float32" if _x == "W" else "bfloat16")
 SEMAPHORES = ["qv", "qs", "qp", "qg", "ls", "ldO", "ldW", "go1", "go2"] + [
-    "%s%s%d" % (k, x, e) for k in ("arr", "own", "nbd", "fA", "fB", "dA") for x in "WO" for e in range(3)] + [
-    "%s%d" % (k, e) for k in ("oO", "oR", "oL") for e in range(1, 3)]
-ORDER = ["WO", "OW", "OW"]
+    "%s%s%d" % (k, x, e) for k in ("arr", "own", "nbd") for x in "WO" for e in range(3)] + [
+    k + n for k in ("fA", "fB", "dA", "ls") for n in PARTS] + ["%s%d" % (k, e) for k in ("oO", "oR", "oL") for e in range(1, 3)]
+
+
+STAGE = "u0 f1 c0 k0 d1 A1 f2 d2 A2 a1 r0 c1 B1 b1 f3 m1 a2 r1 B2 n1 b2 c2 m2 r2 n2 c3 r3"
+CUT = [0, 320, 704, 1024]
 
 
 def pl(bits):
@@ -65,68 +72,90 @@ def par(x):
 
 def plan(T, topo):
     cores = list(T.cores)
-    role, of, extra = {}, {}, []
+    role, extra = {}, []
+    for ch in sorted(set(topo.chip(c) for c in cores)):
+        here = [r for r, c in enumerate(cores) if topo.chip(c) == ch]
+        free = [h for h in topo.cores_of(cores[here[0]]) if h not in cores]
+        for x in "WO":
+            for q in [q for q in range(len(cores)) if q not in here]:
+                like = cores[here[0]] if len(here) == 1 else cores[q]
+                free.sort(key=lambda h: topo.die(h) != topo.die(like))
+                if free:
+                    role[free.pop(0)] = {"ranks": here, "A": q, "x": x, "feed": cores[q], "fwd": []}
+                else:
+                    extra.append((here[0], q, x))
+    role2, of, extra2 = {}, {}, []
     for r, c in enumerate(cores):
         near = [h for h in topo.cores_of(c) if topo.die(h) == topo.die(c) and h not in cores]
         off = [q for q, d in enumerate(cores) if topo.chip(d) != topo.chip(c)]
-        extra += [(r, q) for q in off[len(near):]]
+        extra2 += [(r, q, x) for q in off[len(near):] for x in "WO"]
         for q, h in zip(off, near):
-            role[h] = {"rank": r, "A": q, "feed": cores[q], "fwd": []}
+            role2[h] = {"ranks": [r], "A": q, "x": "WO", "feed": cores[q], "fwd": []}
             of[(r, q)] = h
     for (r, q), h in of.items():
         if topo.die(cores[r]) != topo.die(cores[q]):
             for r2 in range(len(cores)):
                 if r2 != r and topo.chip(cores[r2]) == topo.chip(cores[r]) and topo.die(cores[r2]) == topo.die(cores[q]):
-                    role[h]["feed"] = of[(r2, q)]
-                    role[of[(r2, q)]]["fwd"].append(h)
-    return cores, role, extra
+                    role2[h]["feed"] = of[(r2, q)]
+                    role2[of[(r2, q)]]["fwd"].append(h)
+    return cores, [role, role2, role2], [extra, extra2, extra2]
 
 
-def helper(g, core, T, topo, cores, role):
-    info = role[core]
-    rc = cores[info["rank"]]
-    eng = topo.engines(core, rc)
-    direct = info["feed"] in cores
+def calls(info, name, cores):
+    return CALLS.get(name, [[0, 1, 2, 3]])
+
+
+def helper(g, core, T, topo, cores, roles):
     ls = 0
-    for e in range(3):
-        for x in ORDER[e]:
-            n, buf, fa = PN[e], T["D%s%d" % (x, e)], T.sem["fA%s%d" % (x, e)]
-            got = len(topo.engines(info["feed"], core)) * (1 if direct else 2)
-            g.wait_ge(fa, got)
-            if direct:
-                g.sync.wait_ge(fa, got)
-                g.sync.dma_start(buf[128:224, :], buf[0:96, :]).then_inc(T.sem["dA%s%d" % (x, e)], 16)
-            for h in info["fwd"]:
-                en = topo.engines(core, h)
-                g.remote_dma_fused([RemoteDMATransfer(dst_ids=[dst(topo, h)] * 2, dma_engine_mask=pl(en), remote_sem=fa,
-                                                      srcs=[buf[0:128, :]], dsts=[buf[0:128, :], buf[128:256, :]])], local_sem=T.sem.ls)
-                ls += len(en)
-            if e and x == ORDER[e][0]:
-                g.wait_ge(T.sem["go%d" % e], 1)
-            if direct:
-                g.wait_ge(T.sem["dA%s%d" % (x, e)], 16)
-            w = len(eng) // 4
+    for name, (x, e, lo, hi) in PARTS.items():
+        info = roles[e].get(core)
+        if info is None or x not in info["x"]:
+            continue
+        rcs = [cores[r] for r in info["ranks"]]
+        eng = topo.engines(core, rcs[0])
+        direct = info["feed"] in cores
+        got = len(topo.engines(info["feed"], core)) * (1 if direct else 2)
+        buf, fa = T["D" + name], T.sem["fA" + name]
+        if direct:
+            g.sync.wait_ge(fa, got)
+            g.sync.dma_start(buf[128:224, :], buf[0:96, :]).then_inc(T.sem["dA" + name], 16)
+        g.wait_ge(fa, got)
+        for h in info["fwd"]:
+            en = topo.engines(core, h)
+            g.remote_dma_fused([RemoteDMATransfer(dst_ids=[dst(topo, h)] * 2, dma_engine_mask=pl(en), remote_sem=fa,
+                                                  srcs=[buf[0:128, :]], dsts=[buf[0:128, :], buf[128:256, :]])], local_sem=T.sem.ls)
+            ls += len(en)
+        if e and x == "O":
+            g.wait_ge(T.sem["go%d" % e], len(rcs))
+        for call in calls(info, name, cores):
+            if direct and call[-1] and not call[0] > 1:
+                g.wait_ge(T.sem["dA" + name], 16)
+            w = len(eng) // len(call)
             trs = []
-            for k in range(4):
+            for j, k in enumerate(call):
                 c0 = k * G1 + info["A"] * R1 + (e - 1) * B1 * (e > 0)
-                trs.append(RemoteDMATransfer(dst_ids=[dst(topo, rc)], dma_engine_mask=pl(eng[k * w:(k + 1) * w]),
+                trs.append(RemoteDMATransfer(dst_ids=[dst(topo, c) for c in rcs], dma_engine_mask=pl(eng[j * w:(j + 1) * w]),
                                              remote_sem=T.sem["arr%s%d" % (x, e)],
-                                             srcs=[buf[32 * k:32 * k + 128, :]], dsts=[T["W" + x][:, c0:c0 + n]]))
+                                             srcs=[buf[32 * k:32 * k + 128, :]], dsts=[T["W" + x][:, c0 + lo:c0 + hi]] * len(rcs)))
                 ls += w
             g.remote_dma_fused(trs, local_sem=T.sem.ls)
-    g.wait_ge(T.sem.ls, ls)
+    if ls:
+        g.wait_ge(T.sem.ls, ls)
 
 
 def rank_program(g, core, T, topo):
-    cores, role, extra = plan(T, topo)
+    cores, roles, extras = plan(T, topo)
     rank = T.rank_of(core)
     if rank is None:
-        if core in role:
-            helper(g, core, T, topo, cores, role)
+        helper(g, core, T, topo, cores, roles)
         return
-    mine = [h for h in role if role[h]["rank"] == rank]
+    mine = [h for h in roles[1] if rank in roles[1][h]["ranks"]]
     near = [q for q, c in enumerate(cores) if q != rank and topo.chip(c) == topo.chip(core)]
-    arr_n = sum(len(topo.engines(h, core)) for h in mine)
+    arr_n = {}
+    for name, (x, e, lo, hi) in PARTS.items():
+        for h, info in roles[e].items():
+            if rank in info["ranks"] and x in info["x"]:
+                arr_n[x, e] = arr_n.get((x, e), 0) + len(topo.engines(h, core)) * len(calls(info, name, cores))
     Q = {"v": g.vector, "s": g.scalar, "p": g.tensor, "g": g, "y": g.sync}
     QS = {"v": "qv", "s": "qs", "p": "qp", "g": "qg"}
     cnt, known, lastw, readers, lastx, alias = {}, {q: {} for q in Q}, {}, {}, {}, {}
@@ -287,21 +316,22 @@ def rank_program(g, core, T, topo):
     ts(C("SW0", 1, None, 2, key="SW0b"), C("WI", 192, 384), sgn, A_.mult)
     both("SW0")
 
-    def send(e, x):
-        name = "S%s%d" % (x, e)
+    def send(part):
+        x, e, lo, hi = PARTS[part]
+        name, nb = "S%s%d" % (x, e), T["N%s%d" % (x, e)][:, lo:hi]
         deps("g", [name], [], ())
-        offs = [(h, T["D%s%d" % (x, e)][0:128, :]) for h in role if role[h]["feed"] == core]
-        offs += [(cores[r], T["N%s%d" % (x, e)][:]) for r, q in extra if q == rank]
+        offs = [(h, T["D" + part][0:128, :]) for h, info in roles[e].items() if info["feed"] == core and x in info["x"]]
+        offs += [(cores[r], nb) for r, q, y in extras[e] if q == rank and y == x]
         en = topo.engines(core, offs[0][0])
-        trs = [RemoteDMATransfer(dst_ids=[dst(topo, h) for h, _ in offs], dma_engine_mask=pl(en), remote_sem=T.sem["fA%s%d" % (x, e)],
-                                 srcs=[T[name][:]], dsts=[d for _, d in offs])]
-        nls[0] += len(en)
+        trs = [RemoteDMATransfer(dst_ids=[dst(topo, h) for h, _ in offs], dma_engine_mask=pl(en), remote_sem=T.sem["fA" + part],
+                                 srcs=[T[name][:, lo:hi]], dsts=[d for _, d in offs])]
+        cnt["ls" + part] = len(en)
         for q in near:
             e2 = [y for y in topo.engines(core, cores[q]) if y not in en]
-            trs.append(RemoteDMATransfer(dst_ids=[dst(topo, cores[q])], dma_engine_mask=pl(e2), remote_sem=T.sem["fB%s%d" % (x, e)],
-                                         srcs=[T[name][:]], dsts=[T["N%s%d" % (x, e)][:]]))
-            nls[0] += len(e2)
-        g.remote_dma_fused(trs, local_sem=T.sem.ls)
+            trs.append(RemoteDMATransfer(dst_ids=[dst(topo, cores[q])], dma_engine_mask=pl(e2), remote_sem=T.sem["fB" + part],
+                                         srcs=[T[name][:, lo:hi]], dsts=[nb]))
+            cnt["ls" + part] += len(e2)
+        g.remote_dma_fused(trs, local_sem=T.sem["ls" + part])
 
     def put(qu, e, x, sem, name, src, rd):
         nn, W = PN[e], T["W" + x]
@@ -314,18 +344,21 @@ def rank_program(g, core, T, topo):
         deps(qu, [], ["W" + x], ())
         dma(qu, sem + x + str(e), pairs, rd=rd, wr=[sem + x])
 
-    def put_own(qu, e, x):
+    def put_own(qu, e, x, after=None):
+        if after:
+            Q[qu].wait_ge(T.sem["ls" + after], cnt["ls" + after])
         put(qu, e, x, "own", "S%s%d" % (x, e), rank, ["S%s%d" % (x, e)])
 
     def put_nb(qu, e, x):
-        for q in near + [q for r, q in extra if r == rank]:
-            h = [h for h in role if role[h]["feed"] == cores[q]][0]
+        for q in near + [q for r, q, y in extras[e] if r == rank and y == x]:
+            h = [h for h, info in roles[e].items() if info["feed"] == cores[q]][0]
             en = topo.engines(cores[q], core)
-            Q[qu].wait_ge(T.sem["f%s%s%d" % ("B" if q in near else "A", x, e)],
-                          len([y for y in en if y not in topo.engines(cores[q], h)] if q in near else en))
+            for part in [p for p, v in PARTS.items() if v[:2] == (x, e)]:
+                Q[qu].wait_ge(T.sem[("fB" if q in near else "fA") + part],
+                              len([y for y in en if y not in topo.engines(cores[q], h)] if q in near else en))
             put(qu, e, x, "nbd", "N%s%d" % (x, e), q, [])
 
-    send(0, "W")
+    send("Wa")
     put_own("y", 0, "W")
     n = X("OI")
     fls = [C("fl", 192 * j, 192 * j + 192, key="fl%d" % j) for j in range(5)]
@@ -345,10 +378,11 @@ def rank_program(g, core, T, topo):
     act(C("SO0", 0, None, 2, key="SO0a"), C("PX0", 0, 192), IDENT, bias=bO)
     ts(C("SO0", 1, None, 2, key="SO0b"), C("PX1", 0, 192), bO, A_.add)
     both("SO0")
-    send(0, "O")
-    put_own("s", 0, "O")
-    put_nb("y", 0, "W")
+    send("O0")
+    send("Wb")
+    put_own("y", 0, "O", "Wb")
     put_nb("y", 0, "O")
+    put_nb("y", 0, "W")
     def fill(out, val):
         emit("g", lambda e: e.iota(raw(out), [[0, raw(out).shape[1]]], val, 0, allow_small_or_imprecise_dtypes=True), [], out)
 
@@ -443,21 +477,26 @@ def rank_program(g, core, T, topo):
         ts(C("SEL", 8 * t, 8 * t + 8, key="SEL%d" % t), X("js"), z, A_.add, lin((q32, 1), t, q="v") if t else q32, A_.add)
 
     sels(0)
-    act(X("EMB"), X("EMS"), scale=-2.0 ** 30)
-    made = {}
+    act(X("N31"), X("ID"), scale=-31.0)
+    made, dc = {}, {}
 
     def diffs(t):
-        ds = sorted(set((s ^ k) - s for s in range(8) for k in KS[t]) - set(made))
+        ds = sorted(set(abs((s ^ k) - s) for s in sets[t][3] for k in KS[t]) - set(made))
         for i in range(0, len(ds), 3):
-            bank, o = "PZ%d" % (1 + i // 3), 144 * len(made)
+            bank, o = ("PZ1", "PDM")[i // 3], 144 * len(made)
             for j, d in enumerate(ds[i:i + 3]):
                 made[d] = (144 * len(made), "AD%d" % o)
                 mm(C(bank, 144 * j, 144 * j + 144), X("ID"), C("EMS", 16, 160), True, False)
-                mm(C(bank, 144 * j, 144 * j + 144), X("ID"), C("EMB", 16 - d, 160 - d), False, True)
+                mm(C(bank, 144 * j, 144 * j + 144), X("ID"), C("EMS", 16 - d, 160 - d), False, True)
             act(C("AD", o, 144 * len(made), key="AD%d" % o), C(bank, 0, 144 * len(made) - o))
+        f = F[sets[t][0]]
+        q = "s" if t else "v"
+        act(C("DG", 128 * t, 128 * t + 128, key="DG%d" % t), X("ID"), scale=lin((f, 33), -1, q=q))
+        b = lin((f, -129 * 33), 129 * 32 - 0.25, q=q)
+        for z, k in enumerate(KS[t]):
+            dc[t, z + 1] = lin((F[4 if k >= 4 else 2 if k >= 2 else 1], 0.5), b, q=q)
 
     diffs(0)
-    tie = {hb: lin((F[hb], 0.5), -0.25) for hb in (1, 2, 4)}
 
     def own_walls(t):
         act(X("XL"), ("SW0", T.SW0[:, 128 * t:128 * t + 128].indirect(T.XBL[:])), IDENT, bias=dL, more=[("XBL", 0)])
@@ -470,16 +509,15 @@ def rank_program(g, core, T, topo):
     temp = lin((p15, 1024), 0, q="v")
     hc = lin((p15, -512), (sgn, -0.25), 0, q="v")
     act(X("TMPT"), C("CI", 0, 128), IDENT, scale=0.0, bias=temp)
+    act(X("NEC"), C("CI", 0, 64), IDENT, scale=0.0, bias=nEC)
+    act(X("HHT"), C("CI", 0, 128), IDENT, scale=0.0, bias=Hh)
+    act(X("NID"), X("ID"), scale=-1.0)
+    act(X("PLW"), X("PLM"), scale=float(WC))
     act(X("EWN"), X("EWP"), scale=-1.0)
     act(X("NSW"), X("SWB"), scale=-1.0)
     lists(1)
     sels(1)
     lists2(1)
-    lists(2)
-    diffs(1)
-    sels(2)
-    lists2(2)
-    act(X("KZF"), ("KZ0", T.KZ[:]), more=[("KZ1", 0)])
     later = {}
 
     def out_setup(part):
@@ -508,7 +546,7 @@ def rank_program(g, core, T, topo):
 
     def arrived(x, t):
         for q in "vs":
-            Q[q].wait_ge(T.sem["arr%s%d" % (x, t)], arr_n)
+            Q[q].wait_ge(T.sem["arr%s%d" % (x, t)], arr_n[x, t])
 
     def gather_slots(t):
         arrived("O", t)
@@ -525,17 +563,17 @@ def rank_program(g, core, T, topo):
             o, l = C("PPF", 64 * s2, 64 * s2 + 64), C("KM", 160 * s2 + 16, 160 * s2 + 144, key="KM%d" % s2)
             mm(o, l, C("PK", 64, 128), True, False)
             mm(o, l, X("PW"), False, True)
+        ts(X("LK"), C("PPF", 0, 128), nH, A_.add)
+
+    def reply_parts():
+        mm(C("PPF", 128, 192), X("ID"), X("NEC"), True, False)
         for hl in range(2):
             for y in range(2):
                 for b in range(2):
                     o = 160 * y + 16 - 16 * b
-                    mm(C("PCH", 64 * hl + y, 64 * hl + 64, 2), C("KZ", o, o + 128, key="KZ%d" % y),
-                       C("PK", 96 - 32 * b, 128 - 32 * b) if hl else C("PW", 32 - 32 * b, 64 - 32 * b), b == 0, b == 1)
-        ts(X("LK"), C("PPF", 0, 128), nH, A_.add)
-
-    def reply_parts():
-        act(X("KH"), C("PCH", 0, 64), IDENT, bias=nEC)
-        act(X("KL"), C("PCH", 64, 128))
+                    mm(C("PPF", 128 + 64 * hl + y, 192 + 64 * hl, 2), C("KZ", o, o + 128, key="KZ%d" % y),
+                       C("PK", 96 - 32 * b, 128 - 32 * b) if hl else C("PW", 32 - 32 * b, 64 - 32 * b),
+                       hl == 1 and b == 0, b == 1 and hl + y > 0)
 
     def gather_one(t):
         act(X("U1"), win("W", "LD", 96 * t, 96 * t + 32), more=wm("W", "LD"))
@@ -543,22 +581,24 @@ def rank_program(g, core, T, topo):
     def diff(t, z):
         tt(X("D%d" % z), win("W", "LD", 96 * t + 32 * z, 96 * t + 32 * z + 32), X("U1"), A_.subtract, more=wm("W", "LD"))
 
-    def signs(z, q):
-        for name, sc in (("IA%d" % z, 1.0), ("IB%d" % z, -1.0)):
-            if q == "v":
-                ts(X(name), X("D%d" % z), sc, A_.mult, 0.0, A_.max)
-            else:
-                act(X(name), X("D%d" % z), RELU, scale=sc)
+    def signs(z):
+        ts(X("IA%d" % z), X("D%d" % z), 1.0, A_.min, -31 / 512, A_.max)
 
-    def count_del(t, z, x):
+    def count_del(t, z):
         k = KS[t][z - 1]
-        o = C("PZ%d" % z, 0, 64)
         for y in range(2):
             for i, s in enumerate(sets[t][3]):
-                a, b = (s ^ k, s) if x else (s, s ^ k)
-                w = made[b - a][0] + 16 - 8 * y - a
-                mm(o, C("AD", w, w + 128, key=made[b - a][1]), C(("IA%d", "IB%d")[x] % z, 4 * y + i, None, 8),
-                   x + y + i == 0, x == 1 and y == 1 and i == 3)
+                d = abs((s ^ k) - s)
+                w = made[d][0] + 16 - 8 * y - min(s, s ^ k)
+                mm(C("PZ%d" % z, 0, 64), C("AD", w, w + 128, key=made[d][1]), C("IA%d" % z, 4 * y + i, None, 8), y + i == 0, y + i == 4)
+
+    def whole(t, z):
+        act(X("AR%d" % z), C("PZ%d" % z, 0, 64), IDENT, bias=129.485)
+        act(X("AQ%d" % z), C("PZ%d" % z, 0, 64), IDENT, bias=129 - 0.48)
+
+    def whole2(t, z):
+        mm(C("PZ%d" % z, 256, 320), X("N31"), X("AR%d" % z), True, False)
+        mm(C("PZ%d" % z, 256, 320), C("DG", 128 * t, 128 * t + 128, key="DG%d" % t), X("AQ%d" % z), False, True)
 
     def fetch(j):
         act(C("TL", 512 * j - 512, 512 * j, key="TL%d" % j), win("W", "LK", 32 * j, 32 * j + 32), more=wm("W", "LK"))
@@ -578,8 +618,7 @@ def rank_program(g, core, T, topo):
                    False, j == 3 and y == 1 and s == 3)
 
     def flags(z):
-        k = KS[now[0]][z - 1]
-        act(X("m%d" % z), C("PZ%d" % z, 0, 64), RELU, bias=tie[4 if k >= 4 else 2 if k >= 2 else 1])
+        act(X("m%d" % z), C("PZ%d" % z, 256, 320), RELU, bias=dc[now[0], z])
 
     def Y(x, t):
         return C("Y" + x, 64 * t, 64 * t + 64, key="Y%s%d" % (x, t))
@@ -611,58 +650,36 @@ def rank_program(g, core, T, topo):
         ne = C("NE", 64 * t, 64 * t + 64, key="NE%d" % t)
         now[0] = t
         if t == 0:
-            arrived("W", t)
-            gather_one(t)
-            diff(t, 1)
-            signs(1, "v")
-            count_del(t, 1, 0)
-            count_del(t, 1, 1)
-            diff(t, 2)
             gather_slots(t)
-            signs(2, "s")
-            count_del(t, 2, 0)
             replies(t)
-            count_del(t, 2, 1)
-            mm(C("PCN", 0, 64), X("SWB"), ne, True, False)
-            fetch(1)
-            compare(0)
-            count_rep(0)
-            flags(1)
-            flags(2)
-            fetch(2)
-            compare(1)
-            count_rep(1)
-            reply_parts()
-            fetch(3)
-            compare(2)
-            count_rep(2)
-        else:
-            arrived("W", t)
-            mm(C("PCN", 0, 64), X("SWB"), ne, True, False)
-            gather_one(t)
-            compare(0)
-            count_rep(0)
-            fetch(1)
-            diff(t, 1)
-            signs(1, "v")
-            count_del(t, 1, 0)
-            count_del(t, 1, 1)
-            fetch(2)
-            diff(t, 2)
-            signs(2, "s")
-            compare(1)
-            count_rep(1)
-            count_del(t, 2, 0)
-            fetch(3)
-            compare(2)
-            count_rep(2)
-            count_del(t, 2, 1)
-            flags(1)
-            flags(2)
-        compare(3)
-        for z in (1, 2):
-            mm(C("PCN", 0, 64), X("ID"), X("m%d" % z), False, False)
-        count_rep(3)
+        arrived("W", t)
+        mm(C("PCN", 0, 64), X("SWB"), ne, True, False)
+        for step in STAGE.split():
+            z = int(step[1])
+            if step[0] == "u":
+                gather_one(t)
+            elif step[0] == "c":
+                compare(z)
+            elif step[0] == "r":
+                count_rep(z)
+            elif step[0] == "f":
+                fetch(z)
+            elif step[0] == "d":
+                diff(t, z)
+            elif step[0] == "A":
+                signs(z)
+            elif step[0] == "a":
+                count_del(t, z)
+            elif step[0] == "B":
+                whole(t, z)
+            elif step[0] == "b":
+                whole2(t, z)
+            elif step[0] == "k":
+                reply_parts()
+            elif step[0] == "m":
+                flags(z)
+            else:
+                mm(C("PCN", 0, 64), X("ID"), X("m%d" % z), False, False)
         o = C("PZ1", 64, 128)
         mm(o, X("SWB"), ne, True, False)
         mm(o, X("ID"), X("m1"), False, False)
@@ -676,48 +693,57 @@ def rank_program(g, core, T, topo):
         for y in range(2):
             mm(C("PDM", y, 128, 2), C("DM", 128 * y, 128 * y + 128, key="DM%d" % y), X("GX"), False, False)
         ts(X("FI"), C("PPF", 0, 64), 0.0, A_.is_lt)
-        tt(X("FH"), X("FI"), X("KH"), A_.mult)
-        tt(X("FL"), X("FI"), X("KL"), A_.mult)
+        tt(X("FH"), X("FI"), C("PPF", 128, 192), A_.mult)
+        tt(X("FL"), X("FI"), C("PPF", 192, 256), A_.mult)
         for x in ("FH", "FL"):
             for c in range(8):
                 mm(C("PCH", 0, 8), C("CM", 16 - 2 * c, 144 - 2 * c), C(x, c, None, 8), x == "FH" and c == 0, x == "FL" and c == 7)
         for y in range(2):
             mm(C("PDM", y, 128, 2), C("DM", 128 * y, 128 * y + 128, key="DM%d" % y), X("FI"), False, y == 1)
-        mm(C("PZ2", 0, 128), X("ID"), X("TMPT"), True, False)
-        mm(C("PZ2", 0, 128), X("NSW"), C("SW0", 128 * t, 128 * t + 128), False, False)
+        mm(C("PZ1", 128, 256), X("ID"), X("HHT"), True, False)
+        mm(C("PZ1", 128, 256), X("NID"), oc, False, True)
+        mm(C("PCN", 128, 256), X("ID"), oc, True, True)
+        for y in range(2):
+            mm(C("PPF", 0, 64), C("PLM", 8 - 8 * y, 136 - 8 * y), C("SO0", 128 * t + y, 128 * t + 128, 2), y == 0, False)
         if t == 0:
             out_setup(0)
         ts(X("CLS"), C("PCH", 0, 8), EHc, A_.add)
         tt(X("dd"), win("O", "CLS", 0, 8), oc, A_.subtract, more=wm("O", "CLS"))
         tt(X("ee"), X("dd"), C("PDM", 0, 128), A_.mult)
         so = "SO%d" % (t + 1)
-        tt(X(so), X("ee"), oc, A_.add)
-        ts(X("zN"), X(so), Hh, A_.is_lt, float(WC), A_.mult)
-        for j, r in enumerate((so, "zN")):
+        tt(X("zN"), X("ee"), C("PZ1", 128, 256), A_.is_lt)
+        for M, r in (("PLM", "ee"), ("PLW", "zN")):
             for y in range(2):
-                mm(C("PPF", 0, 64), C("PLM", 8 - 8 * y, 136 - 8 * y), C(r, y, None, 2), j + y == 0, j + y == 2)
-        act(X("FG"), X(so), ABS, bias=-float(EC))
-        mm(C("PZ2", 0, 128), X("SLM"), X("FG"), False, True)
+                mm(C("PPF", 0, 64), C(M, 8 - 8 * y, 136 - 8 * y), C(r, y, None, 2), False, r == "zN" and y == 1)
+        tt(X(so), X("ee"), C("PCN", 128, 256), A_.add)
         ts(X("LN"), C("PPF", 0, 64), nH, A_.add)
+        act(X("FG"), X(so), ABS, bias=-float(EC))
+        mm(C("PZ2", 0, 128), X("ID"), X("TMPT"), True, False)
+        mm(C("PZ2", 0, 128), X("NSW"), C("SW0", 128 * t, 128 * t + 128), False, False)
+        mm(C("PZ2", 0, 128), X("SLM"), X("FG"), False, True)
         if t < 2:
-            send(t + 1, "O")
+            send("O%d" % (t + 1))
             put_own("y", t + 1, "O")
+            put_nb("y", t + 1, "O")
             mm(C("PCH", 0, 128), X("ID"), X("TMPT"), True, False)
-        cp(C("U2", 0, 384, key="U2a"), win("W", "LN", 0, 24), more=wm("W", "LN"))
-        act(C("U2", 384, 704, key="U2b"), win("W", "LN", 24, 44), more=wm("W", "LN"))
-        act(C("U2", 704, 1024, key="U2c"), win("W", "LN", 44, 64), more=wm("W", "LN"))
+        cuts = list(zip(CUT, CUT[1:]))
+        for lo, hi in cuts:
+            (act if lo else cp)(C("U2", lo, hi, key="U2%d" % lo), win("W", "LN", lo // 16, hi // 16), more=wm("W", "LN"))
         if t < 2:
-            need("g", lastw["U2a"])
-            need("g", lastw["U2c"])
+            need("g", lastw["U20"])
+            need("g", lastw["U2%d" % CUT[-2]])
             g.remote_dma_fused([RemoteDMATransfer(dst_ids=[dst(topo, h)], dma_engine_mask=1 << topo.engines(core, h)[j],
                                                   remote_sem=T.sem["go%d" % (t + 1)]) for j, h in enumerate(mine)], local_sem=T.sem.ls)
             nls[0] += len(mine)
+            diffs(t + 1)
+            if t == 0:
+                act(X("KZF"), ("KZ0", T.KZ[:]), more=[("KZ1", 0)])
         else:
             numbers(t)
-        for hf, lo, hi in (("a", 0, 384), ("b", 384, 704), ("c", 704, 1024)):
+        for lo, hi in cuts:
             emit("v", lambda e, c=slice(lo, hi), w=hi - lo: e.tensor_tensor_scan(T.SC[:, c], T.RS[:, 0:w], T.U2[:, c], 0.0, A_.add, A_.max),
-                 [("RS", 0), ("U2" + hf, 0)], ("SC" + hf, 0))
-        tt(X("ww"), C("SC", 7, None, 8, key="SCa"), C("PZ2", 0, 128), A_.max, more=[("SCb", 0), ("SCc", 0)])
+                 [("RS", 0), ("U2%d" % lo, 0)], ("SC%d" % lo, 0))
+        tt(X("ww"), C("SC", 7, None, 8, key="SC0"), C("PZ2", 0, 128), A_.max, more=[("SC%d" % lo, 0) for lo, hi in cuts])
         if t < 2:
             sw = "SW%d" % (t + 1)
             mm(C("PCH", 0, 128), X("NSW"), X("ww"), False, True)
@@ -726,21 +752,22 @@ def rank_program(g, core, T, topo):
             tt(X("ws"), X("ww"), C("PCH", 0, 128), A_.add)
             ts(X("wi"), X("ws"), 0.5, A_.mult, hc, A_.add)
             tt(X(sw), X("wi"), C("PCH", 0, 128), A_.min)
-            send(t + 1, "W")
-            put_own("s", t + 1, "W")
-            put_nb("y", t + 1, "O")
+            send("W%d" % (t + 1))
+            put_own("y", t + 1, "W", "W%d" % (t + 1))
             put_nb("y", t + 1, "W")
             if t == 0:
                 out_setup(2)
-                diffs(2)
             numbers(t)
             unpair(sw, ("PZ1", "PZ2"))
             act(Y("R", t), C("PZ1", 256, 320))
             act(Y("L", t), C("PZ2", 256, 320), scale=-1.0)
+            if t == 0:
+                lists(2)
+                sels(2)
+                lists2(2)
             now[0] = t + 1
             gather_slots(t + 1)
             replies(t + 1)
-            reply_parts()
         else:
             unpair("ww", ("PX0", "PX1"))
             act(C("wn", 0, 64, key="wl"), C("PX0", 256, 320), IDENT, bias=later["nt"])

@@ -23,29 +23,30 @@ def _u(n): return ("sbuf", [128, n], "uint16")
 
 
 SCRATCH = {
-    "WW": _f(WC), "WO": _b(WC), "WI": _i(384), "OI": _i(192),
+    "WW": _f(WC), "WO": _b(WC + 16), "WI": _i(384), "OI": _i(192),
     "SW0": _f(384), "SW1": _f(128), "SW2": _f(128), "SO0": _b(384), "SO1": _b(128), "SO2": _b(128), "SO3": _b(128),
-    "NW0": _f(384), "NW1": _f(128), "NW2": _f(128), "NO0": _b(384), "NO1": _b(128), "NO2": _b(128),
+    "NO0": _b(384), "DNW": ("dram", [256, 384], "float32"),
     "PI": _i(1), "pc": _i(16), "fc": _f(128), "CI": _f(176), "tmp": _f(176), "tb": _b(176), "tb2": _b(176),
     "EH": _b(256), "EL": _b(256), "MS": _b(1280), "fl": _b(960), "ni": _i(192), "OZ": _b(384), "OW": _b(384),
     "jx": _i(32), "js": _i(8), "RS": _f(384),
     "ID": _b(128), "SWB": _b(128), "NSW": _f(128), "TMPT": _b(128), "PLM": _b(136), "ED": _b(420), "EMS": _b(192), "EMB": _b(192),
-    "AD": _b(144 * 15), "UPC": _b(192), "EWP": _b(160), "EWN": _b(160), "KM": _b(320), "KZ": _b(320), "KZF": _f(320), "CM": _b(144),
+    "AD": _b(144 * 15), "UPC": _b(192), "EWP": _b(160), "EWN": _b(160), "KM": _b(320), "KZ": _b(320), "KZF": _f(320), "KZN": _f(160), "CM": _b(144),
     "DM": _b(256), "LT": _b(128), "SLM": _b(128), "ZB": _b(160), "ON": _b(192), "SG": _b(160), "NM": _b(432),
     "SEL": _u(24), "XBL": _u(32), "LU": _u(192), "LD": _u(288), "NE": _b(192),
-    "T0": _b(1024), "T1": _b(1024), "PK": _b(128), "PW": _b(64), "pz": _b(64), "LK": _u(128), "NEC": _b(64), "HHT": _b(128),
+    "T0": _b(1024), "T1": _b(1024), "PK": _b(128), "PW": _b(64), "pz": _b(64), "LK": _u(128), "NEC": _b(128), "HHT": _b(128),
     "NID": _b(128), "PLW": _b(136), "N31": _b(128), "DG": _b(384), "AR1": _b(64), "AR2": _b(64), "AQ1": _b(64), "AQ2": _b(64),
-    "XL": _f(512), "U1": _f(512), "D1": _b(512), "D2": _b(512), "IA1": _b(512), "IA2": _b(512),
-    "TL": _f(1536), "VI": _b(2048), "m1": _b(64), "m2": _b(64), "GX": _b(64), "REV": _b(64), "FI": _b(64), "FH": _b(64), "FL": _b(64),
+    "XL": _f(512), "U1": _f(512), "D1": _b(512), "D2": _b(512), "IA1": _b(512), "IA2": _b(512), "IB1": _b(512), "IB2": _b(512),
+    "TL": _f(1536), "VI": _b(2048), "m1": _b(64), "m2": _b(64), "GX": _b(64), "REV": _b(64), "FI": _b(64), "FK": _b(128), "HSW": _f(128),
+    "C16": _b(64), "NSB": _b(128),
     "CLS": _u(8), "dd": _f(128), "ee": _b(128), "zN": _b(128), "FG": _b(128), "LN": _u(64), "U2": _f(1024), "SC": _f(1024),
     "ww": _f(128), "ws": _f(128), "wi": _i(128), "wn": _f(128), "nA": _b(128), "nB": _b(128), "YR": _f(192), "YL": _f(192), "YO": _f(192),
     "PX0": ("psum", [128, 512], "float32"), "PX1": ("psum", [128, 512], "float32"), "PZ1": ("psum", [128, 512], "float32"),
     "PZ2": ("psum", [128, 512], "float32"), "PCN": ("psum", [128, 512], "float32"), "PPF": ("psum", [128, 512], "float32"),
     "PCH": ("psum", [128, 512], "float32"), "PDM": ("psum", [128, 512], "float32"),
 }
-PARTS = {"Wa": ("W", 0, 0, 192), "O0": ("O", 0, 0, 384), "Wb": ("W", 0, 192, 384),
+PARTS = {"Wa": ("W", 0, 0, 96), "O0": ("O", 0, 0, 384), "Wb": ("W", 0, 96, 384),
          "O1": ("O", 1, 0, 128), "W1": ("W", 1, 0, 128), "O2": ("O", 2, 0, 128), "W2": ("W", 2, 0, 128)}
-CALLS = {"Wa": [[0], [1, 2], [3]], "O0": [[0], [1, 2], [3]], "Wb": [[0], [1, 2], [3]]}
+CALLS = {"Wa": [([0], 0), ([1], 1), ([2, 3], 2)], "O0": [([0], 0), ([1], 1), ([2, 3], 2)], "Wb": [([0], 2), ([1, 2], 2), ([3], 2)]}
 for _n, (_x, _e, _lo, _hi) in PARTS.items():
     SCRATCH["D" + _n] = ("dram", [256, _hi - _lo], "float32" if _x == "W" else "bfloat16")
 SEMAPHORES = ["qv", "qs", "qp", "qg", "ls", "ldO", "ldW", "go1", "go2"] + [
@@ -53,8 +54,13 @@ SEMAPHORES = ["qv", "qs", "qp", "qg", "ls", "ldO", "ldW", "go1", "go2"] + [
     k + n for k in ("fA", "fB", "dA", "ls") for n in PARTS] + ["%s%d" % (k, e) for k in ("oO", "oR", "oL") for e in range(1, 3)]
 
 
-STAGE = "u0 f1 c0 k0 d1 A1 f2 d2 A2 a1 r0 c1 B1 b1 f3 m1 a2 r1 B2 n1 b2 c2 m2 r2 n2 c3 r3"
-CUT = [0, 320, 704, 1024]
+STAGE = "u0 k0 c0 r0 f1 d1 f2 d2 A1 a1 A2 a2 f3 c1 B1 B2 r1 c2 b1 b2 r2 m1 m2 c3 r3 c4 n1 r4"
+TWO = False
+GAP = 128
+OWNO = "O0"
+EARLY = 0
+CAP = 16384.0
+CUT = [0, 384, 768, 1024]
 
 
 def pl(bits):
@@ -86,9 +92,8 @@ def plan(T, topo):
                     extra.append((here[0], q, x))
     role2, of, extra2 = {}, {}, []
     for r, c in enumerate(cores):
-        near = [h for h in topo.cores_of(c) if topo.die(h) == topo.die(c) and h not in cores]
+        near = sorted([h for h in topo.cores_of(c) if h not in cores], key=lambda h: topo.die(h) != topo.die(c))
         off = [q for q, d in enumerate(cores) if topo.chip(d) != topo.chip(c)]
-        extra2 += [(r, q, x) for q in off[len(near):] for x in "WO"]
         for q, h in zip(off, near):
             role2[h] = {"ranks": [r], "A": q, "x": "WO", "feed": cores[q], "fwd": []}
             of[(r, q)] = h
@@ -102,7 +107,11 @@ def plan(T, topo):
 
 
 def calls(info, name, cores):
-    return CALLS.get(name, [[0, 1, 2, 3]])
+    return CALLS.get(name, [([0, 1, 2, 3], 2)])
+
+
+def share(eng, part):
+    return eng if part == 2 else eng[part * len(eng) // 2:(part + 1) * len(eng) // 2]
 
 
 def helper(g, core, T, topo, cores, roles):
@@ -127,17 +136,19 @@ def helper(g, core, T, topo, cores, roles):
             ls += len(en)
         if e and x == "O":
             g.wait_ge(T.sem["go%d" % e], len(rcs))
-        for call in calls(info, name, cores):
+        for call, part in calls(info, name, cores):
             if direct and call[-1] and not call[0] > 1:
                 g.wait_ge(T.sem["dA" + name], 16)
-            w = len(eng) // len(call)
+            use = share(eng, part)
+            w = len(use) // len(call)
             trs = []
             for j, k in enumerate(call):
                 c0 = k * G1 + info["A"] * R1 + (e - 1) * B1 * (e > 0)
-                trs.append(RemoteDMATransfer(dst_ids=[dst(topo, c) for c in rcs], dma_engine_mask=pl(eng[j * w:(j + 1) * w]),
-                                             remote_sem=T.sem["arr%s%d" % (x, e)],
-                                             srcs=[buf[32 * k:32 * k + 128, :]], dsts=[T["W" + x][:, c0 + lo:c0 + hi]] * len(rcs)))
-                ls += w
+                for i, c in enumerate(rcs):
+                    m = use[j * w:(j + 1) * w][i::len(rcs)]
+                    trs.append(RemoteDMATransfer(dst_ids=[dst(topo, c)], dma_engine_mask=pl(m), remote_sem=T.sem["arr%s%d" % (x, e)],
+                                                 srcs=[buf[32 * k:32 * k + 128, :]], dsts=[T["W" + x][:, c0 + lo:c0 + hi]]))
+                    ls += len(m)
             g.remote_dma_fused(trs, local_sem=T.sem.ls)
     if ls:
         g.wait_ge(T.sem.ls, ls)
@@ -155,7 +166,7 @@ def rank_program(g, core, T, topo):
     for name, (x, e, lo, hi) in PARTS.items():
         for h, info in roles[e].items():
             if rank in info["ranks"] and x in info["x"]:
-                arr_n[x, e] = arr_n.get((x, e), 0) + len(topo.engines(h, core)) * len(calls(info, name, cores))
+                arr_n[x, e] = arr_n.get((x, e), 0) + sum(len(share(topo.engines(h, core), p)) for _, p in calls(info, name, cores)) // len(info["ranks"])
     Q = {"v": g.vector, "s": g.scalar, "p": g.tensor, "g": g, "y": g.sync}
     QS = {"v": "qv", "s": "qs", "p": "qp", "g": "qg"}
     cnt, known, lastw, readers, lastx, alias = {}, {q: {} for q in Q}, {}, {}, {}, {}
@@ -318,44 +329,58 @@ def rank_program(g, core, T, topo):
 
     def send(part):
         x, e, lo, hi = PARTS[part]
-        name, nb = "S%s%d" % (x, e), T["N%s%d" % (x, e)][:, lo:hi]
+        name = "S%s%d" % (x, e)
         deps("g", [name], [], ())
         offs = [(h, T["D" + part][0:128, :]) for h, info in roles[e].items() if info["feed"] == core and x in info["x"]]
-        offs += [(cores[r], nb) for r, q, y in extras[e] if q == rank and y == x]
+        offs += [(cores[r], T["N%s%d" % (x, e)][:]) for r, q, y in extras[e] if q == rank and y == x]
         en = topo.engines(core, offs[0][0])
         trs = [RemoteDMATransfer(dst_ids=[dst(topo, h) for h, _ in offs], dma_engine_mask=pl(en), remote_sem=T.sem["fA" + part],
                                  srcs=[T[name][:, lo:hi]], dsts=[d for _, d in offs])]
         cnt["ls" + part] = len(en)
+        if e:
+            trs += to_near(part, en, part)
+        g.remote_dma_fused(trs, local_sem=T.sem["ls" + part])
+        if part in ("O0", "Wb") and near:
+            g.remote_dma_fused(to_near(part, en, "Wa"), local_sem=T.sem.lsWa)
+
+    def to_near(part, en, sem):
+        x, e, lo, hi = PARTS[part]
+        trs = []
         for q in near:
             e2 = [y for y in topo.engines(core, cores[q]) if y not in en]
-            trs.append(RemoteDMATransfer(dst_ids=[dst(topo, cores[q])], dma_engine_mask=pl(e2), remote_sem=T.sem["fB" + part],
-                                         srcs=[T[name][:, lo:hi]], dsts=[nb]))
-            cnt["ls" + part] += len(e2)
-        g.remote_dma_fused(trs, local_sem=T.sem["ls" + part])
+            buf = T["DNW" if part == "Wb" else "D" + part]
+            trs.append(RemoteDMATransfer(dst_ids=[dst(topo, cores[q])] * 2, dma_engine_mask=pl(e2), remote_sem=T.sem["fB" + part],
+                                         srcs=[T["S%s%d" % (x, e)][:]], dsts=[buf[0:128, :], buf[128:256, :]]))
+            cnt["ls" + sem] += len(e2)
+        return trs
 
-    def put(qu, e, x, sem, name, src, rd):
+    def put(qu, e, x, sem, name, src, rd, some=slice(None)):
         nn, W = PN[e], T["W" + x]
         c0 = src * R1 + (e - 1) * B1 * (e > 0)
-        pairs = [(W[:, c0:c0 + nn], T[name][:])]
+        pairs = [(W[:, c0:c0 + nn], T[name][0:128, :])]
         for k in range(1, 4):
             c = c0 + k * G1
-            pairs.append((W[0:128 - 32 * k, c:c + nn], T[name][32 * k:128, :]))
-            pairs.append((W[128 - 32 * k:128, c:c + nn], T[name][0:32 * k, :]))
+            if name[0] == "D":
+                pairs.append((W[:, c:c + nn], T[name][32 * k:32 * k + 128, :]))
+            else:
+                pairs.append((W[0:128 - 32 * k, c:c + nn], T[name][32 * k:128, :]))
+                pairs.append((W[128 - 32 * k:128, c:c + nn], T[name][0:32 * k, :]))
         deps(qu, [], ["W" + x], ())
-        dma(qu, sem + x + str(e), pairs, rd=rd, wr=[sem + x])
+        dma(qu, sem + x + str(e), pairs[some], rd=rd, wr=[sem + x] if some.stop is None else [])
 
-    def put_own(qu, e, x, after=None):
+    def put_own(qu, e, x, after=None, some=slice(None)):
         if after:
             Q[qu].wait_ge(T.sem["ls" + after], cnt["ls" + after])
-        put(qu, e, x, "own", "S%s%d" % (x, e), rank, ["S%s%d" % (x, e)])
+        put(qu, e, x, "own", "S%s%d" % (x, e), rank, ["S%s%d" % (x, e)], some)
 
     def put_nb(qu, e, x):
-        for q in near + [q for r, q, y in extras[e] if r == rank and y == x]:
+        part = [p for p, v in PARTS.items() if v[:2] == (x, e)][-1]
+        for q in near:
             h = [h for h, info in roles[e].items() if info["feed"] == cores[q]][0]
-            en = topo.engines(cores[q], core)
-            for part in [p for p, v in PARTS.items() if v[:2] == (x, e)]:
-                Q[qu].wait_ge(T.sem[("fB" if q in near else "fA") + part],
-                              len([y for y in en if y not in topo.engines(cores[q], h)] if q in near else en))
+            Q[qu].wait_ge(T.sem["fB" + part], 2 * len([y for y in topo.engines(cores[q], core) if y not in topo.engines(cores[q], h)]))
+            put(qu, e, x, "nbd", "DNW" if part == "Wb" else "D" + part, q, [])
+        for q in [q for r, q, y in extras[e] if r == rank and y == x]:
+            Q[qu].wait_ge(T.sem["fA" + part], len(topo.engines(cores[q], core)))
             put(qu, e, x, "nbd", "N%s%d" % (x, e), q, [])
 
     send("Wa")
@@ -380,7 +405,7 @@ def rank_program(g, core, T, topo):
     both("SO0")
     send("O0")
     send("Wb")
-    put_own("y", 0, "O", "Wb")
+    put_own("y", 0, "O", OWNO)
     put_nb("y", 0, "O")
     put_nb("y", 0, "W")
     def fill(out, val):
@@ -406,9 +431,10 @@ def rank_program(g, core, T, topo):
         pick(C("KZ", 160 * y, 160 * y + 160, key="KZ%d" % y), C("ZB", 0, 160), [(32, 5), (-1000, 2), (1, 16)], 1000 + 16 * y, 1.0)
     pick(X("SWB"), C("ZB", 0, 128), [(32, 4), (-16, 2), (1, 16)], 16, 1.0)
     band(X("EWP"), X("SG"), [(32, 5), (1000, 32)], -32, 32)
-    band(X("LT"), C("ON", 0, 128), [(8, 16), (0, 8)], 0, 8)
+    fill(X("LT"), int(CAP))
+    band(X("LT"), X("LT"), [(8, 16), (0, 8)], 0, 8)
     emit("g", lambda e: e.affine_select(T.LT[:], T.LT[:], [[1, 128]], A_.is_gt, 0.0, 0, -1), [X("LT")], X("LT"))
-    pick(X("LT"), X("LT"), [(1, 128)], 0, -0.5)
+    pick(X("LT"), X("LT"), [(1, 128)], 0, -CAP)
     for y in range(2):
         pick(C("DM", 128 * y, 128 * y + 128, key="DM%d" % y), C("ZB", 0, 128), [(16, 8), (0, 2), (1, 8)], 8 * y, 1.0)
     band(X("CM"), C("ON", 0, 144), [(16, 9), (1000, 8), (8, 2)], -16, 8)
@@ -477,18 +503,30 @@ def rank_program(g, core, T, topo):
         ts(C("SEL", 8 * t, 8 * t + 8, key="SEL%d" % t), X("js"), z, A_.add, lin((q32, 1), t, q="v") if t else q32, A_.add)
 
     sels(0)
-    act(X("N31"), X("ID"), scale=-31.0)
+    if TWO:
+        act(X("EMB"), X("EMS"), scale=-2.0 ** 30)
+    else:
+        act(X("N31"), X("ID"), scale=-31.0)
     made, dc = {}, {}
 
     def diffs(t):
         ds = sorted(set(abs((s ^ k) - s) for s in sets[t][3] for k in KS[t]) - set(made))
+        if TWO:
+            ds = sorted(set((s ^ k) - s for s in range(8) for k in KS[t]) - set(made))
         for i in range(0, len(ds), 3):
             bank, o = ("PZ1", "PDM")[i // 3], 144 * len(made)
             for j, d in enumerate(ds[i:i + 3]):
                 made[d] = (144 * len(made), "AD%d" % o)
                 mm(C(bank, 144 * j, 144 * j + 144), X("ID"), C("EMS", 16, 160), True, False)
-                mm(C(bank, 144 * j, 144 * j + 144), X("ID"), C("EMS", 16 - d, 160 - d), False, True)
+                mm(C(bank, 144 * j, 144 * j + 144), X("ID"), C("EMB" if TWO else "EMS", 16 - d, 160 - d), False, True)
             act(C("AD", o, 144 * len(made), key="AD%d" % o), C(bank, 0, 144 * len(made) - o))
+        if TWO:
+            for z, k in enumerate(KS[t]):
+                hb = 4 if k >= 4 else 2 if k >= 2 else 1
+                if hb not in dc:
+                    dc[hb] = lin((F[hb], 0.5), -0.25, q="s" if t else "v")
+                dc[t, z + 1] = dc[hb]
+            return
         f = F[sets[t][0]]
         q = "s" if t else "v"
         act(C("DG", 128 * t, 128 * t + 128, key="DG%d" % t), X("ID"), scale=lin((f, 33), -1, q=q))
@@ -504,37 +542,41 @@ def rank_program(g, core, T, topo):
         act(X("PX1"), X("XL"), IDENT, bias=dR)
 
     own_walls(0)
-    nEC = lin((ECw, -1), 0, q="v")
-    EHc = lin((ECw, 1), nH, q="v")
     temp = lin((p15, 1024), 0, q="v")
-    hc = lin((p15, -512), (sgn, -0.25), 0, q="v")
+    hc = lin((sgn, -0.25), 0, q="v")
+    ts(C("NEC", 0, 64, key="NECa"), C("CI", 0, 64), 0.0, A_.mult, lin((nH, 1), CAP, q="v"), A_.add)
+    ts(C("NEC", 64, 128, key="NECb"), C("CI", 0, 64), 0.0, A_.mult, CAP, A_.add)
+    both("NEC")
     act(X("TMPT"), C("CI", 0, 128), IDENT, scale=0.0, bias=temp)
-    act(X("NEC"), C("CI", 0, 64), IDENT, scale=0.0, bias=nEC)
+    act(("WOf", T.WO[:, WC:WC + 8]), C("CI", 0, 8), IDENT, scale=0.0, bias=eo)
     act(X("HHT"), C("CI", 0, 128), IDENT, scale=0.0, bias=Hh)
     act(X("NID"), X("ID"), scale=-1.0)
     act(X("PLW"), X("PLM"), scale=float(WC))
     act(X("EWN"), X("EWP"), scale=-1.0)
+    act(X("C16"), C("CI", 0, 64), IDENT, scale=0.0, bias=-15.875)
+    act(X("NSB"), X("SWB"), scale=-1.0)
     act(X("NSW"), X("SWB"), scale=-1.0)
-    lists(1)
-    sels(1)
-    lists2(1)
     later = {}
 
     def out_setup(part):
         if part == 0:
             later["tN"] = lin((pb, 0.5), tL, q="v")
             later["w"] = [lin((ph, (wl - wh) / 8), wh, q="v") for wh, wl in ((0.5, 192), (1344, -384), (-8832, 1))]
-            later["tN"] = col(later["tN"], 24.0, A_.add)
+            later["tN"] = lin((later["tN"], 1), 24, q="v")
             later["sA"] = lin((ph, (0.5 - 1 / 384) / 8), 1 / 384, q="v")
             later["bA"] = lin((ph, (1 / 3 - 0.25) / 8), 129 - 1 / 3, q="v")
-        elif part == 1:
             later["sB"] = lin((ph, (0.5 - 1 / 2304) / 8), 1 / 2304, q="v")
             later["bB"] = lin((ph, (8.5 / 18 - 0.25) / 8), 129 - 8.5 / 18, q="v")
-            later["nt"] = lin((p15, -1024), 0, q="v")
-            later["hf"] = lin((p15, 512), -0.25, q="v")
         else:
             for j in range(3):
                 ts(C("NM", 144 * j, 144 * j + 144, key="NM%d" % j), C("CI", 0, 144), later["tN"], A_.is_equal, later["w"][j], A_.mult)
+
+    lists(1)
+    out_setup(0)
+    sels(1)
+    lists2(1)
+    tt(X("HSW"), X("ID"), X("SWB"), A_.subtract)
+    out_setup(2)
 
     def win(x, L, lo, hi):
         return ("W" + x, T["W" + x][:].indirect(T[L][:, lo:hi]))
@@ -542,7 +584,7 @@ def rank_program(g, core, T, topo):
     now = [0]
 
     def wm(x, L):
-        return [(L, 0), (L + str(now[0]), 0), ("own" + x, 0), ("nbd" + x, 0), ("W%se" % x, 0)]
+        return [(L, 0), (L + str(now[0]), 0), ("own" + x, 0), ("nbd" + x, 0), ("W%se" % x, 0), ("W%sf" % x, 0)]
 
     def arrived(x, t):
         for q in "vs":
@@ -558,22 +600,20 @@ def rank_program(g, core, T, topo):
             emit("v", lambda e, c=c: e.transpose(T.T1[:, c], T.T0[:, c]), [("T0" + h, 0)], ("T1" + h, 0))
         cp(X("PK"), ("T1a", T.T1[:].indirect(T.SEL[:, 8 * t:8 * t + 8])), more=[("SEL%d" % t, 0), ("T1b", 0)])
         ts(X("pz"), C("PK", 0, 64), H, A_.is_lt, float(WC), A_.mult)
-        tt(X("PW"), X("pz"), C("PK", 0, 64), A_.add)
-        for s2 in range(2):
-            o, l = C("PPF", 64 * s2, 64 * s2 + 64), C("KM", 160 * s2 + 16, 160 * s2 + 144, key="KM%d" % s2)
-            mm(o, l, C("PK", 64, 128), True, False)
-            mm(o, l, X("PW"), False, True)
+        mm(C("PPF", 0, 128), X("ID"), C("ZB", 0, 128), True, False)
+        for r in (C("PK", 0, 64), C("PK", 64, 128), X("pz")):
+            for s2 in range(2):
+                mm(C("PPF", 64 * s2, 64 * s2 + 64), C("KM", 160 * s2 + 16, 160 * s2 + 144, key="KM%d" % s2), r, False, r[0] == "pz" and s2 == 1)
         ts(X("LK"), C("PPF", 0, 128), nH, A_.add)
 
     def reply_parts():
-        mm(C("PPF", 128, 192), X("ID"), X("NEC"), True, False)
-        for hl in range(2):
+        mm(C("PPF", 128, 256), X("ID"), X("NEC"), True, False)
+        for M, w, hl in (("PK", 0, 0), ("pz", 0, 0), ("PK", 64, 1)):
             for y in range(2):
                 for b in range(2):
                     o = 160 * y + 16 - 16 * b
                     mm(C("PPF", 128 + 64 * hl + y, 192 + 64 * hl, 2), C("KZ", o, o + 128, key="KZ%d" % y),
-                       C("PK", 96 - 32 * b, 128 - 32 * b) if hl else C("PW", 32 - 32 * b, 64 - 32 * b),
-                       hl == 1 and b == 0, b == 1 and hl + y > 0)
+                       C(M, w + 32 - 32 * b, w + 64 - 32 * b), False, False)
 
     def gather_one(t):
         act(X("U1"), win("W", "LD", 96 * t, 96 * t + 32), more=wm("W", "LD"))
@@ -600,22 +640,44 @@ def rank_program(g, core, T, topo):
         mm(C("PZ%d" % z, 256, 320), X("N31"), X("AR%d" % z), True, False)
         mm(C("PZ%d" % z, 256, 320), C("DG", 128 * t, 128 * t + 128, key="DG%d" % t), X("AQ%d" % z), False, True)
 
+    def signs2(z, x, q):
+        name, sc = "I%s%d" % (x, z), 1.0 if x == "A" else -1.0
+        if q == "v":
+            ts(X(name), X("D%d" % z), sc, A_.mult, 0.0, A_.max)
+        else:
+            act(X(name), X("D%d" % z), RELU, scale=sc)
+
+    def count2(t, z, x, first):
+        k = KS[t][z - 1]
+        for y in range(2):
+            for i, s in enumerate(sets[t][3]):
+                a, b = (s ^ k, s) if x else (s, s ^ k)
+                w = made[b - a][0] + 16 - 8 * y - a
+                mm(C("PZ%d" % z, 256, 320), C("AD", w, w + 128, key=made[b - a][1]), C(("IA%d", "IB%d")[x] % z, 4 * y + i, None, 8),
+                   first and y + i == 0, not first and y + i == 4)
+
     def fetch(j):
-        act(C("TL", 512 * j - 512, 512 * j, key="TL%d" % j), win("W", "LK", 32 * j, 32 * j + 32), more=wm("W", "LK"))
+        w = GAP * (j == 2)
+        act(C("TL", 512 * j - 512 + w, 512 * j, key="TL%d" % j), win("W", "LK", 32 * j + w // 16, 32 * j + 32), more=wm("W", "LK"))
 
     def compare(j):
-        o = C("VI", 512 * j, 512 * j + 512, key="VI%d" % j)
         if j == 0:
-            tt(o, win("W", "LK", 0, 32), X("XL"), A_.is_gt, more=wm("W", "LK"))
+            tt(C("VI", 0, 512, key="VI0"), win("W", "LK", 0, 32), X("XL"), A_.is_gt, more=wm("W", "LK"))
+            if GAP:
+                tt(C("VI", 1024, 1024 + GAP, key="VI5"), win("W", "LK", 64, 64 + GAP // 16), C("XL", 0, GAP), A_.is_gt, more=wm("W", "LK"))
+        elif j < 3:
+            w = GAP * (j == 2)
+            tt(C("VI", 512 * j + w, 512 * j + 512, key="VI%d" % j), C("TL", 512 * j - 512 + w, 512 * j, key="TL%d" % j), C("PX%d" % (j & 1), w, 512), A_.is_gt)
         else:
-            tt(o, C("TL", 512 * j - 512, 512 * j, key="TL%d" % j), X("PX%d" % (j & 1)), A_.is_gt)
+            tt(C("VI", 1533 + j, 2048, 2, key="VI%d" % j), C("TL", 1021 + j, 1536, 2, key="TL3"), C("PX1", j - 3, 512, 2), A_.is_gt)
 
     def count_rep(j):
+        p = min(j, 3)
         for y in range(2):
-            for s in range(4):
-                w = 32 - (16 * (1 - (j & 1)) + 8 * y + 4 * (j >> 1) + s)
-                mm(C("PCN", 0, 64), C(("EWP", "EWN")[j & 1], w, w + 128), C("VI", 512 * j + 4 * y + s, 512 * j + 512, 8, key="VI%d" % j),
-                   False, j == 3 and y == 1 and s == 3)
+            for s in range(4) if j < 3 else range(j - 3, 4, 2):
+                w = 32 - (16 * (1 - (p & 1)) + 8 * y + 4 * (p >> 1) + s)
+                mm(C("PCN", 0, 64), C(("EWN", "EWP")[p & 1], w, w + 128), C("VI", 512 * p + 4 * y + s, 512 * p + 512, 8, key="VI%d" % j),
+                   False, j == 4 and y == 1 and s == 3, more=[("VI5", 0)] * (j == 2))
 
     def flags(z):
         act(X("m%d" % z), C("PZ%d" % z, 256, 320), RELU, bias=dc[now[0], z])
@@ -653,7 +715,8 @@ def rank_program(g, core, T, topo):
             gather_slots(t)
             replies(t)
         arrived("W", t)
-        mm(C("PCN", 0, 64), X("SWB"), ne, True, False)
+        mm(C("PCN", 0, 64), X("ID"), X("C16"), True, False)
+        mm(C("PCN", 0, 64), X("NSB"), ne, False, False)
         for step in STAGE.split():
             z = int(step[1])
             if step[0] == "u":
@@ -666,6 +729,10 @@ def rank_program(g, core, T, topo):
                 fetch(z)
             elif step[0] == "d":
                 diff(t, z)
+            elif TWO and step[0] in "AB":
+                signs2(z, step[0], step[2])
+            elif TWO and step[0] in "ab":
+                count2(t, z, "ab".index(step[0]), STAGE.index("a%d" % z) < STAGE.index("b%d" % z) if step[0] == "a" else STAGE.index("b%d" % z) < STAGE.index("a%d" % z))
             elif step[0] == "A":
                 signs(z)
             elif step[0] == "a":
@@ -679,7 +746,7 @@ def rank_program(g, core, T, topo):
             elif step[0] == "m":
                 flags(z)
             else:
-                mm(C("PCN", 0, 64), X("ID"), X("m%d" % z), False, False)
+                mm(C("PCN", 0, 64), X("NID"), X("m%d" % z), False, False)
         o = C("PZ1", 64, 128)
         mm(o, X("SWB"), ne, True, False)
         mm(o, X("ID"), X("m1"), False, False)
@@ -687,27 +754,24 @@ def rank_program(g, core, T, topo):
         act(X("GX"), o, SIGN)
         if t < 2:
             own_walls(t + 1)
-        ts(X("REV"), C("PCN", 0, 64), -15.9, A_.is_lt)
-        mm(C("PPF", 0, 64), X("LT"), X("REV"), True, True)
-        mm(C("PDM", 0, 128), X("ID"), C("ZB", 0, 128), True, False)
-        for y in range(2):
-            mm(C("PDM", y, 128, 2), C("DM", 128 * y, 128 * y + 128, key="DM%d" % y), X("GX"), False, False)
-        ts(X("FI"), C("PPF", 0, 64), 0.0, A_.is_lt)
-        tt(X("FH"), X("FI"), C("PPF", 128, 192), A_.mult)
-        tt(X("FL"), X("FI"), C("PPF", 192, 256), A_.mult)
-        for x in ("FH", "FL"):
+        tt(X("REV"), X("m2"), C("PCN", 0, 64), A_.is_lt)
+        for x in range(2):
+            mm(C("PPF", 128 + 64 * x, 192 + 64 * x), X("LT"), X("REV"), False, x == 1)
+        ts(X("FK"), C("PPF", 128, 256), CAP, A_.min)
+        ts(X("FI"), C("PPF", 128, 192), CAP, A_.is_lt)
+        for x in range(2):
             for c in range(8):
-                mm(C("PCH", 0, 8), C("CM", 16 - 2 * c, 144 - 2 * c), C(x, c, None, 8), x == "FH" and c == 0, x == "FL" and c == 7)
-        for y in range(2):
-            mm(C("PDM", y, 128, 2), C("DM", 128 * y, 128 * y + 128, key="DM%d" % y), X("FI"), False, y == 1)
+                mm(C("PCH", 0, 8), C("CM", 16 - 2 * c, 144 - 2 * c), C("FK", 64 * x + c, 64 * x + 64, 8), x + c == 0, x + c == 8)
+        mm(C("PDM", 0, 128), X("ID"), C("ZB", 0, 128), True, False)
+        for r in ("GX", "FI"):
+            for y in range(2):
+                mm(C("PDM", y, 128, 2), C("DM", 128 * y, 128 * y + 128, key="DM%d" % y), X(r), False, r == "FI" and y == 1)
         mm(C("PZ1", 128, 256), X("ID"), X("HHT"), True, False)
         mm(C("PZ1", 128, 256), X("NID"), oc, False, True)
         mm(C("PCN", 128, 256), X("ID"), oc, True, True)
         for y in range(2):
             mm(C("PPF", 0, 64), C("PLM", 8 - 8 * y, 136 - 8 * y), C("SO0", 128 * t + y, 128 * t + 128, 2), y == 0, False)
-        if t == 0:
-            out_setup(0)
-        ts(X("CLS"), C("PCH", 0, 8), EHc, A_.add)
+        ts(X("CLS"), C("PCH", 0, 8), -14 * CAP, A_.add, float(WC), A_.min)
         tt(X("dd"), win("O", "CLS", 0, 8), oc, A_.subtract, more=wm("O", "CLS"))
         tt(X("ee"), X("dd"), C("PDM", 0, 128), A_.mult)
         so = "SO%d" % (t + 1)
@@ -736,9 +800,13 @@ def rank_program(g, core, T, topo):
                                                   remote_sem=T.sem["go%d" % (t + 1)]) for j, h in enumerate(mine)], local_sem=T.sem.ls)
             nls[0] += len(mine)
             diffs(t + 1)
+            if t == 1:
+                act(X("KZN"), C("KZ", 160, 320, key="KZ1"), scale=-1.0)
             if t == 0:
                 act(X("KZF"), ("KZ0", T.KZ[:]), more=[("KZ1", 0)])
         else:
+            mm(C("PX0", 256, 320), X("NID"), C("TMPT", 0, 64), True, False)
+            mm(C("PX1", 256, 320), X("ID"), C("TMPT", 0, 64), True, False)
             numbers(t)
         for lo, hi in cuts:
             emit("v", lambda e, c=slice(lo, hi), w=hi - lo: e.tensor_tensor_scan(T.SC[:, c], T.RS[:, 0:w], T.U2[:, c], 0.0, A_.add, A_.max),
@@ -746,17 +814,16 @@ def rank_program(g, core, T, topo):
         tt(X("ww"), C("SC", 7, None, 8, key="SC0"), C("PZ2", 0, 128), A_.max, more=[("SC%d" % lo, 0) for lo, hi in cuts])
         if t < 2:
             sw = "SW%d" % (t + 1)
+            mm(C("PPF", 0, 128), X("HSW"), X("ww"), True, True)
             mm(C("PCH", 0, 128), X("NSW"), X("ww"), False, True)
-            if t == 0:
-                out_setup(1)
-            tt(X("ws"), X("ww"), C("PCH", 0, 128), A_.add)
-            ts(X("wi"), X("ws"), 0.5, A_.mult, hc, A_.add)
+            ts(X("wi"), C("PPF", 0, 128), 0.5, A_.mult, hc, A_.add)
             tt(X(sw), X("wi"), C("PCH", 0, 128), A_.min)
             send("W%d" % (t + 1))
-            put_own("y", t + 1, "W", "W%d" % (t + 1))
+            if EARLY:
+                put_own("y", t + 1, "W", None, slice(0, EARLY))
+            if EARLY < 4:
+                put_own("y", t + 1, "W", "W%d" % (t + 1), slice(EARLY, 4))
             put_nb("y", t + 1, "W")
-            if t == 0:
-                out_setup(2)
             numbers(t)
             unpair(sw, ("PZ1", "PZ2"))
             act(Y("R", t), C("PZ1", 256, 320))
@@ -767,15 +834,17 @@ def rank_program(g, core, T, topo):
                 lists2(2)
             now[0] = t + 1
             gather_slots(t + 1)
+            put_own("s", t + 1, "W", "W%d" % (t + 1), slice(4, None))
             replies(t + 1)
         else:
-            unpair("ww", ("PX0", "PX1"))
-            act(C("wn", 0, 64, key="wl"), C("PX0", 256, 320), IDENT, bias=later["nt"])
-            tt(C("ws", 0, 64), C("wn", 0, 64, key="wl"), C("PX1", 256, 320), A_.subtract)
-            act(C("wn", 64, 128, key="wr"), C("PX1", 256, 320), IDENT, scale=-1.0, bias=temp)
-            ts(C("wi", 0, 64), C("ws", 0, 64), 0.5, A_.mult, later["hf"], A_.add)
-            tt(Y("L", t), C("wn", 0, 64, key="wl"), C("wi", 0, 64), A_.max)
-            tt(Y("R", t), C("wn", 64, 128, key="wr"), C("wi", 0, 64), A_.min)
+            for bank, parts in (("PPF", ((0, "KZF"), (1, "KZN"))), ("PX0", ((0, "KZF"),)), ("PX1", ((1, "KZN"),))):
+                for b, M in parts:
+                    for f in range(2):
+                        o = 160 * b * (M == "KZF") + 16 - 16 * f
+                        mm(C(bank, 256, 320), C(M, o, o + 128), C("ww", f, None, 2), bank == "PPF" and b + f == 0, f == 1 and b == parts[-1][0])
+            ts(C("wi", 0, 64), C("PPF", 256, 320), 0.5, A_.mult, -0.25, A_.add)
+            tt(Y("L", t), C("wi", 0, 64), C("PX0", 256, 320), A_.max)
+            tt(Y("R", t), C("wi", 0, 64), C("PX1", 256, 320), A_.min)
         if t:
             store("y", "L", t)
             store("s" if t == 2 else "y", "R", t)

import numpy as np
from concourse.bass import DstId, RemoteDMATransfer
from concourse.mybir import dt, AluOpType, AxisListType, ActivationFunctionType

A_ = AluOpType
COPY = ActivationFunctionType.Copy
IDENT = ActivationFunctionType.Identity
RELU = ActivationFunctionType.Relu
SIGN = ActivationFunctionType.Sign
ABS = ActivationFunctionType.Abs
G1, R1, B1 = 2304, 384, 128
WC = 4 * G1
EC = 5 * R1
BIG = 8388608.0
PN = [384, 128, 128]
KS = [(1, 4), (2, 5), (3, 6)]


def _f(n): return ("sbuf", [128, n], "float32")
def _i(n): return ("sbuf", [128, n], "int32")
def _b(n): return ("sbuf", [128, n], "bfloat16")
def _u(n): return ("sbuf", [128, n], "uint16")


SCRATCH = {
    "WW": _f(WC), "WO": _b(WC + 16), "WI": _i(384), "OI": _i(192),
    "SW0": _f(384), "SW1": _f(128), "SW2": _f(128), "SO0": _b(384), "SO1": _b(128), "SO2": _b(128), "SO3": _b(128),
    "NO0": _b(384), "DNW": ("dram", [256, 384], "float32"),
    "PI": _i(1), "pc": _i(16), "fc": _f(128), "CI": _f(176), "tmp": _f(176), "tb": _b(176), "tb2": _b(176),
    "EH": _b(256), "EL": _b(256), "MS": _b(1280), "fl": _b(960), "ni": _i(192), "OZ": _b(384), "OW": _b(384),
    "jx": _i(32), "js": _i(8), "RS": _f(384),
    "ID": _b(128), "SWB": _b(128), "NSW": _f(128), "TMPT": _b(128), "PLM": _b(136), "ED": _b(420), "EMS": _b(192), "EMB": _b(192),
    "AD": _b(144 * 15), "UPC": _b(192), "EWP": _b(160), "EWN": _b(160), "KM": _b(320), "KZ": _b(320), "KZF": _f(320), "KZN": _f(160), "CM": _b(144),
    "DM": _b(256), "LT": _b(128), "SLM": _b(128), "ZB": _b(160), "ON": _b(192), "SG": _b(160), "NM": _b(432),
    "SEL": _u(24), "XBL": _u(32), "LU": _u(192), "LD": _u(288), "NE": _b(192),
    "T0": _b(1024), "T1": _b(1024), "PK": _b(128), "PW": _b(64), "pz": _b(64), "LK": _u(128), "NEC": _b(128), "HHT": _b(128),
    "NID": _b(128), "PLW": _b(136), "N31": _b(128), "DG": _b(384), "AR1": _b(64), "AR2": _b(64), "AQ1": _b(64), "AQ2": _b(64),
    "XL": _f(512), "U1": _f(512), "D1": _b(512), "D2": _b(512), "IA1": _b(512), "IA2": _b(512), "IB1": _b(512), "IB2": _b(512),
    "TL": _f(1536), "VI": _b(2048), "m1": _b(64), "m2": _b(64), "GX": _b(64), "REV": _b(64), "FI": _b(64), "FK": _b(128), "HSW": _f(128),
    "C16": _b(64), "NSB": _b(128),
    "CLS": _u(8), "dd": _f(128), "ee": _b(128), "zN": _b(128), "FG": _b(128), "LN": _u(64), "U2": _f(1024), "SC": _f(1024),
    "ww": _f(128), "ws": _f(128), "wi": _i(128), "wn": _f(128), "nA": _b(128), "nB": _b(128), "YR": _f(192), "YL": _f(192), "YO": _f(192),
    "PX0": ("psum", [128, 512], "float32"), "PX1": ("psum", [128, 512], "float32"), "PZ1": ("psum", [128, 512], "float32"),
    "PZ2": ("psum", [128, 512], "float32"), "PCN": ("psum", [128, 512], "float32"), "PPF": ("psum", [128, 512], "float32"),
    "PCH": ("psum", [128, 512], "float32"), "PDM": ("psum", [128, 512], "float32"),
}
PARTS = {"Wa": ("W", 0, 0, 96), "O0": ("O", 0, 0, 384), "Wb": ("W", 0, 96, 384),
         "O1": ("O", 1, 0, 128), "W1": ("W", 1, 0, 128), "O2": ("O", 2, 0, 128), "W2": ("W", 2, 0, 128)}
CALLS = {"Wa": [([0], 0), ([1], 1), ([2, 3], 2)], "O0": [([0], 0), ([1], 1), ([2, 3], 2)], "Wb": [([0], 2), ([1, 2], 2), ([3], 2)]}
for _n, (_x, _e, _lo, _hi) in PARTS.items():
    SCRATCH["D" + _n] = ("dram", [256, _hi - _lo], "float32" if _x == "W" else "bfloat16")
SEMAPHORES = ["qv", "qs", "qp", "qg", "ls", "ldO", "ldW", "go1", "go2"] + [
    "%s%s%d" % (k, x, e) for k in ("arr", "own", "nbd") for x in "WO" for e in range(3)] + [
    k + n for k in ("fA", "fB", "dA", "ls") for n in PARTS] + ["%s%d" % (k, e) for k in ("oO", "oR", "oL") for e in range(1, 3)]


STAGE = "u0 k0 c0 r0 f1 d1 f2 d2 A1 a1 A2 a2 f3 c1 B1 B2 r1 c2 b1 b2 r2 m1 m2 c3 r3 c4 n1 r4"
TWO = False
GAP = 128
OWNO = "O0"
EARLY = 0
CAP = 16384.0
CUT = [0, 384, 768, 1024]


def pl(bits):
    return sum(1 << b for b in bits)


def dst(topo, c):
    rid, pid, _ = topo.addr(c)
    return DstId(rid=rid, pnc=pid)


def par(x):
    return bin(x).count("1") & 1


def plan(T, topo):
    cores = list(T.cores)
    role, extra = {}, []
    for ch in sorted(set(topo.chip(c) for c in cores)):
        here = [r for r, c in enumerate(cores) if topo.chip(c) == ch]
        free = [h for h in topo.cores_of(cores[here[0]]) if h not in cores]
        for x in "WO":
            for q in [q for q in range(len(cores)) if q not in here]:
                like = cores[here[0]] if len(here) == 1 else cores[q]
                free.sort(key=lambda h: topo.die(h) != topo.die(like))
                if free:
                    role[free.pop(0)] = {"ranks": here, "A": q, "x": x, "feed": cores[q], "fwd": []}
                else:
                    extra.append((here[0], q, x))
    role2, of, extra2 = {}, {}, []
    for r, c in enumerate(cores):
        near = sorted([h for h in topo.cores_of(c) if h not in cores], key=lambda h: topo.die(h) != topo.die(c))
        off = [q for q, d in enumerate(cores) if topo.chip(d) != topo.chip(c)]
        for q, h in zip(off, near):
            role2[h] = {"ranks": [r], "A": q, "x": "WO", "feed": cores[q], "fwd": []}
            of[(r, q)] = h
    for (r, q), h in of.items():
        if topo.die(cores[r]) != topo.die(cores[q]):
            for r2 in range(len(cores)):
                if r2 != r and topo.chip(cores[r2]) == topo.chip(cores[r]) and topo.die(cores[r2]) == topo.die(cores[q]):
                    role2[h]["feed"] = of[(r2, q)]
                    role2[of[(r2, q)]]["fwd"].append(h)
    return cores, [role, role2, role2], [extra, extra2, extra2]


def calls(info, name, cores):
    return CALLS.get(name, [([0, 1, 2, 3], 2)])


def share(eng, part):
    return eng if part == 2 else eng[part * len(eng) // 2:(part + 1) * len(eng) // 2]


def helper(g, core, T, topo, cores, roles):
    ls = 0
    for name, (x, e, lo, hi) in PARTS.items():
        info = roles[e].get(core)
        if info is None or x not in info["x"]:
            continue
        rcs = [cores[r] for r in info["ranks"]]
        eng = topo.engines(core, rcs[0])
        direct = info["feed"] in cores
        got = len(topo.engines(info["feed"], core)) * (1 if direct else 2)
        buf, fa = T["D" + name], T.sem["fA" + name]
        if direct:
            g.sync.wait_ge(fa, got)
            g.sync.dma_start(buf[128:224, :], buf[0:96, :]).then_inc(T.sem["dA" + name], 16)
        g.wait_ge(fa, got)
        for h in info["fwd"]:
            en = topo.engines(core, h)
            g.remote_dma_fused([RemoteDMATransfer(dst_ids=[dst(topo, h)] * 2, dma_engine_mask=pl(en), remote_sem=fa,
                                                  srcs=[buf[0:128, :]], dsts=[buf[0:128, :], buf[128:256, :]])], local_sem=T.sem.ls)
            ls += len(en)
        if e and x == "O":
            g.wait_ge(T.sem["go%d" % e], len(rcs))
        for call, part in calls(info, name, cores):
            if direct and call[-1] and not call[0] > 1:
                g.wait_ge(T.sem["dA" + name], 16)
            use = share(eng, part)
            w = len(use) // len(call)
            trs = []
            for j, k in enumerate(call):
                c0 = k * G1 + info["A"] * R1 + (e - 1) * B1 * (e > 0)
                for i, c in enumerate(rcs):
                    m = use[j * w:(j + 1) * w][i::len(rcs)]
                    trs.append(RemoteDMATransfer(dst_ids=[dst(topo, c)], dma_engine_mask=pl(m), remote_sem=T.sem["arr%s%d" % (x, e)],
                                                 srcs=[buf[32 * k:32 * k + 128, :]], dsts=[T["W" + x][:, c0 + lo:c0 + hi]]))
                    ls += len(m)
            g.remote_dma_fused(trs, local_sem=T.sem.ls)
    if ls:
        g.wait_ge(T.sem.ls, ls)


def rank_program(g, core, T, topo):
    cores, roles, extras = plan(T, topo)
    rank = T.rank_of(core)
    if rank is None:
        helper(g, core, T, topo, cores, roles)
        return
    mine = [h for h in roles[1] if rank in roles[1][h]["ranks"]]
    near = [q for q, c in enumerate(cores) if q != rank and topo.chip(c) == topo.chip(core)]
    arr_n = {}
    for name, (x, e, lo, hi) in PARTS.items():
        for h, info in roles[e].items():
            if rank in info["ranks"] and x in info["x"]:
                arr_n[x, e] = arr_n.get((x, e), 0) + sum(len(share(topo.engines(h, core), p)) for _, p in calls(info, name, cores)) // len(info["ranks"])
    Q = {"v": g.vector, "s": g.scalar, "p": g.tensor, "g": g, "y": g.sync}
    QS = {"v": "qv", "s": "qs", "p": "qp", "g": "qg"}
    cnt, known, lastw, readers, lastx, alias = {}, {q: {} for q in Q}, {}, {}, {}, {}

    def need(q, tok):
        _, sem, c, clock = tok
        if known[q].get(sem, 0) >= c:
            return
        Q[q].wait_ge(T.sem[sem], c)
        for s2, c2 in clock.items():
            known[q][s2] = max(known[q].get(s2, 0), c2)
        known[q][sem] = max(known[q].get(sem, 0), c)

    def deps(q, rd, wr, ps):
        toks = []
        for k in [k2 for k in rd for k2 in alias.get(k, [k])]:
            if k in lastw:
                toks.append(lastw[k])
        for k in wr:
            if k in lastw:
                toks.append(lastw[k])
            toks += readers.get(k, [])
        for k in ps:
            if k in lastx:
                toks += [t for t in lastx[k].values() if t[0] != q]
        best = {}
        for t in toks:
            if q == "p" and t[0] == "p":
                continue
            if t[1] not in best or best[t[1]][2] < t[2]:
                best[t[1]] = t
        for t in sorted(best.values(), key=lambda t: -t[2]):
            need(q, t)

    def note(q, rd, wr, ps, tok):
        for k in rd:
            readers.setdefault(k, [])
            readers[k] = [t for t in readers[k] if not (t[0] == q and t[1] == tok[1])] + [tok]
        for k in wr:
            lastw[k] = tok
            readers[k] = []
        for k in ps:
            lastx.setdefault(k, {})
            lastx[k][q] = tok

    def op(q, fn, rd=(), wr=(), ps=()):
        deps(q, rd, wr, ps)
        sem = QS[q]
        c = cnt.get(sem, 0) + 1
        cnt[sem] = c
        fn(Q[q]).then_inc(T.sem[sem], 1)
        clock = dict(known[q])
        clock[sem] = c
        note(q, rd, wr, ps, (q, sem, c, clock))

    def dma(q, sem, pairs, rd=(), wr=()):
        deps(q, rd, wr, ())
        for o, i in pairs:
            Q[q].dma_start(o, i).then_inc(T.sem[sem], 16)
        cnt[sem] = cnt.get(sem, 0) + 16 * len(pairs)
        clock = dict(known[q])
        clock[sem] = cnt[sem]
        note(q, rd, wr, (), (q, sem, cnt[sem], clock))

    banks = [k for k, v in SCRATCH.items() if v[0] == "psum"]

    def split(xs):
        ks = [x[0] for x in xs if isinstance(x, tuple)]
        return [k for k in ks if k not in banks], [k for k in ks if k in banks]

    def raw(x):
        return x[1] if isinstance(x, tuple) else x

    def emit(q, fn, ins, out):
        r, rp = split(ins)
        w, wp = split([out])
        return op(q, fn, r, w, rp + wp)

    def ts(out, a, s1, o1, s2=None, o2=None, more=()):
        if o2 is None:
            return emit("v", lambda e: e.tensor_scalar(raw(out), raw(a), raw(s1), None, o1), [a, s1] + list(more), out)
        return emit("v", lambda e: e.tensor_scalar(raw(out), raw(a), raw(s1), raw(s2), o1, o2), [a, s1, s2] + list(more), out)

    def tt(out, a, b, o, more=()):
        return emit("v", lambda e: e.tensor_tensor(raw(out), raw(a), raw(b), o), [a, b] + list(more), out)

    def cp(out, a, more=()):
        return emit("v", lambda e: e.tensor_copy(raw(out), raw(a)), [a] + list(more), out)

    def act(out, a, f=COPY, scale=1.0, more=(), bias=0.0):
        return emit("s", lambda e: e.activation(raw(out), raw(a), f, bias=raw(bias), scale=raw(scale)), [a, bias, scale] + list(more), out)

    def mm(out, l, r, start, stop, more=()):
        return emit("p", lambda e: e.matmul(raw(out), raw(l), raw(r), start, stop), [l, r] + list(more), out)

    def C(name, a, b=None, st=None, key=None):
        return (key or name, T[name][:, a:b:st])

    def X(name):
        return (name, T[name][:])

    npc, nfc, nls = [0], [16], [0]

    def both(name):
        alias[name] = [name + "a", name + "b"]

    def icol(shop, val):
        k = npc[0]
        npc[0] += 1
        o = ("pc%d" % k, T.pc[:, k:k + 1])
        ts(o, X("PI"), val, shop)
        return o

    def col(a, s1, o1, s2=None, o2=None):
        k = nfc[0]
        nfc[0] += 1
        o = ("fc%d" % k, T.fc[:, k:k + 1])
        ts(o, a, s1, o1, s2, o2)
        return o

    def scol(a, w, b, f=IDENT):
        k = nfc[0]
        nfc[0] += 1
        o = ("fc%d" % k, T.fc[:, k:k + 1])
        act(o, a, f, scale=w, bias=b)
        return o

    def lin(*terms, q="s"):
        acc = terms[-1] if isinstance(terms[-1], tuple) and not isinstance(terms[-1][0], tuple) else float(terms[-1])
        for c, w in terms[:-1]:
            acc = col(c, float(w), A_.mult, acc, A_.add) if q == "v" else scol(c, float(w), acc)
        return acc

    def hot(out, lo, tgt, shift=0.0):
        n = raw(out).shape[1]
        ts(out, C("CI", lo, lo + n), -float(shift), A_.add, tgt, A_.is_equal)

    dma("y", "ldO", [(T.OI[:], T.opts[:])], wr=["OI"])
    lds = [(T.WI[32 * a + 16 * b:32 * a + 16 * b + 16, 192 * f:192 * f + 192], (T.rw, T.lw)[b][32 * a + 16 * f:32 * a + 16 * f + 16, :])
           for a in range(4) for b in range(2) for f in range(2)]
    dma("s", "ldW", lds[:9], wr=["WIa"])
    dma("y", "ldW", lds[9:], wr=["WI"])
    op("g", lambda e: e.iota(T.PI[:], [[0, 1]], 0, 1), wr=["PI"])
    op("g", lambda e: e.iota(T.CI[:], [[1, 176]], 0, 0, allow_small_or_imprecise_dtypes=True), wr=["CI"])
    masks = (103, 8, 16, 96, 7, 15, 12, 1, 2, 4)
    p103, ph, pb = [icol(A_.bitwise_and, m) for m in masks[:3]]
    tO = lin((p103, 1), 16, q="v")
    sgn = lin((pb, -0.125), 1, q="v")
    tO = lin((ph, -2), tO, q="v")
    bO = lin((ph, (129 - 875136) / 8), 875136, q="v")
    tf = [lin((pb, 64 - 128 * f), tO, q="v") for f in range(2)]
    for M, o in (("EH", 0), ("EL", 8)):
        for f in range(2):
            hot(C(M, 128 * f, 128 * f + 128, key=M + str(f)), 0, tf[f], o + 1024 * f)
    for j, (M, w) in enumerate((("EH", 128.0), ("EH", -384.0), ("EH", 2304.0), ("EL", -2.0), ("EH", -8832.0))):
        act(C("MS", 256 * j, 256 * j + 256, key="MS%d" % j), (M + "0", T[M][:]), scale=w, more=[(M + "1", 0)])
    ts(C("SW0", 0, None, 2, key="SW0a"), C("WI", 0, 192), sgn, A_.mult)
    ts(C("SW0", 1, None, 2, key="SW0b"), C("WI", 192, 384), sgn, A_.mult)
    both("SW0")

    def send(part):
        x, e, lo, hi = PARTS[part]
        name = "S%s%d" % (x, e)
        deps("g", [name], [], ())
        offs = [(h, T["D" + part][0:128, :]) for h, info in roles[e].items() if info["feed"] == core and x in info["x"]]
        offs += [(cores[r], T["N%s%d" % (x, e)][:]) for r, q, y in extras[e] if q == rank and y == x]
        en = topo.engines(core, offs[0][0])
        trs = [RemoteDMATransfer(dst_ids=[dst(topo, h) for h, _ in offs], dma_engine_mask=pl(en), remote_sem=T.sem["fA" + part],
                                 srcs=[T[name][:, lo:hi]], dsts=[d for _, d in offs])]
        cnt["ls" + part] = len(en)
        if e:
            trs += to_near(part, en, part)
        g.remote_dma_fused(trs, local_sem=T.sem["ls" + part])
        if part in ("O0", "Wb") and near:
            g.remote_dma_fused(to_near(part, en, "Wa"), local_sem=T.sem.lsWa)

    def to_near(part, en, sem):
        x, e, lo, hi = PARTS[part]
        trs = []
        for q in near:
            e2 = [y for y in topo.engines(core, cores[q]) if y not in en]
            buf = T["DNW" if part == "Wb" else "D" + part]
            trs.append(RemoteDMATransfer(dst_ids=[dst(topo, cores[q])] * 2, dma_engine_mask=pl(e2), remote_sem=T.sem["fB" + part],
                                         srcs=[T["S%s%d" % (x, e)][:]], dsts=[buf[0:128, :], buf[128:256, :]]))
            cnt["ls" + sem] += len(e2)
        return trs

    def put(qu, e, x, sem, name, src, rd, some=slice(None)):
        nn, W = PN[e], T["W" + x]
        c0 = src * R1 + (e - 1) * B1 * (e > 0)
        pairs = [(W[:, c0:c0 + nn], T[name][0:128, :])]
        for k in range(1, 4):
            c = c0 + k * G1
            if name[0] == "D":
                pairs.append((W[:, c:c + nn], T[name][32 * k:32 * k + 128, :]))
            else:
                pairs.append((W[0:128 - 32 * k, c:c + nn], T[name][32 * k:128, :]))
                pairs.append((W[128 - 32 * k:128, c:c + nn], T[name][0:32 * k, :]))
        deps(qu, [], ["W" + x], ())
        dma(qu, sem + x + str(e), pairs[some], rd=rd, wr=[sem + x] if some.stop is None else [])

    def put_own(qu, e, x, after=None, some=slice(None)):
        if after:
            Q[qu].wait_ge(T.sem["ls" + after], cnt["ls" + after])
        put(qu, e, x, "own", "S%s%d" % (x, e), rank, ["S%s%d" % (x, e)], some)

    def put_nb(qu, e, x):
        part = [p for p, v in PARTS.items() if v[:2] == (x, e)][-1]
        for q in near:
            h = [h for h, info in roles[e].items() if info["feed"] == cores[q]][0]
            Q[qu].wait_ge(T.sem["fB" + part], 2 * len([y for y in topo.engines(cores[q], core) if y not in topo.engines(cores[q], h)]))
            put(qu, e, x, "nbd", "DNW" if part == "Wb" else "D" + part, q, [])
        for q in [q for r, q, y in extras[e] if r == rank and y == x]:
            Q[qu].wait_ge(T.sem["fA" + part], len(topo.engines(cores[q], core)))
            put(qu, e, x, "nbd", "N%s%d" % (x, e), q, [])

    send("Wa")
    put_own("y", 0, "W")
    n = X("OI")
    fls = [C("fl", 192 * j, 192 * j + 192, key="fl%d" % j) for j in range(5)]
    for j, d in enumerate((64, 192, 384, 1536)):
        ts(fls[j], n, 1.0 / d, A_.mult, 129 - (d - 1) / 2.0 / d, A_.add)
    ts(X("ni"), n, 63, A_.bitwise_and)
    ts(fls[4], X("ni"), -1.0, A_.mult)
    for m in masks[3:]:
        icol(A_.bitwise_and, m)
    cp(C("fc", 0, len(masks), key="pf"), ("pc0", T.pc[:, 0:len(masks)]), more=[("pc%d" % k, 0) for k in range(len(masks))])
    p103, ph, pb, pa, p7, p15, p12, u1, u2, u4 = [("pf", T.fc[:, k:k + 1]) for k in range(len(masks))]
    terms = [("MS", 0, 0), ("EL", 0, 1), ("MS", 1, 1), ("MS", 2, 2), ("MS", 3, 2), ("MS", 4, 3), ("MS", 3, 4)]
    for i, (M, j, r) in enumerate(terms):
        for f in range(2):
            mm(C("PX%d" % f, 0, 192), C(M, 256 * j + 128 * f, 256 * j + 128 * f + 128, key="MS%d" % j if M == "MS" else M + str(f)), fls[r],
               i == 0, i == len(terms) - 1)
    act(C("SO0", 0, None, 2, key="SO0a"), C("PX0", 0, 192), IDENT, bias=bO)
    ts(C("SO0", 1, None, 2, key="SO0b"), C("PX1", 0, 192), bO, A_.add)
    both("SO0")
    send("O0")
    send("Wb")
    put_own("y", 0, "O", OWNO)
    put_nb("y", 0, "O")
    put_nb("y", 0, "W")
    def fill(out, val):
        emit("g", lambda e: e.iota(raw(out), [[0, raw(out).shape[1]]], val, 0, allow_small_or_imprecise_dtypes=True), [], out)

    def pick(out, src, levels, row0, val):
        emit("g", lambda e: e.affine_select(raw(out), raw(src), [[-s, c] for s, c in levels], A_.not_equal, val, -row0, 1), [src], out)

    def band(out, src, levels, row0, rows):
        emit("g", lambda e: e.affine_select(raw(out), raw(src), [[-s, c] for s, c in levels], A_.is_ge, 0.0, -row0, 1), [src], out)
        emit("g", lambda e: e.affine_select(raw(out), raw(out), [[s, c] for s, c in levels], A_.is_ge, 0.0, row0 + rows - 1, -1), [out], out)

    act(X("SG"), C("CI", 0, 160), IDENT, scale=0.0, bias=sgn)
    fill(X("ON"), 1)
    fill(X("ZB"), 0)
    band(X("EMS"), X("ON"), [(32, 6), (-16, 2), (1000, 16)], -16, 16)
    pick(X("ID"), C("ZB", 0, 128), [(1, 128)], 0, 1.0)
    op("g", lambda e: e.iota(T.jx[:], [[4, 32]], 0, 0), wr=["jx"])
    op("g", lambda e: e.iota(T.js[:], [[8, 2], [16, 2], [512, 2]], 0, 0), wr=["js"])
    for y in range(2):
        pick(C("KM", 160 * y, 160 * y + 160, key="KM%d" % y), C("ZB", 0, 160), [(32, 5), (8, 8), (1, 4)], 4 * y - 32, 1.0)
    for y in range(2):
        pick(C("KZ", 160 * y, 160 * y + 160, key="KZ%d" % y), C("ZB", 0, 160), [(32, 5), (-1000, 2), (1, 16)], 1000 + 16 * y, 1.0)
    pick(X("SWB"), C("ZB", 0, 128), [(32, 4), (-16, 2), (1, 16)], 16, 1.0)
    band(X("EWP"), X("SG"), [(32, 5), (1000, 32)], -32, 32)
    fill(X("LT"), int(CAP))
    band(X("LT"), X("LT"), [(8, 16), (0, 8)], 0, 8)
    emit("g", lambda e: e.affine_select(T.LT[:], T.LT[:], [[1, 128]], A_.is_gt, 0.0, 0, -1), [X("LT")], X("LT"))
    pick(X("LT"), X("LT"), [(1, 128)], 0, -CAP)
    for y in range(2):
        pick(C("DM", 128 * y, 128 * y + 128, key="DM%d" % y), C("ZB", 0, 128), [(16, 8), (0, 2), (1, 8)], 8 * y, 1.0)
    band(X("CM"), C("ON", 0, 144), [(16, 9), (1000, 8), (8, 2)], -16, 8)
    fill(X("SLM"), -131072)
    band(X("SLM"), X("SLM"), [(32, 4), (-16, 2), (0, 16)], 16, 8)
    fill(X("RS"), 0)
    op("g", lambda e: e.affine_select(T.RS[:], T.RS[:], [[0, 48], [1, 8]], A_.not_equal, -2.0 ** 25, 0, 0), rd=["RS"], wr=["RS"])
    H = lin((pa, G1 / 32), 0, q="v")
    base = lin((pb, -1), pa, q="v")
    F = {1: u1, 2: lin((u2, 0.5), 0, q="v"), 4: lin((u4, 0.25), 0, q="v")}
    Hh = lin((ph, -4096), H, q="v")
    tL = lin((p7, 1), base, q="v")
    for m, x, y in ((5, 1, 4), (3, 1, 2), (6, 2, 4), (7, 3, 4)):
        F[m] = col(F[x], F[y], A_.not_equal)
    nH = lin((pa, -G1 / 32), 0, q="v")
    ECw = col(H, 1.0, A_.is_ge, float(WC), A_.mult)
    ts(X("OZ"), X("SO0"), Hh, A_.is_lt, float(WC), A_.mult)
    hot(X("PLM"), 0, tL, 24)
    ECw = col(ECw, float(EC), A_.add)
    sets = []
    for k1, k2 in KS:
        phi = [m for m in range(1, 8) if par(m & k1) and par(m & k2)][0]
        one = [s for s in range(8) if par(s & phi)]
        ps1, ps2 = [(x, y) for x in (1, 2, 4) for y in (1, 2, 4) if len(set(par(s & x) + 2 * par(s & y) for s in one)) == 4][0]
        one.sort(key=lambda s: par(s & ps1) + 2 * par(s & ps2))
        sets.append((phi, ps1, ps2, one))

    def lists(t):
        c0 = 128 * t
        phi, ps1, ps2, one = sets[t]
        ks = (0,) + KS[t]
        tg = [lin((F[phi], -1000 if k == 0 else 1000), base, q="v") for k in ks[:2]]
        tg = [lin((F[ps1], 1 - 2 * par(ps1 & k)), tg[min(j, 1)], q="v") for j, k in enumerate(ks)]
        tg = [lin((F[ps2], 2 - 4 * par(ps2 & k)), tg[j], q="v") for j, k in enumerate(ks)]
        for j, k in enumerate(ks):
            hot(C("ED", 140 * j, 140 * j + 140, key="ED%d" % j), 0, tg[j], 28 + 1000 * (j == 0) + par(ps1 & k) + 2 * par(ps2 & k))
        for j in range(3):
            for r in ("SO0", "OZ"):
                for y in range(4):
                    o = 140 * j + 12 - 4 * y
                    mm(C("PDM", 32 * j, 32 * j + 32), C("ED", o, o + 128, key="ED%d" % j), C(r, c0 + y, c0 + 128, 4),
                       y == 0 and r == "SO0", y == 3 and r == "OZ")
        for r in ("SO0", "OZ"):
            for y in range(2):
                mm(C("PCN", 0, 64), C("PLM", 8 - 8 * y, 136 - 8 * y), C(r, c0 + y, c0 + 128, 2), y == 0 and r == "SO0", y == 1 and r == "OZ")

    def lists2(t):
        ts(C("LD", 96 * t, 96 * t + 96, key="LD%d" % t), C("PDM", 0, 96), nH, A_.add)
        ts(C("LU", 64 * t, 64 * t + 64, key="LU%d" % t), C("PCN", 0, 64), nH, A_.add)
        ts(C("NE", 64 * t, 64 * t + 64, key="NE%d" % t), C("PCN", 0, 64), ECw, A_.is_equal)

    lists(0)
    op("v", lambda e: e.memset(T.WW[:, EC::G1], -BIG), wr=["WWe"])
    eo = lin((ph, -EC / 8), EC)
    act(("WOe", T.WO[:, EC::G1]), C("CI", 0, 4), IDENT, scale=0.0, bias=eo)
    w8 = lin((u1, 2), (u2, 2), (pb, 0.0625), 0)
    q32 = lin((p15, 32), w8)
    xb = lin((p12, 0.25), 0)
    dL = lin((pb, -1 / 32), 0)
    dR = lin((pb, 1 / 16), -0.5)
    ts(X("XBL"), X("jx"), xb, A_.add)
    lists2(0)

    def sels(t):
        z = col(w8, 8.0 - t, A_.is_ge, -8.0, A_.mult)
        ts(C("SEL", 8 * t, 8 * t + 8, key="SEL%d" % t), X("js"), z, A_.add, lin((q32, 1), t, q="v") if t else q32, A_.add)

    sels(0)
    if TWO:
        act(X("EMB"), X("EMS"), scale=-2.0 ** 30)
    else:
        act(X("N31"), X("ID"), scale=-31.0)
    made, dc = {}, {}

    def diffs(t):
        ds = sorted(set(abs((s ^ k) - s) for s in sets[t][3] for k in KS[t]) - set(made))
        if TWO:
            ds = sorted(set((s ^ k) - s for s in range(8) for k in KS[t]) - set(made))
        for i in range(0, len(ds), 3):
            bank, o = ("PZ1", "PDM")[i // 3], 144 * len(made)
            for j, d in enumerate(ds[i:i + 3]):
                made[d] = (144 * len(made), "AD%d" % o)
                mm(C(bank, 144 * j, 144 * j + 144), X("ID"), C("EMS", 16, 160), True, False)
                mm(C(bank, 144 * j, 144 * j + 144), X("ID"), C("EMB" if TWO else "EMS", 16 - d, 160 - d), False, True)
            act(C("AD", o, 144 * len(made), key="AD%d" % o), C(bank, 0, 144 * len(made) - o))
        if TWO:
            for z, k in enumerate(KS[t]):
                hb = 4 if k >= 4 else 2 if k >= 2 else 1
                if hb not in dc:
                    dc[hb] = lin((F[hb], 0.5), -0.25, q="s" if t else "v")
                dc[t, z + 1] = dc[hb]
            return
        f = F[sets[t][0]]
        q = "s" if t else "v"
        act(C("DG", 128 * t, 128 * t + 128, key="DG%d" % t), X("ID"), scale=lin((f, 33), -1, q=q))
        b = lin((f, -129 * 33), 129 * 32 - 0.25, q=q)
        for z, k in enumerate(KS[t]):
            dc[t, z + 1] = lin((F[4 if k >= 4 else 2 if k >= 2 else 1], 0.5), b, q=q)

    diffs(0)

    def own_walls(t):
        act(X("XL"), ("SW0", T.SW0[:, 128 * t:128 * t + 128].indirect(T.XBL[:])), IDENT, bias=dL, more=[("XBL", 0)])
        act(X("PX0"), X("XL"))
        act(X("PX1"), X("XL"), IDENT, bias=dR)

    own_walls(0)
    temp = lin((p15, 1024), 0, q="v")
    hc = lin((sgn, -0.25), 0, q="v")
    ts(C("NEC", 0, 64, key="NECa"), C("CI", 0, 64), 0.0, A_.mult, lin((nH, 1), CAP, q="v"), A_.add)
    ts(C("NEC", 64, 128, key="NECb"), C("CI", 0, 64), 0.0, A_.mult, CAP, A_.add)
    both("NEC")
    act(X("TMPT"), C("CI", 0, 128), IDENT, scale=0.0, bias=temp)
    act(("WOf", T.WO[:, WC:WC + 8]), C("CI", 0, 8), IDENT, scale=0.0, bias=eo)
    act(X("HHT"), C("CI", 0, 128), IDENT, scale=0.0, bias=Hh)
    act(X("NID"), X("ID"), scale=-1.0)
    act(X("PLW"), X("PLM"), scale=float(WC))
    act(X("EWN"), X("EWP"), scale=-1.0)
    act(X("C16"), C("CI", 0, 64), IDENT, scale=0.0, bias=-15.875)
    act(X("NSB"), X("SWB"), scale=-1.0)
    act(X("NSW"), X("SWB"), scale=-1.0)
    later = {}

    def out_setup(part):
        if part == 0:
            later["tN"] = lin((pb, 0.5), tL, q="v")
            later["w"] = [lin((ph, (wl - wh) / 8), wh, q="v") for wh, wl in ((0.5, 192), (1344, -384), (-8832, 1))]
            later["tN"] = lin((later["tN"], 1), 24, q="v")
            later["sA"] = lin((ph, (0.5 - 1 / 384) / 8), 1 / 384, q="v")
            later["bA"] = lin((ph, (1 / 3 - 0.25) / 8), 129 - 1 / 3, q="v")
            later["sB"] = lin((ph, (0.5 - 1 / 2304) / 8), 1 / 2304, q="v")
            later["bB"] = lin((ph, (8.5 / 18 - 0.25) / 8), 129 - 8.5 / 18, q="v")
        else:
            for j in range(3):
                ts(C("NM", 144 * j, 144 * j + 144, key="NM%d" % j), C("CI", 0, 144), later["tN"], A_.is_equal, later["w"][j], A_.mult)

    lists(1)
    out_setup(0)
    sels(1)
    lists2(1)
    tt(X("HSW"), X("ID"), X("SWB"), A_.subtract)
    out_setup(2)

    def win(x, L, lo, hi):
        return ("W" + x, T["W" + x][:].indirect(T[L][:, lo:hi]))

    now = [0]

    def wm(x, L):
        return [(L, 0), (L + str(now[0]), 0), ("own" + x, 0), ("nbd" + x, 0), ("W%se" % x, 0), ("W%sf" % x, 0)]

    def arrived(x, t):
        for q in "vs":
            Q[q].wait_ge(T.sem["arr%s%d" % (x, t)], arr_n[x, t])

    def gather_slots(t):
        arrived("O", t)
        cp(C("T0", 0, 512, key="T0a"), win("O", "LU", 64 * t, 64 * t + 32), more=wm("O", "LU"))
        act(C("T0", 512, 1024, key="T0b"), win("O", "LU", 64 * t + 32, 64 * t + 64), more=wm("O", "LU"))

    def replies(t):
        for h, c in (("a", slice(0, 512)), ("b", slice(512, 1024))):
            emit("v", lambda e, c=c: e.transpose(T.T1[:, c], T.T0[:, c]), [("T0" + h, 0)], ("T1" + h, 0))
        cp(X("PK"), ("T1a", T.T1[:].indirect(T.SEL[:, 8 * t:8 * t + 8])), more=[("SEL%d" % t, 0), ("T1b", 0)])
        ts(X("pz"), C("PK", 0, 64), H, A_.is_lt, float(WC), A_.mult)
        mm(C("PPF", 0, 128), X("ID"), C("ZB", 0, 128), True, False)
        for r in (C("PK", 0, 64), C("PK", 64, 128), X("pz")):
            for s2 in range(2):
                mm(C("PPF", 64 * s2, 64 * s2 + 64), C("KM", 160 * s2 + 16, 160 * s2 + 144, key="KM%d" % s2), r, False, r[0] == "pz" and s2 == 1)
        ts(X("LK"), C("PPF", 0, 128), nH, A_.add)

    def reply_parts():
        mm(C("PPF", 128, 256), X("ID"), X("NEC"), True, False)
        for M, w, hl in (("PK", 0, 0), ("pz", 0, 0), ("PK", 64, 1)):
            for y in range(2):
                for b in range(2):
                    o = 160 * y + 16 - 16 * b
                    mm(C("PPF", 128 + 64 * hl + y, 192 + 64 * hl, 2), C("KZ", o, o + 128, key="KZ%d" % y),
                       C(M, w + 32 - 32 * b, w + 64 - 32 * b), False, False)

    def gather_one(t):
        act(X("U1"), win("W", "LD", 96 * t, 96 * t + 32), more=wm("W", "LD"))

    def diff(t, z):
        tt(X("D%d" % z), win("W", "LD", 96 * t + 32 * z, 96 * t + 32 * z + 32), X("U1"), A_.subtract, more=wm("W", "LD"))

    def signs(z):
        ts(X("IA%d" % z), X("D%d" % z), 1.0, A_.min, -31 / 512, A_.max)

    def count_del(t, z):
        k = KS[t][z - 1]
        for y in range(2):
            for i, s in enumerate(sets[t][3]):
                d = abs((s ^ k) - s)
                w = made[d][0] + 16 - 8 * y - min(s, s ^ k)
                mm(C("PZ%d" % z, 0, 64), C("AD", w, w + 128, key=made[d][1]), C("IA%d" % z, 4 * y + i, None, 8), y + i == 0, y + i == 4)

    def whole(t, z):
        act(X("AR%d" % z), C("PZ%d" % z, 0, 64), IDENT, bias=129.485)
        act(X("AQ%d" % z), C("PZ%d" % z, 0, 64), IDENT, bias=129 - 0.48)

    def whole2(t, z):
        mm(C("PZ%d" % z, 256, 320), X("N31"), X("AR%d" % z), True, False)
        mm(C("PZ%d" % z, 256, 320), C("DG", 128 * t, 128 * t + 128, key="DG%d" % t), X("AQ%d" % z), False, True)

    def signs2(z, x, q):
        name, sc = "I%s%d" % (x, z), 1.0 if x == "A" else -1.0
        if q == "v":
            ts(X(name), X("D%d" % z), sc, A_.mult, 0.0, A_.max)
        else:
            act(X(name), X("D%d" % z), RELU, scale=sc)

    def count2(t, z, x, first):
        k = KS[t][z - 1]
        for y in range(2):
            for i, s in enumerate(sets[t][3]):
                a, b = (s ^ k, s) if x else (s, s ^ k)
                w = made[b - a][0] + 16 - 8 * y - a
                mm(C("PZ%d" % z, 256, 320), C("AD", w, w + 128, key=made[b - a][1]), C(("IA%d", "IB%d")[x] % z, 4 * y + i, None, 8),
                   first and y + i == 0, not first and y + i == 4)

    def fetch(j):
        w = GAP * (j == 2)
        act(C("TL", 512 * j - 512 + w, 512 * j, key="TL%d" % j), win("W", "LK", 32 * j + w // 16, 32 * j + 32), more=wm("W", "LK"))

    def compare(j):
        if j == 0:
            tt(C("VI", 0, 512, key="VI0"), win("W", "LK", 0, 32), X("XL"), A_.is_gt, more=wm("W", "LK"))
            if GAP:
                tt(C("VI", 1024, 1024 + GAP, key="VI5"), win("W", "LK", 64, 64 + GAP // 16), C("XL", 0, GAP), A_.is_gt, more=wm("W", "LK"))
        elif j < 3:
            w = GAP * (j == 2)
            tt(C("VI", 512 * j + w, 512 * j + 512, key="VI%d" % j), C("TL", 512 * j - 512 + w, 512 * j, key="TL%d" % j), C("PX%d" % (j & 1), w, 512), A_.is_gt)
        else:
            tt(C("VI", 1533 + j, 2048, 2, key="VI%d" % j), C("TL", 1021 + j, 1536, 2, key="TL3"), C("PX1", j - 3, 512, 2), A_.is_gt)

    def count_rep(j):
        p = min(j, 3)
        for y in range(2):
            for s in range(4) if j < 3 else range(j - 3, 4, 2):
                w = 32 - (16 * (1 - (p & 1)) + 8 * y + 4 * (p >> 1) + s)
                mm(C("PCN", 0, 64), C(("EWN", "EWP")[p & 1], w, w + 128), C("VI", 512 * p + 4 * y + s, 512 * p + 512, 8, key="VI%d" % j),
                   False, j == 4 and y == 1 and s == 3, more=[("VI5", 0)] * (j == 2))

    def flags(z):
        act(X("m%d" % z), C("PZ%d" % z, 256, 320), RELU, bias=dc[now[0], z])

    def Y(x, t):
        return C("Y" + x, 64 * t, 64 * t + 64, key="Y%s%d" % (x, t))

    def store(q, x, t):
        lo = 0 if t == 1 else 64 * t
        dma(q, "o%s%d" % (x, t), [(T["y" + x.lower()][:, lo:64 * t + 64], T["Y" + x][:, lo:64 * t + 64])], rd=["Y%s%d" % (x, t), "Y%s0" % x])

    def numbers(t):
        nw = X("SO%d" % (t + 1))
        act(X("nA"), nw, IDENT, scale=later["sA"], bias=later["bA"])
        act(X("nB"), nw, IDENT, scale=later["sB"], bias=later["bB"])
        for j, r in enumerate(("SO%d" % (t + 1), "nA", "nB")):
            for f in range(2):
                o = 144 * j + 16 - 16 * f
                mm(C("PCN", 0, 64), C("NM", o, o + 128, key="NM%d" % j), C(r, f, None, 2), j + f == 0, j + f == 3)
        act(Y("O", t), C("PCN", 0, 64), IDENT, bias=1015359.0)
        if t:
            store("y", "O", t)

    def unpair(src, banks2):
        for b in range(2):
            for f in range(2):
                o = 160 * b + 16 - 16 * f
                mm(C(banks2[b], 256, 320), C("KZF", o, o + 128), C(src, f, None, 2), f == 0, f == 1)

    for t in range(3):
        oc = C("SO0", 128 * t, 128 * t + 128)
        ne = C("NE", 64 * t, 64 * t + 64, key="NE%d" % t)
        now[0] = t
        if t == 0:
            gather_slots(t)
            replies(t)
        arrived("W", t)
        mm(C("PCN", 0, 64), X("ID"), X("C16"), True, False)
        mm(C("PCN", 0, 64), X("NSB"), ne, False, False)
        for step in STAGE.split():
            z = int(step[1])
            if step[0] == "u":
                gather_one(t)
            elif step[0] == "c":
                compare(z)
            elif step[0] == "r":
                count_rep(z)
            elif step[0] == "f":
                fetch(z)
            elif step[0] == "d":
                diff(t, z)
            elif TWO and step[0] in "AB":
                signs2(z, step[0], step[2])
            elif TWO and step[0] in "ab":
                count2(t, z, "ab".index(step[0]), STAGE.index("a%d" % z) < STAGE.index("b%d" % z) if step[0] == "a" else STAGE.index("b%d" % z) < STAGE.index("a%d" % z))
            elif step[0] == "A":
                signs(z)
            elif step[0] == "a":
                count_del(t, z)
            elif step[0] == "B":
                whole(t, z)
            elif step[0] == "b":
                whole2(t, z)
            elif step[0] == "k":
                reply_parts()
            elif step[0] == "m":
                flags(z)
            else:
                mm(C("PCN", 0, 64), X("NID"), X("m%d" % z), False, False)
        o = C("PZ1", 64, 128)
        mm(o, X("SWB"), ne, True, False)
        mm(o, X("ID"), X("m1"), False, False)
        mm(o, X("ID"), X("m2"), False, True)
        act(X("GX"), o, SIGN)
        if t < 2:
            own_walls(t + 1)
        tt(X("REV"), X("m2"), C("PCN", 0, 64), A_.is_lt)
        for x in range(2):
            mm(C("PPF", 128 + 64 * x, 192 + 64 * x), X("LT"), X("REV"), False, x == 1)
        ts(X("FK"), C("PPF", 128, 256), CAP, A_.min)
        ts(X("FI"), C("PPF", 128, 192), CAP, A_.is_lt)
        for x in range(2):
            for c in range(8):
                mm(C("PCH", 0, 8), C("CM", 16 - 2 * c, 144 - 2 * c), C("FK", 64 * x + c, 64 * x + 64, 8), x + c == 0, x + c == 8)
        mm(C("PDM", 0, 128), X("ID"), C("ZB", 0, 128), True, False)
        for r in ("GX", "FI"):
            for y in range(2):
                mm(C("PDM", y, 128, 2), C("DM", 128 * y, 128 * y + 128, key="DM%d" % y), X(r), False, r == "FI" and y == 1)
        mm(C("PZ1", 128, 256), X("ID"), X("HHT"), True, False)
        mm(C("PZ1", 128, 256), X("NID"), oc, False, True)
        mm(C("PCN", 128, 256), X("ID"), oc, True, True)
        for y in range(2):
            mm(C("PPF", 0, 64), C("PLM", 8 - 8 * y, 136 - 8 * y), C("SO0", 128 * t + y, 128 * t + 128, 2), y == 0, False)
        ts(X("CLS"), C("PCH", 0, 8), -14 * CAP, A_.add, float(WC), A_.min)
        tt(X("dd"), win("O", "CLS", 0, 8), oc, A_.subtract, more=wm("O", "CLS"))
        tt(X("ee"), X("dd"), C("PDM", 0, 128), A_.mult)
        so = "SO%d" % (t + 1)
        tt(X("zN"), X("ee"), C("PZ1", 128, 256), A_.is_lt)
        for M, r in (("PLM", "ee"), ("PLW", "zN")):
            for y in range(2):
                mm(C("PPF", 0, 64), C(M, 8 - 8 * y, 136 - 8 * y), C(r, y, None, 2), False, r == "zN" and y == 1)
        tt(X(so), X("ee"), C("PCN", 128, 256), A_.add)
        ts(X("LN"), C("PPF", 0, 64), nH, A_.add)
        act(X("FG"), X(so), ABS, bias=-float(EC))
        mm(C("PZ2", 0, 128), X("ID"), X("TMPT"), True, False)
        mm(C("PZ2", 0, 128), X("NSW"), C("SW0", 128 * t, 128 * t + 128), False, False)
        mm(C("PZ2", 0, 128), X("SLM"), X("FG"), False, True)
        if t < 2:
            send("O%d" % (t + 1))
            put_own("y", t + 1, "O")
            put_nb("y", t + 1, "O")
            mm(C("PCH", 0, 128), X("ID"), X("TMPT"), True, False)
        cuts = list(zip(CUT, CUT[1:]))
        for lo, hi in cuts:
            (act if lo else cp)(C("U2", lo, hi, key="U2%d" % lo), win("W", "LN", lo // 16, hi // 16), more=wm("W", "LN"))
        if t < 2:
            need("g", lastw["U20"])
            need("g", lastw["U2%d" % CUT[-2]])
            g.remote_dma_fused([RemoteDMATransfer(dst_ids=[dst(topo, h)], dma_engine_mask=1 << topo.engines(core, h)[j],
                                                  remote_sem=T.sem["go%d" % (t + 1)]) for j, h in enumerate(mine)], local_sem=T.sem.ls)
            nls[0] += len(mine)
            diffs(t + 1)
            if t == 1:
                act(X("KZN"), C("KZ", 160, 320, key="KZ1"), scale=-1.0)
            if t == 0:
                act(X("KZF"), ("KZ0", T.KZ[:]), more=[("KZ1", 0)])
        else:
            mm(C("PX0", 256, 320), X("NID"), C("TMPT", 0, 64), True, False)
            mm(C("PX1", 256, 320), X("ID"), C("TMPT", 0, 64), True, False)
            numbers(t)
        for lo, hi in cuts:
            emit("v", lambda e, c=slice(lo, hi), w=hi - lo: e.tensor_tensor_scan(T.SC[:, c], T.RS[:, 0:w], T.U2[:, c], 0.0, A_.add, A_.max),
                 [("RS", 0), ("U2%d" % lo, 0)], ("SC%d" % lo, 0))
        tt(X("ww"), C("SC", 7, None, 8, key="SC0"), C("PZ2", 0, 128), A_.max, more=[("SC%d" % lo, 0) for lo, hi in cuts])
        if t < 2:
            sw = "SW%d" % (t + 1)
            mm(C("PPF", 0, 128), X("HSW"), X("ww"), True, True)
            mm(C("PCH", 0, 128), X("NSW"), X("ww"), False, True)
            ts(X("wi"), C("PPF", 0, 128), 0.5, A_.mult, hc, A_.add)
            tt(X(sw), X("wi"), C("PCH", 0, 128), A_.min)
            send("W%d" % (t + 1))
            if EARLY:
                put_own("y", t + 1, "W", None, slice(0, EARLY))
            if EARLY < 4:
                put_own("y", t + 1, "W", "W%d" % (t + 1), slice(EARLY, 4))
            put_nb("y", t + 1, "W")
            numbers(t)
            unpair(sw, ("PZ1", "PZ2"))
            act(Y("R", t), C("PZ1", 256, 320))
            act(Y("L", t), C("PZ2", 256, 320), scale=-1.0)
            if t == 0:
                lists(2)
                sels(2)
                lists2(2)
            now[0] = t + 1
            gather_slots(t + 1)
            put_own("s", t + 1, "W", "W%d" % (t + 1), slice(4, None))
            replies(t + 1)
        else:
            for bank, parts in (("PPF", ((0, "KZF"), (1, "KZN"))), ("PX0", ((0, "KZF"),)), ("PX1", ((1, "KZN"),))):
                for b, M in parts:
                    for f in range(2):
                        o = 160 * b * (M == "KZF") + 16 - 16 * f
                        mm(C(bank, 256, 320), C(M, o, o + 128), C("ww", f, None, 2), bank == "PPF" and b + f == 0, f == 1 and b == parts[-1][0])
            ts(C("wi", 0, 64), C("PPF", 256, 320), 0.5, A_.mult, -0.25, A_.add)
            tt(Y("L", t), C("wi", 0, 64), C("PX0", 256, 320), A_.max)
            tt(Y("R", t), C("wi", 0, 64), C("PX1", 256, 320), A_.min)
        if t:
            store("y", "L", t)
            store("s" if t == 2 else "y", "R", t)
    g.wait_ge(T.sem.ls, nls[0])
    for sem, c in cnt.items():
        if known["g"].get(sem, 0) < c:
            g.wait_ge(T.sem[sem], c)
